import numpy as np
import ml_dtypes


def mxq(x, axis, fmt="e4m3"):
    dtype, down = {"e4m3": (ml_dtypes.float8_e4m3fn, 7), "e5m2": (ml_dtypes.float8_e5m2, 14)}[fmt]
    v = np.moveaxis(np.asarray(x, np.float32).astype(ml_dtypes.bfloat16).astype(np.float64), axis, -1)
    blocks = v.reshape(v.shape[:-1] + (-1, 32))
    amax = np.abs(blocks).max(-1, keepdims=True)
    byte = np.maximum(np.where(amax > 0, np.frexp(amax)[1] - 1 + 127, 0) - down, 1)
    scale = np.exp2(byte - 127.0)
    codes = (blocks / scale).astype(np.float32).astype(dtype).astype(np.float64)
    return np.moveaxis((codes * scale).reshape(v.shape), -1, axis)


WIDE = False


def mx_kscale(k):
    if not WIDE:
        return np.ones(k)
    levels = np.array([10, -10, 5, -5, 0])
    if k % 512:
        return np.exp2(np.random.permutation(np.resize(levels, k // 32))).repeat(32)
    a = np.empty((k // 512, 16))
    for p in range(k // 512):
        a[p, :8] = np.random.permutation(np.resize(levels, 8))
        for g in range(8):
            far = levels[np.abs(levels - a[p, g]) >= 10]
            a[p, g + 8] = far[np.random.randint(len(far))]
    return np.exp2(a.ravel()).repeat(32)


def f64(x):
    return np.asarray(x).astype(np.float64)


def striped(idx):
    return np.tile(idx.reshape(-1, 16).T, (8, 1)).astype(np.uint16)


def unstriped(offs):
    return offs[:16].T.reshape(-1).astype(np.int64)


E2M1 = np.array([0.0, 0.5, 1.0, 1.5, 2.0, 3.0, 4.0, 6.0, -0.0, -0.5, -1.0, -1.5, -2.0, -3.0, -4.0, -6.0])


def pack_weight(w, fmt):
    k, n = w.shape
    w = f64(np.asarray(w, np.float32).astype(ml_dtypes.bfloat16)).reshape(k // 32, 32, n)
    amax = np.abs(w).max(1)
    if fmt == "e4m3":
        byte = np.frexp(amax)[1] - 1 + 127 - 7
    else:
        mant, ex = np.frexp(amax / 6.0)
        byte = np.where(mant > 0.5, ex, ex - 1) + 127
    byte = np.clip(np.where(amax > 0, byte, 1), 1, 254)
    scaled = (w * np.exp2(127.0 - byte)[:, None, :]).reshape(k, n).astype(np.float32)
    by_word = np.ascontiguousarray(scaled.reshape(k // 512, 128, 4, n).transpose(0, 1, 3, 2))
    if fmt == "e4m3":
        words = by_word.astype(ml_dtypes.float8_e4m3fn).view(np.uint8)
    else:
        c = by_word.astype(ml_dtypes.float4_e2m1fn).view(np.uint8) & 0xF
        words = (c[..., 0::2] | (c[..., 1::2] << 4)).reshape(k // 512, 128, 2 * n)
    return np.ascontiguousarray(words), np.ascontiguousarray(byte.astype(np.uint8).reshape(k // 512, 16, n))


def unpack_weight(words, scales, fmt):
    g, _, n = scales.shape
    words = np.ascontiguousarray(words).reshape(g, 128, n, -1)
    if fmt == "e4m3":
        vals = words.view(ml_dtypes.float8_e4m3fn).astype(np.float64)
    else:
        nib = np.empty((g, 128, n, 4), np.uint8)
        nib[..., 0::2] = words & 0xF
        nib[..., 1::2] = words >> 4
        vals = E2M1[nib]
    vals = vals * np.repeat(np.exp2(scales.astype(np.float64) - 127.0), 8, axis=1)[..., None]
    return vals.transpose(0, 1, 3, 2).reshape(g * 512, n)


def gelu(v):
    return 0.5 * v * (1.0 + np.tanh(np.sqrt(2.0 / np.pi) * (v + 0.044715 * v**3)))


def striped8(idx):
    return np.concatenate([v.reshape(-1, 16).T for v in idx]).astype(np.uint16)


def unstriped8(offs):
    return np.stack([offs[16 * g:16 * g + 16].T.reshape(-1) for g in range(8)]).astype(np.int64)


def put_heads(h, wgs, idx8, t2):
    r = np.arange(h.shape[0])
    page = np.zeros((h.shape[0], t2))
    page[r[:, None], idx8[r % 512 // 64]] = wgs[r // 4 % 128] * h
    return page


K, T, S, T2, H, N = 1024, 2048, 1024, 2048, 1024, 512


def setup_inputs():
    n = np.random.standard_normal
    s = mx_kscale(K)[:, None]
    u = mx_kscale(H)[:, None]
    tab_words, tab_scales = pack_weight(n((K, T)) * s, "e4m3")
    w1_words, w1_scales = pack_weight(n((K, H)) / np.sqrt(K) / s * u.T, "e2m1")
    return {
        "tab_words": tab_words,
        "tab_scales": tab_scales,
        "offs": striped(np.random.permutation(T)[:S]),
        "w1_words": w1_words,
        "w1_scales": w1_scales,
        "b1": (0.5 * n(H) * u[:, 0]).astype(np.float32),
        "offs2": striped8(np.stack([np.random.permutation(T2)[:S] for _ in range(8)])),
        "wgs": np.repeat(np.random.uniform(0.5, 2.0, (8, S)), 16, axis=0).astype(np.float32),
        "road": (n((H, T2)) * u).astype(np.float32),
        "w2": (n((H, N)) / np.sqrt(H) / u).astype(np.float32),
        "jam": np.exp(0.4 * n((N, T2))).astype(np.float32),
    }


def reference(tab_words, tab_scales, offs, w1_words, w1_scales, b1, offs2, wgs, road, w2, jam):
    v = unpack_weight(tab_words, tab_scales, "e4m3")[:, unstriped(offs)]
    w1 = unpack_weight(w1_words, w1_scales, "e2m1")
    h = np.maximum((w1.T @ v) + f64(b1)[:, None], 0.0)
    page = put_heads(h, f64(wgs), unstriped8(offs2), T2)
    z = page + f64(road)
    q = mxq(f64(w2), 0, "e4m3").T @ mxq(z, 0, "e4m3")
    return q + f64(jam) * np.tanh(q)

@@ -1,0 +1,330 @@
+from contextlib import ExitStack
+
+import concourse.mybir as mybir
+from concourse.masks import make_identity
+
+K, T, S, T2, H, N = 1024, 2048, 1024, 2048, 1024, 512
+FLOPS = 2 * K * H * S + 2 * H * N * T2
+
+F32 = mybir.dt.float32
+BF16 = mybir.dt.bfloat16
+I32 = mybir.dt.int32
+U32 = mybir.dt.uint32
+U16 = mybir.dt.uint16
+U8 = mybir.dt.uint8
+E4M3 = mybir.dt.float8_e4m3fn_x4
+E2M1 = mybir.dt.float4_e2m1fn_x4
+MULT = mybir.AluOpType.mult
+ADD = mybir.AluOpType.add
+RELU = mybir.ActivationFunctionType.Relu
+TANH = mybir.ActivationFunctionType.Tanh
+
+P = 128
+PACK = 4
+BANK = 512
+PASSES = 2
+SLICES = PASSES * PACK
+STRIP = 256
+STRIPS = T2 // STRIP
+CHUNKS = T2 // BANK
+SUM_BANKS = 6
+
+
+def tile_list_courier_eta_banks_kernel(
+    tc, tab_words, tab_scales, offs, w1_words, w1_scales, b1, offs2, wgs, road, w2, jam, out
+):
+    nc = tc.nc
+    with ExitStack() as ctx:
+        lists = ctx.enter_context(tc.tile_pool(name="lists", bufs=1))
+        keep = ctx.enter_context(tc.tile_pool(name="keep", bufs=1))
+        roads = ctx.enter_context(tc.tile_pool(name="roads", bufs=4))
+        results = ctx.enter_context(tc.tile_pool(name="results", bufs=6))
+        psum = ctx.enter_context(tc.psum_pool(name="psum", bufs=1))
+        banks = [psum.tile([P, BANK], F32, name=f"bank{j}") for j in range(8)]
+
+        tab_plane = keep.tile([P, T], U8, name="tab_plane", align_bytes=64)
+        for q in range(4):
+            nc.vector.memset(tab_plane[32 * q : 32 * q + 24, :].bitcast(I32), 0)
+        w1_plane = keep.tile([P, PASSES * H], U8, name="w1_plane", align_bytes=64)
+        nc.gpsimd.memset(w1_plane[:].bitcast(I32), 0)
+        v_plane = [keep.tile([P, S], U8, name=f"v_plane{a}", align_bytes=64) for a in range(PASSES)]
+        for a in range(PASSES):
+            nc.gpsimd.memset(v_plane[a][96:128, :].bitcast(I32), 0)
+        pages = [keep.tile([P, T2], F32, name="page0")]
+        nc.vector.memset(pages[0][:], 0.0)
+
+        picks = lists.tile([P, S // 16], U16, name="picks")
+        nc.sync.dma_start(picks[:], offs)
+        for q in range(4):
+            nc.sync.dma_start(
+                tab_plane[32 * q + 24 : 32 * q + 32, :].bitcast(I32),
+                tab_scales[:, 4 * q : 4 * q + 4, :].bitcast(I32),
+            )
+        w1_raw = keep.tile([P, PASSES * 2 * H], U8, name="w1_raw", align_bytes=64)
+        nc.sync.dma_start(
+            w1_raw[:].bitcast(I32).rearrange("p (a c) -> p a c", a=PASSES),
+            w1_words.bitcast(I32).rearrange("a p c -> p a c"),
+        )
+        tab = []
+        for a in range(PASSES):
+            words = keep.tile([P, T], I32, name=f"tab{a}", tag=f"wide{a}", align_bytes=64)
+            nc.sync.dma_start(words[:], tab_words[a].rearrange("p t i -> p (t i)").bitcast(I32))
+            tab.append(words)
+            if a == 0:
+                for q in range(4):
+                    nc.sync.dma_start(
+                        w1_plane[32 * q : 32 * q + 4, :].bitcast(I32).rearrange("r (a c) -> r a c", a=PASSES),
+                        w1_scales[:, 4 * q : 4 * q + 4, :].bitcast(I32).rearrange("a r c -> r a c"),
+                    )
+        picked = keep.tile([P, S], U8, name="picked", align_bytes=64)
+        nc.vector.tensor_copy(picked[:], tab_plane[:].indirect(picks[:]))
+        for a in range(PASSES):
+            first = 24 + 4 * a
+            nc.scalar.dma_start(v_plane[a][0:100, :].bitcast(I32), picked[first : first + 100, :].bitcast(I32))
+        bias = keep.tile([P, SLICES], F32, name="bias")
+        nc.sync.dma_start(
+            bias[:].rearrange("p (b i) -> p b i", i=PACK), b1.rearrange("(b p i) -> p b i", b=PASSES, i=PACK)
+        )
+        places = lists.tile([P, S // 16], U16, name="places")
+        nc.sync.dma_start(places[:], offs2)
+        weights = keep.tile([P, S], F32, name="weights")
+        nc.sync.dma_start(weights[:], wgs)
+
+        ident = keep.tile([P, P], F32, name="ident")
+        make_identity(nc, ident[:])
+
+        road_rows = road.rearrange("(b p i) t -> b i p t", b=PASSES, i=PACK)
+
+        def load_road(k):
+            rows = roads.tile([P, T2], F32, name="road_rows")
+            nc.sync.dma_start(rows[:], road_rows[k // PACK, k % PACK])
+            return rows
+
+        road_tiles = [load_road(k) for k in range(2)]
+        w2_raw = []
+        for b in range(PASSES):
+            raw = keep.tile([P, PACK * N], F32, name=f"w2_raw{b}", tag=f"wide{2 + b}", align_bytes=64)
+            nc.sync.dma_start(
+                raw[:], w2[b * P * PACK : (b + 1) * P * PACK, :].rearrange("(p i) n -> p (i n)", i=PACK)
+            )
+            w2_raw.append(raw)
+        road_tiles.extend([load_road(k) for k in range(2, 4)])
+
+
+        w1_codes = keep.tile([P, PASSES * 2 * H], U8, name="w1_codes", align_bytes=64)
+        nc.vector.tensor_copy(
+            w1_codes[:].bitcast(U16).rearrange("p (g i m) -> p g i m", i=PACK, m=P),
+            w1_raw[:].bitcast(U16).rearrange("p (g m i) -> p g i m", i=PACK, m=P),
+        )
+        v_codes = {}
+
+        def gather_words(a, half):
+            words = keep.tile([P, BANK], U32, name=f"v_codes{a}{half}", align_bytes=64)
+            cols = slice(half * BANK // 16, (half + 1) * BANK // 16)
+            nc.vector.tensor_copy(words[:], tab[a][:].bitcast(U32).indirect(picks[:, cols]))
+            v_codes[a, half] = words
+
+        gather_words(0, 0)
+        w1_scale = keep.tile([P, PASSES * H], U8, name="w1_scale", align_bytes=64)
+        nc.vector.tensor_copy(
+            w1_scale[:].rearrange("p (g i m) -> p g i m", i=PACK, m=P),
+            w1_plane[:].rearrange("p (g m i) -> p g i m", i=PACK, m=P),
+        )
+        gather_words(1, 0)
+        gather_words(0, 1)
+        gather_words(1, 1)
+        for a in range(PASSES):
+            page = keep.tile([P, T2], F32, name=f"page{1 + a}", tag=f"wide{a}", align_bytes=64)
+            nc.gpsimd.memset(page[:], 0.0)
+            pages.append(page)
+
+        jam_tiles = []
+        for nt in range(N // P):
+            rows = keep.tile([P, T2], F32, name=f"jam{nt}")
+            nc.sync.dma_start(rows[:], jam[nt * P : (nt + 1) * P, :])
+            jam_tiles.append(rows)
+
+        h = []
+        for k in range(SLICES):
+            rows = keep.tile([P, S], F32, name=f"h{k}", tag=f"slot{k}", align_bytes=64)
+            for half in range(2):
+                bank = banks[(2 * k + half) % 8]
+                for a in range(PASSES):
+                    g = a * SLICES + k
+                    nc.tensor.matmul_mx(
+                        out=bank[:],
+                        lhsT=w1_codes[:, 2 * P * g : 2 * P * (g + 1)].bitcast(E2M1),
+                        lhsT_scale=w1_scale[:, P * g : P * (g + 1)],
+                        rhs=v_codes[a, half][:].bitcast(E4M3),
+                        rhs_scale=v_plane[a][:, half * BANK : (half + 1) * BANK],
+                        start=(a == 0),
+                        stop=(a == PASSES - 1),
+                    )
+                nc.scalar.activation(
+                    rows[:, half * BANK : (half + 1) * BANK], bank[:], RELU, bias=bias[:, k : k + 1]
+                )
+            h.append(rows)
+
+        w2_grouped = []
+        for b in range(PASSES):
+            raw = w2_raw[b]
+            grouped = keep.tile([P, PACK * N], BF16, name=f"w2_grouped{b}", align_bytes=64)
+            nc.scalar.copy(
+                grouped[:].rearrange("p (n i) -> p n i", i=PACK), raw[:].rearrange("p (i n) -> p n i", i=PACK)
+            )
+            w2_grouped.append(grouped)
+        page = keep.tile([P, T2], F32, name="page3", tag="wide2", align_bytes=64)
+        nc.gpsimd.memset(page[:], 0.0)
+        pages.append(page)
+
+        def scatter(k):
+            page = pages[k % 4]
+            pieces = 2 if k == 0 else 1
+            width = S // pieces
+            for piece in range(pieces):
+                cols = slice(piece * width, (piece + 1) * width)
+                idx = places[:, piece * width // 16 : (piece + 1) * width // 16]
+                nc.vector.tensor_tensor(page[:].indirect(idx), h[k][:, cols], weights[:, cols], MULT)
+
+        turned = [
+            [keep.tile([P, 2 * STRIP], BF16, name=f"turned{u}_{j}", align_bytes=64) for j in range(STRIPS)]
+            for u in range(2)
+        ]
+
+        def sum_bank(pair, j):
+            return banks[2 + (STRIPS * pair + j) % SUM_BANKS]
+
+        def turn(pair, j, source, e, start=False, stop=False):
+            bank = sum_bank(pair, j)
+            for s in range(2):
+                t0 = j * STRIP + s * P
+                c0 = (2 * s + e) * P
+                nc.tensor.matmul(
+                    bank[:, c0 : c0 + P],
+                    source[:, t0 : t0 + P],
+                    ident[:],
+                    start=(start and s == 0),
+                    stop=(stop and s == 1),
+                    is_transpose=True,
+                )
+
+        def turn_roads(pair, j):
+            turn(pair, j, road_tiles[2 * pair], 0, start=True)
+            turn(pair, j, road_tiles[2 * pair + 1], 1)
+
+        def round_strip(pair, j):
+            nc.scalar.copy(
+                turned[pair % 2][j][:].rearrange("t (s p e) -> t s p e", s=2, e=2),
+                sum_bank(pair, j)[:].rearrange("t (s e p) -> t s p e", s=2, e=2),
+            )
+
+        def open_strips(pair):
+            for j in range(SUM_BANKS):
+                turn_roads(pair, j)
+            for j in range(SUM_BANKS):
+                turn(pair, j, pages[2 * pair % 4], 0)
+
+        def close_strip(pair, j):
+            if j >= SUM_BANKS:
+                turn_roads(pair, j)
+                turn(pair, j, pages[2 * pair % 4], 0)
+            turn(pair, j, pages[(2 * pair + 1) % 4], 1, stop=True)
+            round_strip(pair, j)
+
+        def turn_back(b, c):
+            slot = c if b == 0 else 4 + c % 3
+            z = keep.tile([P, PACK * BANK], BF16, name=f"z{b}_{c}", tag=f"slot{slot}", align_bytes=64)
+            for jj in range(2):
+                j = 2 * c + jj
+                bank = banks[jj]
+                for u in range(2):
+                    for s in range(2):
+                        c0 = (2 * u + s) * P
+                        nc.tensor.transpose(
+                            bank[:, c0 : c0 + P], turned[u][j][:].bitcast(F32)[:, s * P : (s + 1) * P], ident[:]
+                        )
+                nc.scalar.copy(
+                    z[:].bitcast(F32)[:, jj * BANK : (jj + 1) * BANK].rearrange("p (t u) -> p t u", u=2),
+                    bank[:].rearrange("p (u t) -> p t u", u=2),
+                )
+            return z
+
+        z0 = []
+        for pair in range(3):
+            scatter(2 * pair)
+            scatter(2 * pair + 1)
+            open_strips(pair)
+            for c in range(CHUNKS):
+                close_strip(pair, 2 * c)
+                close_strip(pair, 2 * c + 1)
+                if pair == 1 and c > 0:
+                    z0.append(turn_back(0, c - 1))
+            if pair == 1:
+                z0.append(turn_back(0, CHUNKS - 1))
+            if pair < 2:
+                road_tiles.append(load_road(2 * pair + 4))
+                road_tiles.append(load_road(2 * pair + 5))
+        scatter(6)
+        scatter(7)
+        open_strips(3)
+
+        late_plane = keep.tile([P, PASSES * N + T2], U8, name="late_plane", tag="slot7", align_bytes=64)
+        w2_codes = keep.tile([P, PASSES * N], U32, name="w2_codes", align_bytes=64)
+        for b in range(PASSES):
+            nc.vector.quantize_mx(
+                out=w2_codes[:, b * N : (b + 1) * N].bitcast(E4M3),
+                scales=late_plane[:, b * N : (b + 1) * N],
+                in_=w2_grouped[b][:],
+            )
+        z_codes = {}
+        z_plane = {}
+        z1_plane = keep.tile([P, T2], U8, name="z1_plane", align_bytes=64)
+
+        def quantise(b, c, z):
+            codes = keep.tile([P, BANK], U32, name=f"z_codes{b}_{c}", align_bytes=64)
+            if b == 0:
+                plane = late_plane[:, PASSES * N + c * BANK : PASSES * N + (c + 1) * BANK]
+            else:
+                plane = z1_plane[:, c * BANK : (c + 1) * BANK]
+            nc.vector.quantize_mx(out=codes[:].bitcast(E4M3), scales=plane, in_=z[:])
+            z_codes[b, c] = codes
+            z_plane[b, c] = plane
+
+        for c in range(CHUNKS):
+            quantise(0, c, z0[c])
+
+        def finish(c):
+            cols = slice(c * BANK, (c + 1) * BANK)
+            for nt in range(N // P):
+                bank = banks[2 + (2 + 4 * c + nt) % SUM_BANKS]
+                for b in range(PASSES):
+                    w_cols = slice(b * N + nt * P, b * N + (nt + 1) * P)
+                    nc.tensor.matmul_mx(
+                        out=bank[:],
+                        lhsT=w2_codes[:, w_cols].bitcast(E4M3),
+                        lhsT_scale=late_plane[:, w_cols],
+                        rhs=z_codes[b, c][:].bitcast(E4M3),
+                        rhs_scale=z_plane[b, c],
+                        start=(b == 0),
+                        stop=(b == PASSES - 1),
+                    )
+                res = results.tile([P, BANK], F32, name="res")
+                nc.scalar.activation(res[:], bank[:], TANH)
+                nc.vector.tensor_tensor(res[:], res[:], jam_tiles[nt][:, cols], MULT)
+                nc.vector.tensor_tensor(res[:], res[:], bank[:], ADD)
+                nc.sync.dma_start(out[nt * P : (nt + 1) * P, cols], res[:])
+
+        for j in range(4):
+            close_strip(3, j)
+        quantise(1, 0, turn_back(1, 0))
+        close_strip(3, 4)
+        close_strip(3, 5)
+        quantise(1, 1, turn_back(1, 1))
+        close_strip(3, 6)
+        close_strip(3, 7)
+        finish(0)
+        quantise(1, 2, turn_back(1, 2))
+        finish(1)
+        quantise(1, 3, turn_back(1, 3))
+        finish(2)
+        finish(3)

@@ -37,15 +37,14 @@ def tile_list_courier_eta_banks_kernel(
     with ExitStack() as ctx:
         lists = ctx.enter_context(tc.tile_pool(name="lists", bufs=1))
         keep = ctx.enter_context(tc.tile_pool(name="keep", bufs=1))
-        roads = ctx.enter_context(tc.tile_pool(name="roads", bufs=4))
         results = ctx.enter_context(tc.tile_pool(name="results", bufs=6))
         psum = ctx.enter_context(tc.psum_pool(name="psum", bufs=1))
         banks = [psum.tile([P, BANK], F32, name=f"bank{j}") for j in range(8)]
 
-        tab_plane = keep.tile([P, T], U8, name="tab_plane", align_bytes=64)
+        tab_plane = keep.tile([P, T], U8, name="tab_plane", tag="road0", align_bytes=64)
         for q in range(4):
             nc.vector.memset(tab_plane[32 * q : 32 * q + 24, :].bitcast(I32), 0)
-        w1_plane = keep.tile([P, PASSES * H], U8, name="w1_plane", align_bytes=64)
+        w1_plane = keep.tile([P, PASSES * H], U8, name="w1_plane", tag="page2", align_bytes=64)
         nc.gpsimd.memset(w1_plane[:].bitcast(I32), 0)
         v_plane = [keep.tile([P, S], U8, name=f"v_plane{a}", align_bytes=64) for a in range(PASSES)]
         for a in range(PASSES):
@@ -60,7 +59,7 @@ def tile_list_courier_eta_banks_kernel(
                 tab_plane[32 * q + 24 : 32 * q + 32, :].bitcast(I32),
                 tab_scales[:, 4 * q : 4 * q + 4, :].bitcast(I32),
             )
-        w1_raw = keep.tile([P, PASSES * 2 * H], U8, name="w1_raw", align_bytes=64)
+        w1_raw = keep.tile([P, PASSES * 2 * H], U8, name="w1_raw", tag="page1", align_bytes=64)
         nc.sync.dma_start(
             w1_raw[:].bitcast(I32).rearrange("p (a c) -> p a c", a=PASSES),
             w1_words.bitcast(I32).rearrange("a p c -> p a c"),
@@ -96,11 +95,11 @@ def tile_list_courier_eta_banks_kernel(
         road_rows = road.rearrange("(b p i) t -> b i p t", b=PASSES, i=PACK)
 
         def load_road(k):
-            rows = roads.tile([P, T2], F32, name="road_rows")
+            rows = keep.tile([P, T2], F32, name=f"road{k}", tag=f"road{k % PACK}", align_bytes=64)
             nc.sync.dma_start(rows[:], road_rows[k // PACK, k % PACK])
             return rows
 
-        road_tiles = [load_road(k) for k in range(2)]
+        road_tiles = [load_road(k) for k in range(4)]
         w2_raw = []
         for b in range(PASSES):
             raw = keep.tile([P, PACK * N], F32, name=f"w2_raw{b}", tag=f"wide{2 + b}", align_bytes=64)
@@ -108,10 +107,9 @@ def tile_list_courier_eta_banks_kernel(
                 raw[:], w2[b * P * PACK : (b + 1) * P * PACK, :].rearrange("(p i) n -> p (i n)", i=PACK)
             )
             w2_raw.append(raw)
-        road_tiles.extend([load_road(k) for k in range(2, 4)])
 
 
-        w1_codes = keep.tile([P, PASSES * 2 * H], U8, name="w1_codes", align_bytes=64)
+        w1_codes = keep.tile([P, PASSES * 2 * H], U8, name="w1_codes", tag="pairs0", align_bytes=64)
         nc.vector.tensor_copy(
             w1_codes[:].bitcast(U16).rearrange("p (g i m) -> p g i m", i=PACK, m=P),
             w1_raw[:].bitcast(U16).rearrange("p (g m i) -> p g i m", i=PACK, m=P),
@@ -119,13 +117,13 @@ def tile_list_courier_eta_banks_kernel(
         v_codes = {}
 
         def gather_words(a, half):
-            words = keep.tile([P, BANK], U32, name=f"v_codes{a}{half}", align_bytes=64)
+            words = keep.tile([P, BANK], U32, name=f"v_codes{a}{half}", tag=f"codes{2 * a + half}", align_bytes=64)
             cols = slice(half * BANK // 16, (half + 1) * BANK // 16)
             nc.vector.tensor_copy(words[:], tab[a][:].bitcast(U32).indirect(picks[:, cols]))
             v_codes[a, half] = words
 
         gather_words(0, 0)
-        w1_scale = keep.tile([P, PASSES * H], U8, name="w1_scale", align_bytes=64)
+        w1_scale = keep.tile([P, PASSES * H], U8, name="w1_scale", tag="page3", align_bytes=64)
         nc.vector.tensor_copy(
             w1_scale[:].rearrange("p (g i m) -> p g i m", i=PACK, m=P),
             w1_plane[:].rearrange("p (g m i) -> p g i m", i=PACK, m=P),
@@ -134,21 +132,15 @@ def tile_list_courier_eta_banks_kernel(
         gather_words(0, 1)
         gather_words(1, 1)
         for a in range(PASSES):
-            page = keep.tile([P, T2], F32, name=f"page{1 + a}", tag=f"wide{a}", align_bytes=64)
+            page = keep.tile([P, T2], F32, name=f"page{1 + a}", tag=f"page{1 + a}", align_bytes=64)
             nc.gpsimd.memset(page[:], 0.0)
             pages.append(page)
-
-        jam_tiles = []
-        for nt in range(N // P):
-            rows = keep.tile([P, T2], F32, name=f"jam{nt}")
-            nc.sync.dma_start(rows[:], jam[nt * P : (nt + 1) * P, :])
-            jam_tiles.append(rows)
 
         h = []
         for k in range(SLICES):
             rows = keep.tile([P, S], F32, name=f"h{k}", tag=f"slot{k}", align_bytes=64)
             for half in range(2):
-                bank = banks[(2 * k + half) % 8]
+                bank = banks[(2 * k + half) % 3]
                 for a in range(PASSES):
                     g = a * SLICES + k
                     nc.tensor.matmul_mx(
@@ -173,18 +165,40 @@ def tile_list_courier_eta_banks_kernel(
                 grouped[:].rearrange("p (n i) -> p n i", i=PACK), raw[:].rearrange("p (i n) -> p n i", i=PACK)
             )
             w2_grouped.append(grouped)
-        page = keep.tile([P, T2], F32, name="page3", tag="wide2", align_bytes=64)
-        nc.gpsimd.memset(page[:], 0.0)
-        pages.append(page)
+        jam_tiles = []
+        for nt in range(N // P):
+            rows = keep.tile([P, T2], F32, name=f"jam{nt}", tag=f"wide{nt}", align_bytes=64)
+            nc.sync.dma_start(rows[:], jam[nt * P : (nt + 1) * P, :])
+            jam_tiles.append(rows)
+
+
+        def pieces_of(k):
+            width = S // 2 if k == 0 else S
+            return [slice(c0, c0 + width) for c0 in range(0, S, width)]
+
+        def weigh(k):
+            for cols in pieces_of(k):
+                nc.gpsimd.tensor_tensor(h[k][:, cols], h[k][:, cols], weights[:, cols], MULT)
 
         def scatter(k):
-            page = pages[k % 4]
-            pieces = 2 if k == 0 else 1
-            width = S // pieces
-            for piece in range(pieces):
-                cols = slice(piece * width, (piece + 1) * width)
-                idx = places[:, piece * width // 16 : (piece + 1) * width // 16]
-                nc.vector.tensor_tensor(page[:].indirect(idx), h[k][:, cols], weights[:, cols], MULT)
+            for cols in pieces_of(k):
+                idx = places[:, cols.start // 16 : cols.stop // 16]
+                nc.vector.tensor_copy(pages[k % 4][:].indirect(idx), h[k][:, cols])
+
+        pairs0 = keep.tile([P, 2 * T2 * 2], BF16, name="pairs0", tag="pairs0", align_bytes=64)
+
+        def add_road(k):
+            plane = pairs0[:].rearrange("p (u t e) -> p u t e", u=2, e=2)[:, k // 2, :, k % 2]
+            nc.gpsimd.tensor_tensor(plane, pages[k][:], road_tiles[k][:], ADD)
+            road_tiles.append(load_road(PACK + k))
+
+        def weave(c):
+            z = keep.tile([P, PACK * BANK], BF16, name=f"z0_{c}", tag=f"slot{c}", align_bytes=64)
+            words = pairs0[:].bitcast(F32).rearrange("p (u t) -> p t u", u=2)
+            nc.scalar.copy(
+                z[:].bitcast(F32).rearrange("p (t u) -> p t u", u=2), words[:, c * BANK : (c + 1) * BANK, :]
+            )
+            return z
 
         turned = [
             [keep.tile([P, 2 * STRIP], BF16, name=f"turned{u}_{j}", align_bytes=64) for j in range(STRIPS)]
@@ -249,22 +263,28 @@ def tile_list_courier_eta_banks_kernel(
                 )
             return z
 
-        z0 = []
-        for pair in range(3):
-            scatter(2 * pair)
-            scatter(2 * pair + 1)
-            open_strips(pair)
-            for c in range(CHUNKS):
-                close_strip(pair, 2 * c)
-                close_strip(pair, 2 * c + 1)
-                if pair == 1 and c > 0:
-                    z0.append(turn_back(0, c - 1))
-            if pair == 1:
-                z0.append(turn_back(0, CHUNKS - 1))
-            if pair < 2:
-                road_tiles.append(load_road(2 * pair + 4))
-                road_tiles.append(load_road(2 * pair + 5))
+        for k in range(PACK):
+            weigh(k)
+            if k == 3:
+                page = keep.tile([P, T2], F32, name="page3", tag="page3", align_bytes=64)
+                nc.gpsimd.memset(page[:], 0.0)
+                pages.append(page)
+            scatter(k)
+        add_road(0)
+        weigh(4)
+        scatter(4)
+        add_road(1)
+        weigh(5)
+        scatter(5)
+        add_road(2)
+        add_road(3)
+        open_strips(2)
+        for j in range(STRIPS):
+            close_strip(2, j)
+        z0 = [weave(c) for c in range(CHUNKS)]
+        weigh(6)
         scatter(6)
+        weigh(7)
         scatter(7)
         open_strips(3)
 
@@ -281,7 +301,7 @@ def tile_list_courier_eta_banks_kernel(
         z1_plane = keep.tile([P, T2], U8, name="z1_plane", align_bytes=64)
 
         def quantise(b, c, z):
-            codes = keep.tile([P, BANK], U32, name=f"z_codes{b}_{c}", align_bytes=64)
+            codes = keep.tile([P, BANK], U32, name=f"z_codes{b}_{c}", tag=f"codes{4 * b + c}", align_bytes=64)
             if b == 0:
                 plane = late_plane[:, PASSES * N + c * BANK : PASSES * N + (c + 1) * BANK]
             else:

@@ -24,10 +24,13 @@ PACK = 4
 BANK = 512
 PASSES = 2
 SLICES = PASSES * PACK
+CHUNKS = T2 // BANK
+PAGES = 3
 STRIP = 256
 STRIPS = T2 // STRIP
-CHUNKS = T2 // BANK
-SUM_BANKS = 6
+FIRST_BANKS = 3
+ORDER = (0, 1, 2, 3, 6, 4, 5, 7)
+FIRST_PIECES = (256, 256, 512)
 
 
 def tile_list_courier_eta_banks_kernel(
@@ -37,20 +40,19 @@ def tile_list_courier_eta_banks_kernel(
     with ExitStack() as ctx:
         lists = ctx.enter_context(tc.tile_pool(name="lists", bufs=1))
         keep = ctx.enter_context(tc.tile_pool(name="keep", bufs=1))
-        results = ctx.enter_context(tc.tile_pool(name="results", bufs=6))
+        results = ctx.enter_context(tc.tile_pool(name="results", bufs=3))
         psum = ctx.enter_context(tc.psum_pool(name="psum", bufs=1))
         banks = [psum.tile([P, BANK], F32, name=f"bank{j}") for j in range(8)]
 
+        w1_plane = keep.tile([P, PASSES * H], U8, name="w1_plane", tag="pairs0", align_bytes=64)
+        nc.gpsimd.memset(w1_plane[:].bitcast(I32), 0)
         tab_plane = keep.tile([P, T], U8, name="tab_plane", tag="road0", align_bytes=64)
         for q in range(4):
-            nc.vector.memset(tab_plane[32 * q : 32 * q + 24, :].bitcast(I32), 0)
-        w1_plane = keep.tile([P, PASSES * H], U8, name="w1_plane", tag="page2", align_bytes=64)
-        nc.gpsimd.memset(w1_plane[:].bitcast(I32), 0)
-        v_plane = [keep.tile([P, S], U8, name=f"v_plane{a}", align_bytes=64) for a in range(PASSES)]
-        for a in range(PASSES):
-            nc.gpsimd.memset(v_plane[a][96:128, :].bitcast(I32), 0)
+            nc.gpsimd.memset(tab_plane[32 * q : 32 * q + 24, :].bitcast(I32), 0)
+        v_plane = keep.tile([P, PASSES * S], U8, name="v_plane", align_bytes=64)
+        nc.gpsimd.memset(v_plane[96:128, :].bitcast(I32), 0)
         pages = [keep.tile([P, T2], F32, name="page0")]
-        nc.vector.memset(pages[0][:], 0.0)
+        nc.gpsimd.memset(pages[0][:], 0.0)
 
         picks = lists.tile([P, S // 16], U16, name="picks")
         nc.sync.dma_start(picks[:], offs)
@@ -64,22 +66,28 @@ def tile_list_courier_eta_banks_kernel(
             w1_raw[:].bitcast(I32).rearrange("p (a c) -> p a c", a=PASSES),
             w1_words.bitcast(I32).rearrange("a p c -> p a c"),
         )
-        tab = []
-        for a in range(PASSES):
-            words = keep.tile([P, T], I32, name=f"tab{a}", tag=f"wide{a}", align_bytes=64)
-            nc.sync.dma_start(words[:], tab_words[a].rearrange("p t i -> p (t i)").bitcast(I32))
-            tab.append(words)
-            if a == 0:
-                for q in range(4):
-                    nc.sync.dma_start(
-                        w1_plane[32 * q : 32 * q + 4, :].bitcast(I32).rearrange("r (a c) -> r a c", a=PASSES),
-                        w1_scales[:, 4 * q : 4 * q + 4, :].bitcast(I32).rearrange("a r c -> r a c"),
-                    )
+        tab = keep.tile([P, PASSES * T], I32, name="tab", tag="wide0", align_bytes=64)
+
+        def load_table(cols):
+            nc.sync.dma_start(
+                tab[:].rearrange("p (a t) -> p a t", a=PASSES)[:, :, cols],
+                tab_words.rearrange("a p t i -> p a (t i)").bitcast(I32)[:, :, cols],
+            )
+
+        load_table(slice(0, T // 2))
+        for q in range(4):
+            nc.sync.dma_start(
+                w1_plane[32 * q : 32 * q + 4, :].bitcast(I32).rearrange("r (a c) -> r a c", a=PASSES),
+                w1_scales[:, 4 * q : 4 * q + 4, :].bitcast(I32).rearrange("a r c -> r a c"),
+            )
+        load_table(slice(T // 2, T))
         picked = keep.tile([P, S], U8, name="picked", align_bytes=64)
         nc.vector.tensor_copy(picked[:], tab_plane[:].indirect(picks[:]))
         for a in range(PASSES):
             first = 24 + 4 * a
-            nc.scalar.dma_start(v_plane[a][0:100, :].bitcast(I32), picked[first : first + 100, :].bitcast(I32))
+            nc.scalar.dma_start(
+                v_plane[0:100, a * S : (a + 1) * S].bitcast(I32), picked[first : first + 100, :].bitcast(I32)
+            )
         bias = keep.tile([P, SLICES], F32, name="bias")
         nc.sync.dma_start(
             bias[:].rearrange("p (b i) -> p b i", i=PACK), b1.rearrange("(b p i) -> p b i", b=PASSES, i=PACK)
@@ -89,58 +97,55 @@ def tile_list_courier_eta_banks_kernel(
         weights = keep.tile([P, S], F32, name="weights")
         nc.sync.dma_start(weights[:], wgs)
 
-        ident = keep.tile([P, P], F32, name="ident")
-        make_identity(nc, ident[:])
-
         road_rows = road.rearrange("(b p i) t -> b i p t", b=PASSES, i=PACK)
+        roads = {}
 
-        def load_road(k):
-            rows = keep.tile([P, T2], F32, name=f"road{k}", tag=f"road{k % PACK}", align_bytes=64)
-            nc.sync.dma_start(rows[:], road_rows[k // PACK, k % PACK])
-            return rows
+        def load_road(step):
+            k = ORDER[step]
+            roads[k] = keep.tile([P, T2], F32, name=f"road{k}", tag=f"road{step % PACK}", align_bytes=64)
+            nc.sync.dma_start(roads[k][:], road_rows[k // PACK, k % PACK])
 
-        road_tiles = [load_road(k) for k in range(4)]
-        w2_raw = []
-        for b in range(PASSES):
-            raw = keep.tile([P, PACK * N], F32, name=f"w2_raw{b}", tag=f"wide{2 + b}", align_bytes=64)
-            nc.sync.dma_start(
-                raw[:], w2[b * P * PACK : (b + 1) * P * PACK, :].rearrange("(p i) n -> p (i n)", i=PACK)
-            )
-            w2_raw.append(raw)
+        load_road(0)
+        load_road(1)
+        w2_raw = keep.tile([P, PASSES * PACK * N], F32, name="w2_raw", tag="wide1", align_bytes=64)
+        nc.sync.dma_start(
+            w2_raw[:].rearrange("p (b c) -> p b c", b=PASSES),
+            w2.rearrange("(b p i) n -> p b (i n)", b=PASSES, i=PACK),
+        )
+        load_road(2)
+        load_road(3)
 
-
+        w1_scale = keep.tile([P, PASSES * H], U8, name="w1_scale", tag="page2", align_bytes=64)
+        nc.vector.tensor_copy(
+            w1_scale[:].rearrange("p (g i m) -> p g i m", i=PACK, m=P),
+            w1_plane[:].rearrange("p (g m i) -> p g i m", i=PACK, m=P),
+        )
         w1_codes = keep.tile([P, PASSES * 2 * H], U8, name="w1_codes", tag="pairs0", align_bytes=64)
         nc.vector.tensor_copy(
             w1_codes[:].bitcast(U16).rearrange("p (g i m) -> p g i m", i=PACK, m=P),
             w1_raw[:].bitcast(U16).rearrange("p (g m i) -> p g i m", i=PACK, m=P),
         )
+        pages.append(keep.tile([P, T2], F32, name="page1", tag="page1", align_bytes=64))
+        nc.gpsimd.memset(pages[1][:], 0.0)
         v_codes = {}
+        for half in range(2):
+            for a in range(PASSES):
+                words = keep.tile(
+                    [P, BANK], U32, name=f"v_codes{a}{half}", tag=f"codes{2 * a + half}", align_bytes=64
+                )
+                entries = picks[:, half * BANK // 16 : (half + 1) * BANK // 16]
+                nc.vector.tensor_copy(words[:], tab[:, a * T : (a + 1) * T].bitcast(U32).indirect(entries))
+                v_codes[a, half] = words
 
-        def gather_words(a, half):
-            words = keep.tile([P, BANK], U32, name=f"v_codes{a}{half}", tag=f"codes{2 * a + half}", align_bytes=64)
-            cols = slice(half * BANK // 16, (half + 1) * BANK // 16)
-            nc.vector.tensor_copy(words[:], tab[a][:].bitcast(U32).indirect(picks[:, cols]))
-            v_codes[a, half] = words
+        def pieces_of(k):
+            widths = FIRST_PIECES if k == ORDER[0] else (S,)
+            return [slice(sum(widths[:j]), sum(widths[: j + 1])) for j in range(len(widths))]
 
-        gather_words(0, 0)
-        w1_scale = keep.tile([P, PASSES * H], U8, name="w1_scale", tag="page3", align_bytes=64)
-        nc.vector.tensor_copy(
-            w1_scale[:].rearrange("p (g i m) -> p g i m", i=PACK, m=P),
-            w1_plane[:].rearrange("p (g m i) -> p g i m", i=PACK, m=P),
-        )
-        gather_words(1, 0)
-        gather_words(0, 1)
-        gather_words(1, 1)
-        for a in range(PASSES):
-            page = keep.tile([P, T2], F32, name=f"page{1 + a}", tag=f"page{1 + a}", align_bytes=64)
-            nc.gpsimd.memset(page[:], 0.0)
-            pages.append(page)
-
-        h = []
-        for k in range(SLICES):
-            rows = keep.tile([P, S], F32, name=f"h{k}", tag=f"slot{k}", align_bytes=64)
+        h = {}
+        for step, k in enumerate(ORDER):
+            h[k] = keep.tile([P, S], F32, name=f"h{k}", tag=f"slot{step}", align_bytes=64)
             for half in range(2):
-                bank = banks[(2 * k + half) % 3]
+                bank = banks[(2 * step + half) % FIRST_BANKS]
                 for a in range(PASSES):
                     g = a * SLICES + k
                     nc.tensor.matmul_mx(
@@ -148,73 +153,65 @@ def tile_list_courier_eta_banks_kernel(
                         lhsT=w1_codes[:, 2 * P * g : 2 * P * (g + 1)].bitcast(E2M1),
                         lhsT_scale=w1_scale[:, P * g : P * (g + 1)],
                         rhs=v_codes[a, half][:].bitcast(E4M3),
-                        rhs_scale=v_plane[a][:, half * BANK : (half + 1) * BANK],
+                        rhs_scale=v_plane[:, a * S + half * BANK : a * S + (half + 1) * BANK],
                         start=(a == 0),
                         stop=(a == PASSES - 1),
                     )
-                nc.scalar.activation(
-                    rows[:, half * BANK : (half + 1) * BANK], bank[:], RELU, bias=bias[:, k : k + 1]
-                )
-            h.append(rows)
+                for cols in pieces_of(k):
+                    lo, hi = max(cols.start, half * BANK), min(cols.stop, (half + 1) * BANK)
+                    if lo < hi:
+                        nc.scalar.activation(
+                            h[k][:, lo:hi],
+                            bank[:, lo - half * BANK : hi - half * BANK],
+                            RELU,
+                            bias=bias[:, k : k + 1],
+                        )
 
-        w2_grouped = []
+        w2_grouped = keep.tile([P, PASSES * PACK * N], BF16, name="w2_grouped", tag="codes0", align_bytes=64)
         for b in range(PASSES):
-            raw = w2_raw[b]
-            grouped = keep.tile([P, PACK * N], BF16, name=f"w2_grouped{b}", align_bytes=64)
+            cols = slice(b * PACK * N, (b + 1) * PACK * N)
             nc.scalar.copy(
-                grouped[:].rearrange("p (n i) -> p n i", i=PACK), raw[:].rearrange("p (i n) -> p n i", i=PACK)
+                w2_grouped[:, cols].rearrange("p (n i) -> p n i", i=PACK),
+                w2_raw[:, cols].rearrange("p (i n) -> p n i", i=PACK),
             )
-            w2_grouped.append(grouped)
-        jam_tiles = []
-        for nt in range(N // P):
-            rows = keep.tile([P, T2], F32, name=f"jam{nt}", tag=f"wide{nt}", align_bytes=64)
-            nc.sync.dma_start(rows[:], jam[nt * P : (nt + 1) * P, :])
-            jam_tiles.append(rows)
+        jams = []
+        for u in range(2):
+            rows = keep.tile([P, 2 * T2], F32, name=f"jam{u}", tag=f"wide{u}", align_bytes=64)
+            nc.sync.dma_start(
+                rows[:].rearrange("p (e t) -> p e t", e=2),
+                jam[2 * u * P : 2 * (u + 1) * P, :].rearrange("(e p) t -> p e t", e=2),
+            )
+            jams.append(rows[:].rearrange("p (e t) -> p e t", e=2))
 
+        page_of = {}
 
-        def pieces_of(k):
-            width = S // 2 if k == 0 else S
-            return [slice(c0, c0 + width) for c0 in range(0, S, width)]
-
-        def weigh(k):
+        def weigh(step):
+            k = ORDER[step]
             for cols in pieces_of(k):
                 nc.gpsimd.tensor_tensor(h[k][:, cols], h[k][:, cols], weights[:, cols], MULT)
 
-        def scatter(k):
+        def put(step):
+            k = ORDER[step]
+            page_of[k] = pages[step % PAGES]
             for cols in pieces_of(k):
-                idx = places[:, cols.start // 16 : cols.stop // 16]
-                nc.vector.tensor_copy(pages[k % 4][:].indirect(idx), h[k][:, cols])
+                entries = places[:, cols.start // 16 : cols.stop // 16]
+                nc.vector.tensor_copy(page_of[k][:].indirect(entries), h[k][:, cols])
 
-        pairs0 = keep.tile([P, 2 * T2 * 2], BF16, name="pairs0", tag="pairs0", align_bytes=64)
-
-        def add_road(k):
-            plane = pairs0[:].rearrange("p (u t e) -> p u t e", u=2, e=2)[:, k // 2, :, k % 2]
-            nc.gpsimd.tensor_tensor(plane, pages[k][:], road_tiles[k][:], ADD)
-            road_tiles.append(load_road(PACK + k))
-
-        def weave(c):
-            z = keep.tile([P, PACK * BANK], BF16, name=f"z0_{c}", tag=f"slot{c}", align_bytes=64)
-            words = pairs0[:].bitcast(F32).rearrange("p (u t) -> p t u", u=2)
-            nc.scalar.copy(
-                z[:].bitcast(F32).rearrange("p (t u) -> p t u", u=2), words[:, c * BANK : (c + 1) * BANK, :]
-            )
-            return z
-
-        turned = [
-            [keep.tile([P, 2 * STRIP], BF16, name=f"turned{u}_{j}", align_bytes=64) for j in range(STRIPS)]
-            for u in range(2)
+        pairs = [
+            keep.tile([P, 2 * T2 * 2], BF16, name=f"pairs{b}", tag=f"pairs{b}", align_bytes=64) for b in range(PASSES)
         ]
 
-        def sum_bank(pair, j):
-            return banks[2 + (STRIPS * pair + j) % SUM_BANKS]
+        def add_road(engine, k, cols):
+            b, i = divmod(k, PACK)
+            plane = pairs[b][:].rearrange("p (u t e) -> p u t e", u=2, e=2)[:, i // 2, cols, i % 2]
+            engine.tensor_tensor(plane, page_of[k][:, cols], roads[k][:, cols], ADD)
 
-        def turn(pair, j, source, e, start=False, stop=False):
-            bank = sum_bank(pair, j)
+        def turn(j, source, e, start=False, stop=False):
             for s in range(2):
                 t0 = j * STRIP + s * P
                 c0 = (2 * s + e) * P
                 nc.tensor.matmul(
-                    bank[:, c0 : c0 + P],
+                    banks[j][:, c0 : c0 + P],
                     source[:, t0 : t0 + P],
                     ident[:],
                     start=(start and s == 0),
@@ -222,80 +219,69 @@ def tile_list_courier_eta_banks_kernel(
                     is_transpose=True,
                 )
 
-        def turn_roads(pair, j):
-            turn(pair, j, road_tiles[2 * pair], 0, start=True)
-            turn(pair, j, road_tiles[2 * pair + 1], 1)
-
-        def round_strip(pair, j):
-            nc.scalar.copy(
-                turned[pair % 2][j][:].rearrange("t (s p e) -> t s p e", s=2, e=2),
-                sum_bank(pair, j)[:].rearrange("t (s e p) -> t s p e", s=2, e=2),
-            )
-
-        def open_strips(pair):
-            for j in range(SUM_BANKS):
-                turn_roads(pair, j)
-            for j in range(SUM_BANKS):
-                turn(pair, j, pages[2 * pair % 4], 0)
-
-        def close_strip(pair, j):
-            if j >= SUM_BANKS:
-                turn_roads(pair, j)
-                turn(pair, j, pages[2 * pair % 4], 0)
-            turn(pair, j, pages[(2 * pair + 1) % 4], 1, stop=True)
-            round_strip(pair, j)
-
-        def turn_back(b, c):
-            slot = c if b == 0 else 4 + c % 3
+        def weave(b, c):
+            slot = c if b == 0 else (5, 6, 0, 1)[c]
             z = keep.tile([P, PACK * BANK], BF16, name=f"z{b}_{c}", tag=f"slot{slot}", align_bytes=64)
-            for jj in range(2):
-                j = 2 * c + jj
-                bank = banks[jj]
-                for u in range(2):
-                    for s in range(2):
-                        c0 = (2 * u + s) * P
-                        nc.tensor.transpose(
-                            bank[:, c0 : c0 + P], turned[u][j][:].bitcast(F32)[:, s * P : (s + 1) * P], ident[:]
-                        )
-                nc.scalar.copy(
-                    z[:].bitcast(F32)[:, jj * BANK : (jj + 1) * BANK].rearrange("p (t u) -> p t u", u=2),
-                    bank[:].rearrange("p (u t) -> p t u", u=2),
-                )
+            words = pairs[b][:].bitcast(F32).rearrange("p (u t) -> p t u", u=2)
+            nc.scalar.copy(
+                z[:].bitcast(F32).rearrange("p (t u) -> p t u", u=2), words[:, c * BANK : (c + 1) * BANK, :]
+            )
             return z
 
-        for k in range(PACK):
-            weigh(k)
-            if k == 3:
-                page = keep.tile([P, T2], F32, name="page3", tag="page3", align_bytes=64)
-                nc.gpsimd.memset(page[:], 0.0)
-                pages.append(page)
-            scatter(k)
-        add_road(0)
+        whole = slice(0, T2)
+        for step in range(PACK):
+            weigh(step)
+        put(0)
+        put(1)
+        pages.append(keep.tile([P, T2], F32, name="page2", tag="page2", align_bytes=64))
+        nc.gpsimd.memset(pages[2][:], 0.0)
+        ident = keep.tile([P, P], F32, name="ident", tag="codes1", align_bytes=64)
+        make_identity(nc, ident[:])
+        put(2)
+        add_road(nc.gpsimd, 0, whole)
+        load_road(4)
+        put(3)
         weigh(4)
-        scatter(4)
-        add_road(1)
-        weigh(5)
-        scatter(5)
-        add_road(2)
-        add_road(3)
-        open_strips(2)
-        for j in range(STRIPS):
-            close_strip(2, j)
-        z0 = [weave(c) for c in range(CHUNKS)]
-        weigh(6)
-        scatter(6)
-        weigh(7)
-        scatter(7)
-        open_strips(3)
-
-        late_plane = keep.tile([P, PASSES * N + T2], U8, name="late_plane", tag="slot7", align_bytes=64)
+        add_road(nc.gpsimd, 1, whole)
+        load_road(5)
+        put(4)
+        for step in range(5, SLICES):
+            weigh(step)
+        w2_plane = keep.tile([P, PASSES * N], U8, name="w2_plane", tag="slot4", align_bytes=64)
         w2_codes = keep.tile([P, PASSES * N], U32, name="w2_codes", align_bytes=64)
-        for b in range(PASSES):
-            nc.vector.quantize_mx(
-                out=w2_codes[:, b * N : (b + 1) * N].bitcast(E4M3),
-                scales=late_plane[:, b * N : (b + 1) * N],
-                in_=w2_grouped[b][:],
+        nc.vector.quantize_mx(out=w2_codes[:].bitcast(E4M3), scales=w2_plane[:], in_=w2_grouped[:])
+        for j in range(STRIPS):
+            turn(j, roads[2], 0, start=True)
+            turn(j, roads[3], 1)
+        load_road(6)
+        load_road(7)
+        for j in range(STRIPS):
+            turn(j, page_of[2], 0)
+        turned = []
+        for j in range(STRIPS):
+            turn(j, page_of[3], 1, stop=True)
+            strip = keep.tile([P, 2 * STRIP], BF16, name=f"turned{j}", align_bytes=64)
+            nc.scalar.copy(
+                strip[:].rearrange("t (s p e) -> t s p e", s=2, e=2),
+                banks[j][:].rearrange("t (s e p) -> t s p e", s=2, e=2),
             )
+            turned.append(strip)
+        for c in range(CHUNKS):
+            for s in range(PACK):
+                words = turned[2 * c + s // 2][:].bitcast(F32)
+                nc.tensor.transpose(
+                    banks[c][:, s * P : (s + 1) * P], words[:, (s % 2) * P : (s % 2 + 1) * P], ident[:]
+                )
+            nc.scalar.copy(pairs[0][:].bitcast(F32)[:, T2 + c * BANK : T2 + (c + 1) * BANK], banks[c][:])
+        z0 = [weave(0, c) for c in range(CHUNKS)]
+        put(5)
+        put(6)
+        add_road(nc.gpsimd, ORDER[4], whole)
+        put(7)
+        add_road(nc.gpsimd, ORDER[5], whole)
+        add_road(nc.gpsimd, ORDER[6], whole)
+
+        late_plane = keep.tile([P, T2], U8, name="late_plane", tag="slot7", align_bytes=64)
         z_codes = {}
         z_plane = {}
         z1_plane = keep.tile([P, T2], U8, name="z1_plane", align_bytes=64)
@@ -303,48 +289,68 @@ def tile_list_courier_eta_banks_kernel(
         def quantise(b, c, z):
             codes = keep.tile([P, BANK], U32, name=f"z_codes{b}_{c}", tag=f"codes{4 * b + c}", align_bytes=64)
             if b == 0:
-                plane = late_plane[:, PASSES * N + c * BANK : PASSES * N + (c + 1) * BANK]
+                plane = late_plane[:, c * BANK : (c + 1) * BANK]
             else:
                 plane = z1_plane[:, c * BANK : (c + 1) * BANK]
             nc.vector.quantize_mx(out=codes[:].bitcast(E4M3), scales=plane, in_=z[:])
             z_codes[b, c] = codes
             z_plane[b, c] = plane
 
-        for c in range(CHUNKS):
-            quantise(0, c, z0[c])
+        def last_sum(c):
+            add_road(nc.vector, ORDER[-1], slice(c * BANK, (c + 1) * BANK))
+            return weave(1, c)
+
+        def bank_of(c, nt):
+            return banks[(4 * c + nt) % 8]
+
+        def multiply(c, nt, curve):
+            bank = bank_of(c, nt)
+            for b in range(PASSES):
+                w_cols = slice(b * N + nt * P, b * N + (nt + 1) * P)
+                nc.tensor.matmul_mx(
+                    out=bank[:],
+                    lhsT=w2_codes[:, w_cols].bitcast(E4M3),
+                    lhsT_scale=w2_plane[:, w_cols],
+                    rhs=z_codes[b, c][:].bitcast(E4M3),
+                    rhs_scale=z_plane[b, c],
+                    start=(b == 0),
+                    stop=(b == PASSES - 1),
+                )
+            nc.scalar.activation(curve[:, nt % 2, :], bank[:], TANH)
+
+        def add_and_store(c, nt, delay):
+            nc.vector.tensor_tensor(delay[:, nt % 2, :], delay[:, nt % 2, :], bank_of(c, nt)[:], ADD)
+            nc.sync.dma_start(out[nt * P : (nt + 1) * P, c * BANK : (c + 1) * BANK], delay[:, nt % 2, :])
+
+        held = []
 
         def finish(c):
             cols = slice(c * BANK, (c + 1) * BANK)
-            for nt in range(N // P):
-                bank = banks[2 + (2 + 4 * c + nt) % SUM_BANKS]
-                for b in range(PASSES):
-                    w_cols = slice(b * N + nt * P, b * N + (nt + 1) * P)
-                    nc.tensor.matmul_mx(
-                        out=bank[:],
-                        lhsT=w2_codes[:, w_cols].bitcast(E4M3),
-                        lhsT_scale=late_plane[:, w_cols],
-                        rhs=z_codes[b, c][:].bitcast(E4M3),
-                        rhs_scale=z_plane[b, c],
-                        start=(b == 0),
-                        stop=(b == PASSES - 1),
-                    )
-                res = results.tile([P, BANK], F32, name="res")
-                nc.scalar.activation(res[:], bank[:], TANH)
-                nc.vector.tensor_tensor(res[:], res[:], jam_tiles[nt][:, cols], MULT)
-                nc.vector.tensor_tensor(res[:], res[:], bank[:], ADD)
-                nc.sync.dma_start(out[nt * P : (nt + 1) * P, cols], res[:])
+            low = results.tile([P, 2, BANK], F32, name="curve_low")
+            high = results.tile([P, 2, BANK], F32, name="curve_high", bufs=2)
+            delay = results.tile([P, 2, BANK], F32, name="delay_low")
+            for nt in range(4):
+                multiply(c, nt, low if nt < 2 else high)
+            nc.vector.tensor_tensor(delay[:], low[:], jams[0][:, :, cols], MULT)
+            shared = 1 if c == 0 else 2
+            nc.gpsimd.tensor_tensor(low[:, :shared, :], high[:, :shared, :], jams[1][:, :shared, cols], MULT)
+            for args in held:
+                add_and_store(*args)
+            held.clear()
+            add_and_store(c, 0, delay)
+            add_and_store(c, 1, delay)
+            if shared < 2:
+                nc.vector.tensor_tensor(low[:, 1, :], high[:, 1, :], jams[1][:, 1, cols], MULT)
+            held.extend([(c, 2, low), (c, 3, low)])
 
-        for j in range(4):
-            close_strip(3, j)
-        quantise(1, 0, turn_back(1, 0))
-        close_strip(3, 4)
-        close_strip(3, 5)
-        quantise(1, 1, turn_back(1, 1))
-        close_strip(3, 6)
-        close_strip(3, 7)
-        finish(0)
-        quantise(1, 2, turn_back(1, 2))
-        finish(1)
-        quantise(1, 3, turn_back(1, 3))
-        finish(2)
-        finish(3)
+        z1 = [last_sum(0), last_sum(1)]
+        for c in range(CHUNKS):
+            quantise(0, c, z0[c])
+            quantise(1, c, z1[c])
+            if c + 2 < CHUNKS:
+                z1.append(last_sum(c + 2))
+            if c > 0:
+                finish(c - 1)
+        finish(CHUNKS - 1)
+        for args in held:
+            add_and_store(*args)

@@ -29,7 +29,7 @@ PAGES = 3
 STRIP = 256
 STRIPS = T2 // STRIP
 FIRST_BANKS = 3
-ORDER = (0, 1, 2, 3, 6, 4, 5, 7)
+ORDER = (0, 1, 2, 3, 4, 5, 6, 7)
 FIRST_PIECES = (256, 256, 512)
 
 
@@ -40,28 +40,29 @@ def tile_list_courier_eta_banks_kernel(
     with ExitStack() as ctx:
         lists = ctx.enter_context(tc.tile_pool(name="lists", bufs=1))
         keep = ctx.enter_context(tc.tile_pool(name="keep", bufs=1))
-        results = ctx.enter_context(tc.tile_pool(name="results", bufs=3))
+        results = ctx.enter_context(tc.tile_pool(name="results", bufs=6))
         psum = ctx.enter_context(tc.psum_pool(name="psum", bufs=1))
         banks = [psum.tile([P, BANK], F32, name=f"bank{j}") for j in range(8)]
 
-        w1_plane = keep.tile([P, PASSES * H], U8, name="w1_plane", tag="pairs0", align_bytes=64)
+        w1_plane = keep.tile([P, PASSES * H], U8, name="w1_plane", tag="page2", align_bytes=64)
         nc.gpsimd.memset(w1_plane[:].bitcast(I32), 0)
-        tab_plane = keep.tile([P, T], U8, name="tab_plane", tag="road0", align_bytes=64)
+        tab_plane = keep.tile([P, T + 4], U8, name="tab_plane", tag="road0", align_bytes=64)
         for q in range(4):
-            nc.gpsimd.memset(tab_plane[32 * q : 32 * q + 24, :].bitcast(I32), 0)
+            nc.vector.memset(tab_plane[32 * q : 32 * q + 24, :].bitcast(I32), 0)
         v_plane = keep.tile([P, PASSES * S], U8, name="v_plane", align_bytes=64)
         nc.gpsimd.memset(v_plane[96:128, :].bitcast(I32), 0)
-        pages = [keep.tile([P, T2], F32, name="page0")]
-        nc.gpsimd.memset(pages[0][:], 0.0)
+        pages = [keep.tile([P, T2], F32, name=f"page{j}") for j in range(2)]
+        for page in pages:
+            nc.gpsimd.memset(page[:], 0.0)
 
         picks = lists.tile([P, S // 16], U16, name="picks")
         nc.sync.dma_start(picks[:], offs)
         for q in range(4):
             nc.sync.dma_start(
-                tab_plane[32 * q + 24 : 32 * q + 32, :].bitcast(I32),
+                tab_plane[32 * q + 24 : 32 * q + 32, :T].bitcast(I32),
                 tab_scales[:, 4 * q : 4 * q + 4, :].bitcast(I32),
             )
-        w1_raw = keep.tile([P, PASSES * 2 * H], U8, name="w1_raw", tag="page1", align_bytes=64)
+        w1_raw = keep.tile([P, PASSES * 2 * H], U8, name="w1_raw", tag="w1", align_bytes=64)
         nc.sync.dma_start(
             w1_raw[:].bitcast(I32).rearrange("p (a c) -> p a c", a=PASSES),
             w1_words.bitcast(I32).rearrange("a p c -> p a c"),
@@ -82,10 +83,10 @@ def tile_list_courier_eta_banks_kernel(
             )
         load_table(slice(T // 2, T))
         picked = keep.tile([P, S], U8, name="picked", align_bytes=64)
-        nc.vector.tensor_copy(picked[:], tab_plane[:].indirect(picks[:]))
+        nc.vector.tensor_copy(picked[:], tab_plane[:, :T].indirect(picks[:]))
         for a in range(PASSES):
             first = 24 + 4 * a
-            nc.scalar.dma_start(
+            (nc.scalar, nc.sync)[a].dma_start(
                 v_plane[0:100, a * S : (a + 1) * S].bitcast(I32), picked[first : first + 100, :].bitcast(I32)
             )
         bias = keep.tile([P, SLICES], F32, name="bias")
@@ -115,18 +116,18 @@ def tile_list_courier_eta_banks_kernel(
         load_road(2)
         load_road(3)
 
-        w1_scale = keep.tile([P, PASSES * H], U8, name="w1_scale", tag="page2", align_bytes=64)
-        nc.vector.tensor_copy(
-            w1_scale[:].rearrange("p (g i m) -> p g i m", i=PACK, m=P),
-            w1_plane[:].rearrange("p (g m i) -> p g i m", i=PACK, m=P),
-        )
         w1_codes = keep.tile([P, PASSES * 2 * H], U8, name="w1_codes", tag="pairs0", align_bytes=64)
         nc.vector.tensor_copy(
             w1_codes[:].bitcast(U16).rearrange("p (g i m) -> p g i m", i=PACK, m=P),
             w1_raw[:].bitcast(U16).rearrange("p (g m i) -> p g i m", i=PACK, m=P),
         )
-        pages.append(keep.tile([P, T2], F32, name="page1", tag="page1", align_bytes=64))
-        nc.gpsimd.memset(pages[1][:], 0.0)
+        w1_scale = keep.tile([P, PASSES * H], U8, name="w1_scale", tag="w1", align_bytes=64)
+        nc.vector.tensor_copy(
+            w1_scale[:].rearrange("p (g i m) -> p g i m", i=PACK, m=P),
+            w1_plane[:].rearrange("p (g m i) -> p g i m", i=PACK, m=P),
+        )
+        pages.append(keep.tile([P, T2], F32, name="page2", tag="page2", align_bytes=64))
+        nc.gpsimd.memset(pages[2][:], 0.0)
         v_codes = {}
         for half in range(2):
             for a in range(PASSES):
@@ -203,7 +204,10 @@ def tile_list_courier_eta_banks_kernel(
 
         def add_road(engine, k, cols):
             b, i = divmod(k, PACK)
-            plane = pairs[b][:].rearrange("p (u t e) -> p u t e", u=2, e=2)[:, i // 2, cols, i % 2]
+            if b == 0:
+                plane = pairs[b][:].rearrange("p (u t e) -> p u t e", u=2, e=2)[:, i // 2, cols, i % 2]
+            else:
+                plane = pairs[b][:].rearrange("p (i t) -> p i t", i=PACK)[:, i, cols]
             engine.tensor_tensor(plane, page_of[k][:, cols], roads[k][:, cols], ADD)
 
         def turn(j, source, e, start=False, stop=False):
@@ -220,36 +224,34 @@ def tile_list_courier_eta_banks_kernel(
                 )
 
         def weave(b, c):
-            slot = c if b == 0 else (5, 6, 0, 1)[c]
-            z = keep.tile([P, PACK * BANK], BF16, name=f"z{b}_{c}", tag=f"slot{slot}", align_bytes=64)
-            words = pairs[b][:].bitcast(F32).rearrange("p (u t) -> p t u", u=2)
-            nc.scalar.copy(
-                z[:].bitcast(F32).rearrange("p (t u) -> p t u", u=2), words[:, c * BANK : (c + 1) * BANK, :]
-            )
+            tag = f"slot{PACK * b + c}" if b == 0 or c < 2 else f"codes{PACK + c - 2}"
+            z = keep.tile([P, PACK * BANK], BF16, name=f"z{b}_{c}", tag=tag, align_bytes=64)
+            cols = slice(c * BANK, (c + 1) * BANK)
+            if b == 0:
+                words = pairs[b][:].bitcast(F32).rearrange("p (u t) -> p t u", u=2)
+                nc.scalar.copy(z[:].bitcast(F32).rearrange("p (t u) -> p t u", u=2), words[:, cols, :])
+            else:
+                planes = pairs[b][:].rearrange("p (i t) -> p i t", i=PACK)[:, :, cols]
+                nc.scalar.copy(
+                    z[:].rearrange("p (g t i) -> p g i t", t=PACK, i=PACK),
+                    planes.rearrange("p i (g t) -> p g i t", t=PACK),
+                )
             return z
 
         whole = slice(0, T2)
         for step in range(PACK):
             weigh(step)
-        put(0)
-        put(1)
-        pages.append(keep.tile([P, T2], F32, name="page2", tag="page2", align_bytes=64))
-        nc.gpsimd.memset(pages[2][:], 0.0)
+        for step in range(PAGES):
+            put(step)
         ident = keep.tile([P, P], F32, name="ident", tag="codes1", align_bytes=64)
         make_identity(nc, ident[:])
-        put(2)
-        add_road(nc.gpsimd, 0, whole)
-        load_road(4)
-        put(3)
-        weigh(4)
-        add_road(nc.gpsimd, 1, whole)
-        load_road(5)
-        put(4)
-        for step in range(5, SLICES):
-            weigh(step)
-        w2_plane = keep.tile([P, PASSES * N], U8, name="w2_plane", tag="slot4", align_bytes=64)
-        w2_codes = keep.tile([P, PASSES * N], U32, name="w2_codes", align_bytes=64)
-        nc.vector.quantize_mx(out=w2_codes[:].bitcast(E4M3), scales=w2_plane[:], in_=w2_grouped[:])
+        for step in range(2):
+            add_road(nc.gpsimd, step, whole)
+            load_road(step + PACK)
+            weigh(step + PACK)
+            put(step + PAGES)
+        weigh(6)
+        weigh(7)
         for j in range(STRIPS):
             turn(j, roads[2], 0, start=True)
             turn(j, roads[3], 1)
@@ -266,22 +268,28 @@ def tile_list_courier_eta_banks_kernel(
                 banks[j][:].rearrange("t (s e p) -> t s p e", s=2, e=2),
             )
             turned.append(strip)
-        for c in range(CHUNKS):
-            for s in range(PACK):
-                words = turned[2 * c + s // 2][:].bitcast(F32)
-                nc.tensor.transpose(
-                    banks[c][:, s * P : (s + 1) * P], words[:, (s % 2) * P : (s % 2 + 1) * P], ident[:]
-                )
-            nc.scalar.copy(pairs[0][:].bitcast(F32)[:, T2 + c * BANK : T2 + (c + 1) * BANK], banks[c][:])
+
+        def turn_back():
+            for c in range(CHUNKS):
+                for s in range(PACK):
+                    words = turned[2 * c + s // 2][:].bitcast(F32)
+                    nc.tensor.transpose(
+                        banks[c][:, s * P : (s + 1) * P], words[:, (s % 2) * P : (s % 2 + 1) * P], ident[:]
+                    )
+                nc.scalar.copy(pairs[0][:].bitcast(F32)[:, T2 + c * BANK : T2 + (c + 1) * BANK], banks[c][:])
+
+        turn_back()
         z0 = [weave(0, c) for c in range(CHUNKS)]
         put(5)
         put(6)
-        add_road(nc.gpsimd, ORDER[4], whole)
+        add_road(nc.gpsimd, 4, whole)
         put(7)
-        add_road(nc.gpsimd, ORDER[5], whole)
-        add_road(nc.gpsimd, ORDER[6], whole)
+        add_road(nc.gpsimd, 5, whole)
+        add_road(nc.gpsimd, 6, whole)
 
-        late_plane = keep.tile([P, T2], U8, name="late_plane", tag="slot7", align_bytes=64)
+        late_plane = keep.tile([P, T2 + PASSES * N], U8, name="late_plane", tag="slot7", align_bytes=64)
+        w2_plane = late_plane[:, T2:]
+        w2_codes = keep.tile([P, PASSES * N], U32, name="w2_codes", align_bytes=64)
         z_codes = {}
         z_plane = {}
         z1_plane = keep.tile([P, T2], U8, name="z1_plane", align_bytes=64)
@@ -298,7 +306,6 @@ def tile_list_courier_eta_banks_kernel(
 
         def last_sum(c):
             add_road(nc.vector, ORDER[-1], slice(c * BANK, (c + 1) * BANK))
-            return weave(1, c)
 
         def bank_of(c, nt):
             return banks[(4 * c + nt) % 8]
@@ -322,35 +329,27 @@ def tile_list_courier_eta_banks_kernel(
             nc.vector.tensor_tensor(delay[:, nt % 2, :], delay[:, nt % 2, :], bank_of(c, nt)[:], ADD)
             nc.sync.dma_start(out[nt * P : (nt + 1) * P, c * BANK : (c + 1) * BANK], delay[:, nt % 2, :])
 
-        held = []
-
         def finish(c):
             cols = slice(c * BANK, (c + 1) * BANK)
-            low = results.tile([P, 2, BANK], F32, name="curve_low")
-            high = results.tile([P, 2, BANK], F32, name="curve_high", bufs=2)
-            delay = results.tile([P, 2, BANK], F32, name="delay_low")
+            curves = [results.tile([P, 2, BANK], F32, name="curve") for u in range(2)]
             for nt in range(4):
-                multiply(c, nt, low if nt < 2 else high)
-            nc.vector.tensor_tensor(delay[:], low[:], jams[0][:, :, cols], MULT)
-            shared = 1 if c == 0 else 2
-            nc.gpsimd.tensor_tensor(low[:, :shared, :], high[:, :shared, :], jams[1][:, :shared, cols], MULT)
-            for args in held:
-                add_and_store(*args)
-            held.clear()
-            add_and_store(c, 0, delay)
-            add_and_store(c, 1, delay)
-            if shared < 2:
-                nc.vector.tensor_tensor(low[:, 1, :], high[:, 1, :], jams[1][:, 1, cols], MULT)
-            held.extend([(c, 2, low), (c, 3, low)])
+                multiply(c, nt, curves[nt // 2])
+            for u in range(2):
+                nc.vector.tensor_tensor(curves[u][:], curves[u][:], jams[u][:, :, cols], MULT)
+            for nt in range(4):
+                add_and_store(c, nt, curves[nt // 2])
 
-        z1 = [last_sum(0), last_sum(1)]
-        for c in range(CHUNKS):
+        last_sum(0)
+        last_sum(1)
+        z1 = [weave(1, 0), weave(1, 1)]
+        nc.vector.quantize_mx(out=w2_codes[:].bitcast(E4M3), scales=w2_plane, in_=w2_grouped[:])
+        for c in range(2):
             quantise(0, c, z0[c])
             quantise(1, c, z1[c])
+        last_sum(2)
+        last_sum(3)
+        for c in range(CHUNKS):
+            finish(c)
             if c + 2 < CHUNKS:
-                z1.append(last_sum(c + 2))
-            if c > 0:
-                finish(c - 1)
-        finish(CHUNKS - 1)
-        for args in held:
-            add_and_store(*args)
+                quantise(0, c + 2, z0[c + 2])
+                quantise(1, c + 2, weave(1, c + 2))

@@ -256,7 +256,11 @@ def tile_list_courier_eta_banks_kernel(
             turn(j, roads[2], 0, start=True)
             turn(j, roads[3], 1)
         load_road(6)
-        load_road(7)
+        last_road = []
+        for u in range(2):
+            rows = keep.tile([P, T2 // 2], F32, name=f"road7_{u}", tag=("w1", "road3")[u], align_bytes=64)
+            nc.sync.dma_start(rows[:], road_rows[1, PACK - 1][:, u * T2 // 2 : (u + 1) * T2 // 2])
+            last_road.append(rows)
         for j in range(STRIPS):
             turn(j, page_of[2], 0)
         turned = []
@@ -287,8 +291,6 @@ def tile_list_courier_eta_banks_kernel(
         add_road(nc.gpsimd, 5, whole)
         add_road(nc.gpsimd, 6, whole)
 
-        late_plane = keep.tile([P, T2 + PASSES * N], U8, name="late_plane", tag="slot7", align_bytes=64)
-        w2_plane = late_plane[:, T2:]
         w2_codes = keep.tile([P, PASSES * N], U32, name="w2_codes", align_bytes=64)
         z_codes = {}
         z_plane = {}
@@ -305,7 +307,10 @@ def tile_list_courier_eta_banks_kernel(
             z_plane[b, c] = plane
 
         def last_sum(c):
-            add_road(nc.vector, ORDER[-1], slice(c * BANK, (c + 1) * BANK))
+            cols = slice(c * BANK, (c + 1) * BANK)
+            plane = pairs[1][:].rearrange("p (i t) -> p i t", i=PACK)[:, PACK - 1, cols]
+            rows = last_road[c // 2][:, c % 2 * BANK : (c % 2 + 1) * BANK]
+            nc.vector.tensor_tensor(plane, page_of[SLICES - 1][:, cols], rows, ADD)
 
         def bank_of(c, nt):
             return banks[(4 * c + nt) % 8]
@@ -329,19 +334,32 @@ def tile_list_courier_eta_banks_kernel(
             nc.vector.tensor_tensor(delay[:, nt % 2, :], delay[:, nt % 2, :], bank_of(c, nt)[:], ADD)
             nc.sync.dma_start(out[nt * P : (nt + 1) * P, c * BANK : (c + 1) * BANK], delay[:, nt % 2, :])
 
+        held = []
+
         def finish(c):
             cols = slice(c * BANK, (c + 1) * BANK)
-            curves = [results.tile([P, 2, BANK], F32, name="curve") for u in range(2)]
+            low = results.tile([P, 2, BANK], F32, name="curve_low", bufs=3)
+            high = results.tile([P, 2, BANK], F32, name="curve_high", bufs=2)
+            delay = results.tile([P, 2, BANK], F32, name="delay_low", bufs=2)
             for nt in range(4):
-                multiply(c, nt, curves[nt // 2])
-            for u in range(2):
-                nc.vector.tensor_tensor(curves[u][:], curves[u][:], jams[u][:, :, cols], MULT)
-            for nt in range(4):
-                add_and_store(c, nt, curves[nt // 2])
+                multiply(c, nt, low if nt < 2 else high)
+            nc.vector.tensor_tensor(delay[:], low[:], jams[0][:, :, cols], MULT)
+            shared = 1 if c == 0 else 2
+            nc.gpsimd.tensor_tensor(low[:, :shared, :], high[:, :shared, :], jams[1][:, :shared, cols], MULT)
+            for args in held:
+                add_and_store(*args)
+            held.clear()
+            add_and_store(c, 0, delay)
+            add_and_store(c, 1, delay)
+            if shared < 2:
+                nc.vector.tensor_tensor(low[:, 1, :], high[:, 1, :], jams[1][:, 1, cols], MULT)
+            held.extend([(c, 2, low), (c, 3, low)])
 
         last_sum(0)
         last_sum(1)
         z1 = [weave(1, 0), weave(1, 1)]
+        late_plane = keep.tile([P, T2 + PASSES * N], U8, name="late_plane", tag="w1", align_bytes=64)
+        w2_plane = late_plane[:, T2:]
         nc.vector.quantize_mx(out=w2_codes[:].bitcast(E4M3), scales=w2_plane, in_=w2_grouped[:])
         for c in range(2):
             quantise(0, c, z0[c])
@@ -353,3 +371,5 @@ def tile_list_courier_eta_banks_kernel(
             if c + 2 < CHUNKS:
                 quantise(0, c + 2, z0[c + 2])
                 quantise(1, c + 2, weave(1, c + 2))
+        for args in held:
+            add_and_store(*args)

@@ -44,16 +44,15 @@ def tile_list_courier_eta_banks_kernel(
         psum = ctx.enter_context(tc.psum_pool(name="psum", bufs=1))
         banks = [psum.tile([P, BANK], F32, name=f"bank{j}") for j in range(8)]
 
-        w1_plane = keep.tile([P, PASSES * H], U8, name="w1_plane", tag="page2", align_bytes=64)
+        w1_plane = keep.tile([P, PASSES * H], U8, name="w1_plane", tag="page1", align_bytes=64)
         nc.gpsimd.memset(w1_plane[:].bitcast(I32), 0)
         tab_plane = keep.tile([P, T + 4], U8, name="tab_plane", tag="road0", align_bytes=64)
         for q in range(4):
             nc.vector.memset(tab_plane[32 * q : 32 * q + 24, :].bitcast(I32), 0)
         v_plane = keep.tile([P, PASSES * S], U8, name="v_plane", align_bytes=64)
         nc.gpsimd.memset(v_plane[96:128, :].bitcast(I32), 0)
-        pages = [keep.tile([P, T2], F32, name=f"page{j}") for j in range(2)]
-        for page in pages:
-            nc.gpsimd.memset(page[:], 0.0)
+        pages = [keep.tile([P, T2], F32, name="page0")]
+        nc.gpsimd.memset(pages[0][:], 0.0)
 
         picks = lists.tile([P, S // 16], U16, name="picks")
         nc.sync.dma_start(picks[:], offs)
@@ -121,13 +120,16 @@ def tile_list_courier_eta_banks_kernel(
             w1_codes[:].bitcast(U16).rearrange("p (g i m) -> p g i m", i=PACK, m=P),
             w1_raw[:].bitcast(U16).rearrange("p (g m i) -> p g i m", i=PACK, m=P),
         )
-        w1_scale = keep.tile([P, PASSES * H], U8, name="w1_scale", tag="w1", align_bytes=64)
-        nc.vector.tensor_copy(
-            w1_scale[:].rearrange("p (g i m) -> p g i m", i=PACK, m=P),
-            w1_plane[:].rearrange("p (g m i) -> p g i m", i=PACK, m=P),
-        )
-        pages.append(keep.tile([P, T2], F32, name="page2", tag="page2", align_bytes=64))
-        nc.gpsimd.memset(pages[2][:], 0.0)
+        w1_scale = []
+        for b in range(PASSES):
+            ordered = keep.tile([P, H], U8, name=f"w1_scale{b}", tag=("page2", "w1")[b], align_bytes=64)
+            nc.vector.tensor_copy(
+                ordered[:].rearrange("p (a i m) -> p a i m", i=PACK, m=P),
+                w1_plane[:].rearrange("p (a b m i) -> p b a i m", a=PASSES, i=PACK, m=P)[:, b],
+            )
+            w1_scale.append(ordered)
+        pages.append(keep.tile([P, T2], F32, name="page1", tag="page1", align_bytes=64))
+        nc.gpsimd.memset(pages[1][:], 0.0)
         v_codes = {}
         for half in range(2):
             for a in range(PASSES):
@@ -152,7 +154,7 @@ def tile_list_courier_eta_banks_kernel(
                     nc.tensor.matmul_mx(
                         out=bank[:],
                         lhsT=w1_codes[:, 2 * P * g : 2 * P * (g + 1)].bitcast(E2M1),
-                        lhsT_scale=w1_scale[:, P * g : P * (g + 1)],
+                        lhsT_scale=w1_scale[k // PACK][:, P * (a * PACK + k % PACK) : P * (a * PACK + k % PACK + 1)],
                         rhs=v_codes[a, half][:].bitcast(E4M3),
                         rhs_scale=v_plane[:, a * S + half * BANK : a * S + (half + 1) * BANK],
                         start=(a == 0),
@@ -206,9 +208,14 @@ def tile_list_courier_eta_banks_kernel(
             b, i = divmod(k, PACK)
             if b == 0:
                 plane = pairs[b][:].rearrange("p (u t e) -> p u t e", u=2, e=2)[:, i // 2, cols, i % 2]
+                engine.tensor_tensor(plane, page_of[k][:, cols], roads[k][:, cols], ADD)
             else:
-                plane = pairs[b][:].rearrange("p (i t) -> p i t", i=PACK)[:, i, cols]
-            engine.tensor_tensor(plane, page_of[k][:, cols], roads[k][:, cols], ADD)
+                engine.tensor_tensor(
+                    pairs[b][:].rearrange("p (c i t) -> p c i t", i=PACK, t=BANK)[:, :, i, :],
+                    page_of[k][:].rearrange("p (c t) -> p c t", t=BANK),
+                    roads[k][:].rearrange("p (c t) -> p c t", t=BANK),
+                    ADD,
+                )
 
         def turn(j, source, e, start=False, stop=False):
             for s in range(2):
@@ -231,16 +238,20 @@ def tile_list_courier_eta_banks_kernel(
                 words = pairs[b][:].bitcast(F32).rearrange("p (u t) -> p t u", u=2)
                 nc.scalar.copy(z[:].bitcast(F32).rearrange("p (t u) -> p t u", u=2), words[:, cols, :])
             else:
-                planes = pairs[b][:].rearrange("p (i t) -> p i t", i=PACK)[:, :, cols]
+                planes = pairs[b][:, c * PACK * BANK : (c + 1) * PACK * BANK]
                 nc.scalar.copy(
                     z[:].rearrange("p (g t i) -> p g i t", t=PACK, i=PACK),
-                    planes.rearrange("p i (g t) -> p g i t", t=PACK),
+                    planes.rearrange("p (i g t) -> p g i t", i=PACK, t=PACK),
                 )
             return z
 
         whole = slice(0, T2)
-        for step in range(PACK):
-            weigh(step)
+        weigh(0)
+        weigh(1)
+        pages.append(keep.tile([P, T2], F32, name="page2", tag="page2", align_bytes=64))
+        nc.gpsimd.memset(pages[2][:], 0.0)
+        weigh(2)
+        weigh(3)
         for step in range(PAGES):
             put(step)
         ident = keep.tile([P, P], F32, name="ident", tag="codes1", align_bytes=64)
@@ -257,9 +268,11 @@ def tile_list_courier_eta_banks_kernel(
             turn(j, roads[3], 1)
         load_road(6)
         last_road = []
-        for u in range(2):
-            rows = keep.tile([P, T2 // 2], F32, name=f"road7_{u}", tag=("w1", "road3")[u], align_bytes=64)
-            nc.sync.dma_start(rows[:], road_rows[1, PACK - 1][:, u * T2 // 2 : (u + 1) * T2 // 2])
+        for u, cols in enumerate((slice(0, BANK), slice(BANK, T2))):
+            rows = keep.tile(
+                [P, cols.stop - cols.start], F32, name=f"road7_{u}", tag=("w1", "road3")[u], align_bytes=64
+            )
+            nc.sync.dma_start(rows[:], road_rows[1, PACK - 1][:, cols])
             last_road.append(rows)
         for j in range(STRIPS):
             turn(j, page_of[2], 0)
@@ -297,7 +310,8 @@ def tile_list_courier_eta_banks_kernel(
         z1_plane = keep.tile([P, T2], U8, name="z1_plane", align_bytes=64)
 
         def quantise(b, c, z):
-            codes = keep.tile([P, BANK], U32, name=f"z_codes{b}_{c}", tag=f"codes{4 * b + c}", align_bytes=64)
+            tag = ("codes0", "slot4", "slot1", "slot2")[c] if b == 0 else f"codes{PACK + c}"
+            codes = keep.tile([P, BANK], U32, name=f"z_codes{b}_{c}", tag=tag, align_bytes=64)
             if b == 0:
                 plane = late_plane[:, c * BANK : (c + 1) * BANK]
             else:
@@ -308,8 +322,8 @@ def tile_list_courier_eta_banks_kernel(
 
         def last_sum(c):
             cols = slice(c * BANK, (c + 1) * BANK)
-            plane = pairs[1][:].rearrange("p (i t) -> p i t", i=PACK)[:, PACK - 1, cols]
-            rows = last_road[c // 2][:, c % 2 * BANK : (c % 2 + 1) * BANK]
+            plane = pairs[1][:, ((c + 1) * PACK - 1) * BANK : (c + 1) * PACK * BANK]
+            rows = last_road[0][:] if c == 0 else last_road[1][:, cols.start - BANK : cols.stop - BANK]
             nc.vector.tensor_tensor(plane, page_of[SLICES - 1][:, cols], rows, ADD)
 
         def bank_of(c, nt):
@@ -334,42 +348,46 @@ def tile_list_courier_eta_banks_kernel(
             nc.vector.tensor_tensor(delay[:, nt % 2, :], delay[:, nt % 2, :], bank_of(c, nt)[:], ADD)
             nc.sync.dma_start(out[nt * P : (nt + 1) * P, c * BANK : (c + 1) * BANK], delay[:, nt % 2, :])
 
-        held = []
+        def curves(c, u):
+            curve = results.tile([P, 2, BANK], F32, name=("curve_low", "curve_high")[u], bufs=2 + u)
+            for nt in (2 * u, 2 * u + 1):
+                multiply(c, nt, curve)
+            return curve
 
-        def finish(c):
-            cols = slice(c * BANK, (c + 1) * BANK)
-            low = results.tile([P, 2, BANK], F32, name="curve_low", bufs=3)
-            high = results.tile([P, 2, BANK], F32, name="curve_high", bufs=2)
-            delay = results.tile([P, 2, BANK], F32, name="delay_low", bufs=2)
-            for nt in range(4):
-                multiply(c, nt, low if nt < 2 else high)
-            nc.vector.tensor_tensor(delay[:], low[:], jams[0][:, :, cols], MULT)
-            shared = 1 if c == 0 else 2
-            nc.gpsimd.tensor_tensor(low[:, :shared, :], high[:, :shared, :], jams[1][:, :shared, cols], MULT)
-            for args in held:
-                add_and_store(*args)
-            held.clear()
-            add_and_store(c, 0, delay)
-            add_and_store(c, 1, delay)
-            if shared < 2:
-                nc.vector.tensor_tensor(low[:, 1, :], high[:, 1, :], jams[1][:, 1, cols], MULT)
-            held.extend([(c, 2, low), (c, 3, low)])
+        def jam_of(c, u):
+            return jams[u][:, :, c * BANK : (c + 1) * BANK]
 
         last_sum(0)
-        last_sum(1)
-        z1 = [weave(1, 0), weave(1, 1)]
+        z1 = [weave(1, 0)]
         late_plane = keep.tile([P, T2 + PASSES * N], U8, name="late_plane", tag="w1", align_bytes=64)
         w2_plane = late_plane[:, T2:]
         nc.vector.quantize_mx(out=w2_codes[:].bitcast(E4M3), scales=w2_plane, in_=w2_grouped[:])
-        for c in range(2):
-            quantise(0, c, z0[c])
-            quantise(1, c, z1[c])
+        quantise(0, 0, z0[0])
+        last_sum(1)
+        z1.append(weave(1, 1))
+        quantise(1, 0, z1[0])
+        quantise(0, 1, z0[1])
         last_sum(2)
         last_sum(3)
+        quantise(1, 1, z1[1])
+        low = curves(0, 0)
+        high = curves(0, 1)
+        nc.vector.tensor_tensor(low[:], low[:], jam_of(0, 0), MULT)
+        delay_low = low
         for c in range(CHUNKS):
-            finish(c)
+            if c + 1 < CHUNKS:
+                low = curves(c + 1, 0)
+            if c + 2 < CHUNKS:
+                z1.append(weave(1, c + 2))
+            delay_high = results.tile([P, 2, BANK], F32, name="delay_high", bufs=2)
+            nc.vector.tensor_tensor(delay_high[:], high[:], jam_of(c, 1), MULT)
+            if c + 1 < CHUNKS:
+                nc.gpsimd.tensor_tensor(high[:], low[:], jam_of(c + 1, 0), MULT)
+            for nt in range(4):
+                add_and_store(c, nt, delay_low if nt < 2 else delay_high)
+            delay_low = high
             if c + 2 < CHUNKS:
                 quantise(0, c + 2, z0[c + 2])
-                quantise(1, c + 2, weave(1, c + 2))
-        for args in held:
-            add_and_store(*args)
+                quantise(1, c + 2, z1[c + 2])
+            if c + 1 < CHUNKS:
+                high = curves(c + 1, 1)

@@ -29,7 +29,7 @@ PAGES = 3
 STRIP = 256
 STRIPS = T2 // STRIP
 FIRST_BANKS = 3
-ORDER = (0, 1, 2, 3, 4, 5, 6, 7)
+ORDER = (0, 1, 2, 3, 6, 4, 5, 7)
 FIRST_PIECES = (256, 256, 512)
 
 
@@ -211,7 +211,7 @@ def tile_list_courier_eta_banks_kernel(
                 engine.tensor_tensor(plane, page_of[k][:, cols], roads[k][:, cols], ADD)
             else:
                 engine.tensor_tensor(
-                    pairs[b][:].rearrange("p (c i t) -> p c i t", i=PACK, t=BANK)[:, :, i, :],
+                    pairs[b][:].rearrange("p (c u t e) -> p c u t e", u=2, t=BANK, e=2)[:, :, i // 2, :, i % 2],
                     page_of[k][:].rearrange("p (c t) -> p c t", t=BANK),
                     roads[k][:].rearrange("p (c t) -> p c t", t=BANK),
                     ADD,
@@ -231,7 +231,7 @@ def tile_list_courier_eta_banks_kernel(
                 )
 
         def weave(b, c):
-            tag = f"slot{PACK * b + c}" if b == 0 or c < 2 else f"codes{PACK + c - 2}"
+            tag = f"slot{PACK * b + c}"
             z = keep.tile([P, PACK * BANK], BF16, name=f"z{b}_{c}", tag=tag, align_bytes=64)
             cols = slice(c * BANK, (c + 1) * BANK)
             if b == 0:
@@ -240,8 +240,8 @@ def tile_list_courier_eta_banks_kernel(
             else:
                 planes = pairs[b][:, c * PACK * BANK : (c + 1) * PACK * BANK]
                 nc.scalar.copy(
-                    z[:].rearrange("p (g t i) -> p g i t", t=PACK, i=PACK),
-                    planes.rearrange("p (i g t) -> p g i t", i=PACK, t=PACK),
+                    z[:].bitcast(F32).rearrange("p (t u) -> p t u", u=2),
+                    planes.bitcast(F32).rearrange("p (u t) -> p t u", u=2),
                 )
             return z
 
@@ -257,7 +257,7 @@ def tile_list_courier_eta_banks_kernel(
         ident = keep.tile([P, P], F32, name="ident", tag="codes1", align_bytes=64)
         make_identity(nc, ident[:])
         for step in range(2):
-            add_road(nc.gpsimd, step, whole)
+            add_road(nc.gpsimd, ORDER[step], whole)
             load_road(step + PACK)
             weigh(step + PACK)
             put(step + PAGES)
@@ -299,10 +299,10 @@ def tile_list_courier_eta_banks_kernel(
         z0 = [weave(0, c) for c in range(CHUNKS)]
         put(5)
         put(6)
-        add_road(nc.gpsimd, 4, whole)
+        add_road(nc.gpsimd, ORDER[4], whole)
         put(7)
-        add_road(nc.gpsimd, 5, whole)
-        add_road(nc.gpsimd, 6, whole)
+        add_road(nc.gpsimd, ORDER[5], whole)
+        add_road(nc.gpsimd, ORDER[6], whole)
 
         w2_codes = keep.tile([P, PASSES * N], U32, name="w2_codes", align_bytes=64)
         z_codes = {}
@@ -322,7 +322,7 @@ def tile_list_courier_eta_banks_kernel(
 
         def last_sum(c):
             cols = slice(c * BANK, (c + 1) * BANK)
-            plane = pairs[1][:, ((c + 1) * PACK - 1) * BANK : (c + 1) * PACK * BANK]
+            plane = pairs[1][:, ((c + 1) * PACK - 2) * BANK + 1 : (c + 1) * PACK * BANK : 2]
             rows = last_road[0][:] if c == 0 else last_road[1][:, cols.start - BANK : cols.stop - BANK]
             nc.vector.tensor_tensor(plane, page_of[SLICES - 1][:, cols], rows, ADD)
 
@@ -349,7 +349,7 @@ def tile_list_courier_eta_banks_kernel(
             nc.sync.dma_start(out[nt * P : (nt + 1) * P, c * BANK : (c + 1) * BANK], delay[:, nt % 2, :])
 
         def curves(c, u):
-            curve = results.tile([P, 2, BANK], F32, name=("curve_low", "curve_high")[u], bufs=2 + u)
+            curve = results.tile([P, 2, BANK], F32, name=("curve_low", "curve_high")[u], bufs=2 + 2 * u)
             for nt in (2 * u, 2 * u + 1):
                 multiply(c, nt, curve)
             return curve
@@ -370,24 +370,22 @@ def tile_list_courier_eta_banks_kernel(
         last_sum(2)
         last_sum(3)
         quantise(1, 1, z1[1])
+        for c in range(2, CHUNKS):
+            quantise(0, c, z0[c])
+            quantise(1, c, weave(1, c))
         low = curves(0, 0)
         high = curves(0, 1)
-        nc.vector.tensor_tensor(low[:], low[:], jam_of(0, 0), MULT)
-        delay_low = low
+        delay_low = results.tile([P, 2, BANK], F32, name="delay", bufs=3)
+        nc.vector.tensor_tensor(delay_low[:], low[:], jam_of(0, 0), MULT)
         for c in range(CHUNKS):
             if c + 1 < CHUNKS:
                 low = curves(c + 1, 0)
-            if c + 2 < CHUNKS:
-                z1.append(weave(1, c + 2))
-            delay_high = results.tile([P, 2, BANK], F32, name="delay_high", bufs=2)
+            delay_high = results.tile([P, 2, BANK], F32, name="delay", bufs=3)
             nc.vector.tensor_tensor(delay_high[:], high[:], jam_of(c, 1), MULT)
             if c + 1 < CHUNKS:
                 nc.gpsimd.tensor_tensor(high[:], low[:], jam_of(c + 1, 0), MULT)
             for nt in range(4):
                 add_and_store(c, nt, delay_low if nt < 2 else delay_high)
             delay_low = high
-            if c + 2 < CHUNKS:
-                quantise(0, c + 2, z0[c + 2])
-                quantise(1, c + 2, z1[c + 2])
             if c + 1 < CHUNKS:
                 high = curves(c + 1, 1)

@@ -22,15 +22,19 @@ TANH = mybir.ActivationFunctionType.Tanh
 P = 128
 PACK = 4
 BANK = 512
+BANKS = 8
 PASSES = 2
 SLICES = PASSES * PACK
 CHUNKS = T2 // BANK
+LIST_ROWS = 16
 PAGES = 3
 STRIP = 256
 STRIPS = T2 // STRIP
 FIRST_BANKS = 3
 ORDER = (0, 1, 2, 3, 6, 4, 5, 7)
-FIRST_PIECES = (256, 256, 512)
+LAST = ORDER[-1]
+FIRST_PIECES = (128, 128, 256, 512)
+FIRST_WEIGHTS = 256
 
 
 def tile_list_courier_eta_banks_kernel(
@@ -40,62 +44,64 @@ def tile_list_courier_eta_banks_kernel(
     with ExitStack() as ctx:
         lists = ctx.enter_context(tc.tile_pool(name="lists", bufs=1))
         keep = ctx.enter_context(tc.tile_pool(name="keep", bufs=1))
-        results = ctx.enter_context(tc.tile_pool(name="results", bufs=6))
+        results = ctx.enter_context(tc.tile_pool(name="results", bufs=3))
         psum = ctx.enter_context(tc.psum_pool(name="psum", bufs=1))
-        banks = [psum.tile([P, BANK], F32, name=f"bank{j}") for j in range(8)]
+        banks = [psum.tile([P, BANK], F32, name=f"bank{j}") for j in range(BANKS)]
 
-        w1_plane = keep.tile([P, PASSES * H], U8, name="w1_plane", tag="page1", align_bytes=64)
+        w1_plane = keep.tile([P, PASSES * H], U8, name="w1_plane", tag="codes1", align_bytes=64)
         nc.gpsimd.memset(w1_plane[:].bitcast(I32), 0)
         tab_plane = keep.tile([P, T + 4], U8, name="tab_plane", tag="road0", align_bytes=64)
         for q in range(4):
             nc.vector.memset(tab_plane[32 * q : 32 * q + 24, :].bitcast(I32), 0)
         v_plane = keep.tile([P, PASSES * S], U8, name="v_plane", align_bytes=64)
         nc.gpsimd.memset(v_plane[96:128, :].bitcast(I32), 0)
-        pages = [keep.tile([P, T2], F32, name="page0")]
-        nc.gpsimd.memset(pages[0][:], 0.0)
+        pages = [keep.tile([P, T2], F32, name=f"page{j}") for j in range(2)]
+        for page in pages:
+            nc.gpsimd.memset(page[:], 0.0)
 
-        picks = lists.tile([P, S // 16], U16, name="picks")
+        picks = lists.tile([P, S // LIST_ROWS], U16, name="picks")
         nc.sync.dma_start(picks[:], offs)
         for q in range(4):
             nc.sync.dma_start(
                 tab_plane[32 * q + 24 : 32 * q + 32, :T].bitcast(I32),
                 tab_scales[:, 4 * q : 4 * q + 4, :].bitcast(I32),
             )
-        w1_raw = keep.tile([P, PASSES * 2 * H], U8, name="w1_raw", tag="w1", align_bytes=64)
+        bias = keep.tile([P, SLICES], F32, name="bias")
+        nc.sync.dma_start(
+            bias[:].rearrange("p (b i) -> p b i", i=PACK), b1.rearrange("(b p i) -> p b i", b=PASSES, i=PACK)
+        )
+        tab = keep.tile([P, PASSES * T], I32, name="tab", tag="wide0", align_bytes=64)
+
+        def load_table(a):
+            nc.sync.dma_start(
+                tab[:, a * T : (a + 1) * T], tab_words[a].rearrange("p t i -> p (t i)").bitcast(I32)
+            )
+
+        load_table(0)
+        w1_raw = keep.tile([P, PASSES * 2 * H], U8, name="w1_raw", tag="page2", align_bytes=64)
         nc.sync.dma_start(
             w1_raw[:].bitcast(I32).rearrange("p (a c) -> p a c", a=PASSES),
             w1_words.bitcast(I32).rearrange("a p c -> p a c"),
         )
-        tab = keep.tile([P, PASSES * T], I32, name="tab", tag="wide0", align_bytes=64)
-
-        def load_table(cols):
-            nc.sync.dma_start(
-                tab[:].rearrange("p (a t) -> p a t", a=PASSES)[:, :, cols],
-                tab_words.rearrange("a p t i -> p a (t i)").bitcast(I32)[:, :, cols],
-            )
-
-        load_table(slice(0, T // 2))
         for q in range(4):
             nc.sync.dma_start(
                 w1_plane[32 * q : 32 * q + 4, :].bitcast(I32).rearrange("r (a c) -> r a c", a=PASSES),
                 w1_scales[:, 4 * q : 4 * q + 4, :].bitcast(I32).rearrange("a r c -> r a c"),
             )
-        load_table(slice(T // 2, T))
-        picked = keep.tile([P, S], U8, name="picked", align_bytes=64)
+        load_table(1)
+
+        picked = keep.tile([P, S], U8, name="picked", tag="late", align_bytes=64)
         nc.vector.tensor_copy(picked[:], tab_plane[:, :T].indirect(picks[:]))
         for a in range(PASSES):
             first = 24 + 4 * a
             (nc.scalar, nc.sync)[a].dma_start(
                 v_plane[0:100, a * S : (a + 1) * S].bitcast(I32), picked[first : first + 100, :].bitcast(I32)
             )
-        bias = keep.tile([P, SLICES], F32, name="bias")
-        nc.sync.dma_start(
-            bias[:].rearrange("p (b i) -> p b i", i=PACK), b1.rearrange("(b p i) -> p b i", b=PASSES, i=PACK)
-        )
-        places = lists.tile([P, S // 16], U16, name="places")
+        places = lists.tile([P, S // LIST_ROWS], U16, name="places")
         nc.sync.dma_start(places[:], offs2)
         weights = keep.tile([P, S], F32, name="weights")
-        nc.sync.dma_start(weights[:], wgs)
+        for cols in (slice(0, FIRST_WEIGHTS), slice(FIRST_WEIGHTS, S)):
+            nc.sync.dma_start(weights[:, cols], wgs[:, cols])
 
         road_rows = road.rearrange("(b p i) t -> b i p t", b=PASSES, i=PACK)
         roads = {}
@@ -122,21 +128,20 @@ def tile_list_courier_eta_banks_kernel(
         )
         w1_scale = []
         for b in range(PASSES):
-            ordered = keep.tile([P, H], U8, name=f"w1_scale{b}", tag=("page2", "w1")[b], align_bytes=64)
-            nc.vector.tensor_copy(
+            ordered = keep.tile([P, H], U8, name=f"w1_scale{b}", tag=("page2", "late")[b], align_bytes=64)
+            nc.gpsimd.tensor_copy(
                 ordered[:].rearrange("p (a i m) -> p a i m", i=PACK, m=P),
                 w1_plane[:].rearrange("p (a b m i) -> p b a i m", a=PASSES, i=PACK, m=P)[:, b],
             )
             w1_scale.append(ordered)
-        pages.append(keep.tile([P, T2], F32, name="page1", tag="page1", align_bytes=64))
-        nc.gpsimd.memset(pages[1][:], 0.0)
+
         v_codes = {}
         for half in range(2):
             for a in range(PASSES):
                 words = keep.tile(
                     [P, BANK], U32, name=f"v_codes{a}{half}", tag=f"codes{2 * a + half}", align_bytes=64
                 )
-                entries = picks[:, half * BANK // 16 : (half + 1) * BANK // 16]
+                entries = picks[:, half * BANK // LIST_ROWS : (half + 1) * BANK // LIST_ROWS]
                 nc.vector.tensor_copy(words[:], tab[:, a * T : (a + 1) * T].bitcast(U32).indirect(entries))
                 v_codes[a, half] = words
 
@@ -146,15 +151,17 @@ def tile_list_courier_eta_banks_kernel(
 
         h = {}
         for step, k in enumerate(ORDER):
+            b, i = divmod(k, PACK)
             h[k] = keep.tile([P, S], F32, name=f"h{k}", tag=f"slot{step}", align_bytes=64)
             for half in range(2):
                 bank = banks[(2 * step + half) % FIRST_BANKS]
                 for a in range(PASSES):
-                    g = a * SLICES + k
+                    code0 = 2 * P * (a * SLICES + k)
+                    scale0 = P * (a * PACK + i)
                     nc.tensor.matmul_mx(
                         out=bank[:],
-                        lhsT=w1_codes[:, 2 * P * g : 2 * P * (g + 1)].bitcast(E2M1),
-                        lhsT_scale=w1_scale[k // PACK][:, P * (a * PACK + k % PACK) : P * (a * PACK + k % PACK + 1)],
+                        lhsT=w1_codes[:, code0 : code0 + 2 * P].bitcast(E2M1),
+                        lhsT_scale=w1_scale[b][:, scale0 : scale0 + P],
                         rhs=v_codes[a, half][:].bitcast(E4M3),
                         rhs_scale=v_plane[:, a * S + half * BANK : a * S + (half + 1) * BANK],
                         start=(a == 0),
@@ -197,20 +204,21 @@ def tile_list_courier_eta_banks_kernel(
             k = ORDER[step]
             page_of[k] = pages[step % PAGES]
             for cols in pieces_of(k):
-                entries = places[:, cols.start // 16 : cols.stop // 16]
+                entries = places[:, cols.start // LIST_ROWS : cols.stop // LIST_ROWS]
                 nc.vector.tensor_copy(page_of[k][:].indirect(entries), h[k][:, cols])
 
         pairs = [
-            keep.tile([P, 2 * T2 * 2], BF16, name=f"pairs{b}", tag=f"pairs{b}", align_bytes=64) for b in range(PASSES)
+            keep.tile([P, PACK * T2], BF16, name=f"pairs{b}", tag=f"pairs{b}", align_bytes=64) for b in range(PASSES)
         ]
 
-        def add_road(engine, k, cols):
+        def add_road(step):
+            k = ORDER[step]
             b, i = divmod(k, PACK)
             if b == 0:
-                plane = pairs[b][:].rearrange("p (u t e) -> p u t e", u=2, e=2)[:, i // 2, cols, i % 2]
-                engine.tensor_tensor(plane, page_of[k][:, cols], roads[k][:, cols], ADD)
+                halves = pairs[b][:].rearrange("p (u t e) -> p u t e", u=2, e=2)[:, i // 2, :, i % 2]
+                nc.gpsimd.tensor_tensor(halves, page_of[k][:], roads[k][:], ADD)
             else:
-                engine.tensor_tensor(
+                nc.gpsimd.tensor_tensor(
                     pairs[b][:].rearrange("p (c u t e) -> p c u t e", u=2, t=BANK, e=2)[:, :, i // 2, :, i % 2],
                     page_of[k][:].rearrange("p (c t) -> p c t", t=BANK),
                     roads[k][:].rearrange("p (c t) -> p c t", t=BANK),
@@ -231,21 +239,15 @@ def tile_list_courier_eta_banks_kernel(
                 )
 
         def weave(b, c):
-            tag = f"slot{PACK * b + c}"
-            z = keep.tile([P, PACK * BANK], BF16, name=f"z{b}_{c}", tag=tag, align_bytes=64)
-            cols = slice(c * BANK, (c + 1) * BANK)
+            z = keep.tile([P, PACK * BANK], BF16, name=f"z{b}_{c}", tag=f"slot{PACK * b + c}", align_bytes=64)
             if b == 0:
-                words = pairs[b][:].bitcast(F32).rearrange("p (u t) -> p t u", u=2)
-                nc.scalar.copy(z[:].bitcast(F32).rearrange("p (t u) -> p t u", u=2), words[:, cols, :])
+                words = pairs[b][:].bitcast(F32).rearrange("p (u t) -> p t u", u=2)[:, c * BANK : (c + 1) * BANK, :]
             else:
-                planes = pairs[b][:, c * PACK * BANK : (c + 1) * PACK * BANK]
-                nc.scalar.copy(
-                    z[:].bitcast(F32).rearrange("p (t u) -> p t u", u=2),
-                    planes.bitcast(F32).rearrange("p (u t) -> p t u", u=2),
-                )
+                chunk = pairs[b][:, c * PACK * BANK : (c + 1) * PACK * BANK]
+                words = chunk.bitcast(F32).rearrange("p (u t) -> p t u", u=2)
+            nc.scalar.copy(z[:].bitcast(F32).rearrange("p (t u) -> p t u", u=2), words)
             return z
 
-        whole = slice(0, T2)
         weigh(0)
         weigh(1)
         pages.append(keep.tile([P, T2], F32, name="page2", tag="page2", align_bytes=64))
@@ -257,12 +259,13 @@ def tile_list_courier_eta_banks_kernel(
         ident = keep.tile([P, P], F32, name="ident", tag="codes1", align_bytes=64)
         make_identity(nc, ident[:])
         for step in range(2):
-            add_road(nc.gpsimd, ORDER[step], whole)
+            add_road(step)
             load_road(step + PACK)
             weigh(step + PACK)
             put(step + PAGES)
         weigh(6)
         weigh(7)
+
         for j in range(STRIPS):
             turn(j, roads[2], 0, start=True)
             turn(j, roads[3], 1)
@@ -270,9 +273,9 @@ def tile_list_courier_eta_banks_kernel(
         last_road = []
         for u, cols in enumerate((slice(0, BANK), slice(BANK, T2))):
             rows = keep.tile(
-                [P, cols.stop - cols.start], F32, name=f"road7_{u}", tag=("w1", "road3")[u], align_bytes=64
+                [P, cols.stop - cols.start], F32, name=f"last_road{u}", tag=("late", "road3")[u], align_bytes=64
             )
-            nc.sync.dma_start(rows[:], road_rows[1, PACK - 1][:, cols])
+            nc.sync.dma_start(rows[:], road_rows[LAST // PACK, LAST % PACK][:, cols])
             last_road.append(rows)
         for j in range(STRIPS):
             turn(j, page_of[2], 0)
@@ -285,24 +288,21 @@ def tile_list_courier_eta_banks_kernel(
                 banks[j][:].rearrange("t (s e p) -> t s p e", s=2, e=2),
             )
             turned.append(strip)
-
-        def turn_back():
-            for c in range(CHUNKS):
-                for s in range(PACK):
-                    words = turned[2 * c + s // 2][:].bitcast(F32)
-                    nc.tensor.transpose(
-                        banks[c][:, s * P : (s + 1) * P], words[:, (s % 2) * P : (s % 2 + 1) * P], ident[:]
-                    )
-                nc.scalar.copy(pairs[0][:].bitcast(F32)[:, T2 + c * BANK : T2 + (c + 1) * BANK], banks[c][:])
-
-        turn_back()
+        for c in range(CHUNKS):
+            for s in range(BANK // P):
+                words = turned[2 * c + s // 2][:].bitcast(F32)
+                nc.tensor.transpose(
+                    banks[c][:, s * P : (s + 1) * P], words[:, (s % 2) * P : (s % 2 + 1) * P], ident[:]
+                )
+            nc.scalar.copy(pairs[0][:].bitcast(F32)[:, T2 + c * BANK : T2 + (c + 1) * BANK], banks[c][:])
         z0 = [weave(0, c) for c in range(CHUNKS)]
+
         put(5)
         put(6)
-        add_road(nc.gpsimd, ORDER[4], whole)
+        add_road(4)
         put(7)
-        add_road(nc.gpsimd, ORDER[5], whole)
-        add_road(nc.gpsimd, ORDER[6], whole)
+        add_road(5)
+        add_road(6)
 
         w2_codes = keep.tile([P, PASSES * N], U32, name="w2_codes", align_bytes=64)
         z_codes = {}
@@ -312,46 +312,36 @@ def tile_list_courier_eta_banks_kernel(
         def quantise(b, c, z):
             tag = ("codes0", "slot4", "slot1", "slot2")[c] if b == 0 else f"codes{PACK + c}"
             codes = keep.tile([P, BANK], U32, name=f"z_codes{b}_{c}", tag=tag, align_bytes=64)
-            if b == 0:
-                plane = late_plane[:, c * BANK : (c + 1) * BANK]
-            else:
-                plane = z1_plane[:, c * BANK : (c + 1) * BANK]
+            plane = (late_plane, z1_plane)[b][:, c * BANK : (c + 1) * BANK]
             nc.vector.quantize_mx(out=codes[:].bitcast(E4M3), scales=plane, in_=z[:])
             z_codes[b, c] = codes
             z_plane[b, c] = plane
 
         def last_sum(c):
             cols = slice(c * BANK, (c + 1) * BANK)
-            plane = pairs[1][:, ((c + 1) * PACK - 2) * BANK + 1 : (c + 1) * PACK * BANK : 2]
+            halves = pairs[1][:, ((c + 1) * PACK - 2) * BANK + 1 : (c + 1) * PACK * BANK : 2]
             rows = last_road[0][:] if c == 0 else last_road[1][:, cols.start - BANK : cols.stop - BANK]
-            nc.vector.tensor_tensor(plane, page_of[SLICES - 1][:, cols], rows, ADD)
+            nc.vector.tensor_tensor(halves, page_of[LAST][:, cols], rows, ADD)
 
         def bank_of(c, nt):
-            return banks[(4 * c + nt) % 8]
-
-        def multiply(c, nt, curve):
-            bank = bank_of(c, nt)
-            for b in range(PASSES):
-                w_cols = slice(b * N + nt * P, b * N + (nt + 1) * P)
-                nc.tensor.matmul_mx(
-                    out=bank[:],
-                    lhsT=w2_codes[:, w_cols].bitcast(E4M3),
-                    lhsT_scale=w2_plane[:, w_cols],
-                    rhs=z_codes[b, c][:].bitcast(E4M3),
-                    rhs_scale=z_plane[b, c],
-                    start=(b == 0),
-                    stop=(b == PASSES - 1),
-                )
-            nc.scalar.activation(curve[:, nt % 2, :], bank[:], TANH)
-
-        def add_and_store(c, nt, delay):
-            nc.vector.tensor_tensor(delay[:, nt % 2, :], delay[:, nt % 2, :], bank_of(c, nt)[:], ADD)
-            nc.sync.dma_start(out[nt * P : (nt + 1) * P, c * BANK : (c + 1) * BANK], delay[:, nt % 2, :])
+            return banks[(N // P * c + nt) % BANKS]
 
         def curves(c, u):
-            curve = results.tile([P, 2, BANK], F32, name=("curve_low", "curve_high")[u], bufs=2 + 2 * u)
-            for nt in (2 * u, 2 * u + 1):
-                multiply(c, nt, curve)
+            curve = results.tile([P, 2, BANK], F32, name=("curve_low", "curve_high")[u], bufs=(2, CHUNKS)[u])
+            for e in range(2):
+                nt = 2 * u + e
+                for b in range(PASSES):
+                    w_cols = slice(b * N + nt * P, b * N + (nt + 1) * P)
+                    nc.tensor.matmul_mx(
+                        out=bank_of(c, nt)[:],
+                        lhsT=w2_codes[:, w_cols].bitcast(E4M3),
+                        lhsT_scale=w2_plane[:, w_cols],
+                        rhs=z_codes[b, c][:].bitcast(E4M3),
+                        rhs_scale=z_plane[b, c],
+                        start=(b == 0),
+                        stop=(b == PASSES - 1),
+                    )
+                nc.scalar.activation(curve[:, e, :], bank_of(c, nt)[:], TANH)
             return curve
 
         def jam_of(c, u):
@@ -359,7 +349,7 @@ def tile_list_courier_eta_banks_kernel(
 
         last_sum(0)
         z1 = [weave(1, 0)]
-        late_plane = keep.tile([P, T2 + PASSES * N], U8, name="late_plane", tag="w1", align_bytes=64)
+        late_plane = keep.tile([P, T2 + PASSES * N], U8, name="late_plane", tag="late", align_bytes=64)
         w2_plane = late_plane[:, T2:]
         nc.vector.quantize_mx(out=w2_codes[:].bitcast(E4M3), scales=w2_plane, in_=w2_grouped[:])
         quantise(0, 0, z0[0])
@@ -373,19 +363,27 @@ def tile_list_courier_eta_banks_kernel(
         for c in range(2, CHUNKS):
             quantise(0, c, z0[c])
             quantise(1, c, weave(1, c))
+
         low = curves(0, 0)
         high = curves(0, 1)
-        delay_low = results.tile([P, 2, BANK], F32, name="delay", bufs=3)
+        delay_low = results.tile([P, 2, BANK], F32, name="delay")
         nc.vector.tensor_tensor(delay_low[:], low[:], jam_of(0, 0), MULT)
         for c in range(CHUNKS):
-            if c + 1 < CHUNKS:
+            last_chunk = c + 1 == CHUNKS
+            if not last_chunk:
                 low = curves(c + 1, 0)
-            delay_high = results.tile([P, 2, BANK], F32, name="delay", bufs=3)
-            nc.vector.tensor_tensor(delay_high[:], high[:], jam_of(c, 1), MULT)
-            if c + 1 < CHUNKS:
+            delay_high = results.tile([P, 2, BANK], F32, name="delay")
+            if last_chunk:
+                nc.vector.tensor_tensor(delay_high[:, 0, :], high[:, 0, :], jam_of(c, 1)[:, 0, :], MULT)
+                nc.gpsimd.tensor_tensor(high[:, 0, :], high[:, 1, :], jam_of(c, 1)[:, 1, :], MULT)
+                last_delay = high[:, 0, :]
+            else:
+                nc.vector.tensor_tensor(delay_high[:], high[:], jam_of(c, 1), MULT)
                 nc.gpsimd.tensor_tensor(high[:], low[:], jam_of(c + 1, 0), MULT)
-            for nt in range(4):
-                add_and_store(c, nt, delay_low if nt < 2 else delay_high)
-            delay_low = high
-            if c + 1 < CHUNKS:
+                last_delay = delay_high[:, 1, :]
+            for nt, delay in enumerate((delay_low[:, 0, :], delay_low[:, 1, :], delay_high[:, 0, :], last_delay)):
+                nc.vector.tensor_tensor(delay, delay, bank_of(c, nt)[:], ADD)
+                nc.sync.dma_start(out[nt * P : (nt + 1) * P, c * BANK : (c + 1) * BANK], delay)
+            if not last_chunk:
+                delay_low = high
                 high = curves(c + 1, 1)

@@ -34,6 +34,14 @@ FIRST_BANKS = 3
 ORDER = (0, 1, 2, 3, 6, 4, 5, 7)
 LAST = ORDER[-1]
 FIRST_PIECES = (128, 128, 256, 512)
+TILES = N // P * CHUNKS
+VECTOR_SHARE = 7
+VECTOR_TILES = [n for n in range(TILES) if (TILES - 1 - n) * VECTOR_SHARE % TILES < VECTOR_SHARE]
+VECTOR_COLUMNS = 1280
+ROAD_BANKS = 3
+AHEAD = 2
+Z_BYTES = 2 * PACK * BANK
+JAM_BANKS = 2
 FIRST_WEIGHTS = 256
 
 
@@ -44,7 +52,7 @@ def tile_list_courier_eta_banks_kernel(
     with ExitStack() as ctx:
         lists = ctx.enter_context(tc.tile_pool(name="lists", bufs=1))
         keep = ctx.enter_context(tc.tile_pool(name="keep", bufs=1))
-        results = ctx.enter_context(tc.tile_pool(name="results", bufs=3))
+        relay = ctx.enter_context(tc.tile_pool(name="relay", bufs=1))
         psum = ctx.enter_context(tc.psum_pool(name="psum", bufs=1))
         banks = [psum.tile([P, BANK], F32, name=f"bank{j}") for j in range(BANKS)]
 
@@ -55,7 +63,7 @@ def tile_list_courier_eta_banks_kernel(
             nc.vector.memset(tab_plane[32 * q : 32 * q + 24, :].bitcast(I32), 0)
         v_plane = keep.tile([P, PASSES * S], U8, name="v_plane", align_bytes=64)
         nc.gpsimd.memset(v_plane[96:128, :].bitcast(I32), 0)
-        pages = [keep.tile([P, T2], F32, name=f"page{j}") for j in range(2)]
+        pages = [keep.tile([P, T2], F32, name=f"page{j}", tag=f"page{j}", align_bytes=64) for j in range(2)]
         for page in pages:
             nc.gpsimd.memset(page[:], 0.0)
 
@@ -239,10 +247,11 @@ def tile_list_courier_eta_banks_kernel(
                 )
 
         def weave(b, c):
-            z = keep.tile([P, PACK * BANK], BF16, name=f"z{b}_{c}", tag=f"slot{PACK * b + c}", align_bytes=64)
             if b == 0:
+                z = keep.tile([P, PACK * BANK], BF16, name=f"z0_{c}", tag=f"slot{c}", align_bytes=64)
                 words = pairs[b][:].bitcast(F32).rearrange("p (u t) -> p t u", u=2)[:, c * BANK : (c + 1) * BANK, :]
             else:
+                z = relay.tile([P, PACK * BANK], BF16, name=f"z1_{c}", offset=c * Z_BYTES, align_bytes=64)
                 chunk = pairs[b][:, c * PACK * BANK : (c + 1) * PACK * BANK]
                 words = chunk.bitcast(F32).rearrange("p (u t) -> p t u", u=2)
             nc.scalar.copy(z[:].bitcast(F32).rearrange("p (t u) -> p t u", u=2), words)
@@ -270,13 +279,7 @@ def tile_list_courier_eta_banks_kernel(
             turn(j, roads[2], 0, start=True)
             turn(j, roads[3], 1)
         load_road(6)
-        last_road = []
-        for u, cols in enumerate((slice(0, BANK), slice(BANK, T2))):
-            rows = keep.tile(
-                [P, cols.stop - cols.start], F32, name=f"last_road{u}", tag=("late", "road3")[u], align_bytes=64
-            )
-            nc.sync.dma_start(rows[:], road_rows[LAST // PACK, LAST % PACK][:, cols])
-            last_road.append(rows)
+        load_road(7)
         for j in range(STRIPS):
             turn(j, page_of[2], 0)
         turned = []
@@ -297,6 +300,47 @@ def tile_list_courier_eta_banks_kernel(
             nc.scalar.copy(pairs[0][:].bitcast(F32)[:, T2 + c * BANK : T2 + (c + 1) * BANK], banks[c][:])
         z0 = [weave(0, c) for c in range(CHUNKS)]
 
+        def jam_of(n):
+            c, nt = divmod(n, N // P)
+            return jams[nt // 2][:, nt % 2, c * BANK : (c + 1) * BANK]
+
+        def turn_blocks(bank, source, width=BANK):
+            for s in range(width // P):
+                nc.tensor.transpose(bank[:, s * P : (s + 1) * P], source[:, s * P : (s + 1) * P], ident[:])
+
+        road_cols = [slice(c * BANK, min((c + 1) * BANK, VECTOR_COLUMNS)) for c in range(ROAD_BANKS)]
+        first_free = BANKS - ROAD_BANKS - JAM_BANKS
+        road_banks = banks[BANKS - ROAD_BANKS :]
+        jam_banks = banks[first_free : first_free + JAM_BANKS]
+        turns = []
+
+        def stage(once, source, width=BANK):
+            bank = banks[len(turns) % first_free]
+            turns.append(bank)
+            turn_blocks(bank, source, width)
+            nc.scalar.copy(once, bank[:, :width])
+            return once
+
+        staged = {}
+        for j in range(JAM_BANKS, VECTOR_SHARE):
+            staged[j] = stage(keep.tile([P, BANK], F32, name=f"staged{j}")[:], jam_of(VECTOR_TILES[j]))
+        early = relay.tile([P, CHUNKS * Z_BYTES // 4], F32, name="early", offset=0, align_bytes=64)
+        for j in range(JAM_BANKS):
+            staged[j] = stage(early[:, j * BANK : (j + 1) * BANK], jam_of(VECTOR_TILES[j]))
+        staged_road = []
+        for cols in road_cols:
+            width = cols.stop - cols.start
+            first = JAM_BANKS * BANK + cols.start
+            staged_road.append(stage(early[:, first : first + width], roads[LAST][:, cols], width))
+
+        def bring_jam(j):
+            turn_blocks(jam_banks[j % JAM_BANKS], staged[j])
+
+        for j in range(JAM_BANKS):
+            bring_jam(j)
+        for c, cols in enumerate(road_cols):
+            turn_blocks(road_banks[c], staged_road[c], cols.stop - cols.start)
+
         put(5)
         put(6)
         add_road(4)
@@ -310,80 +354,86 @@ def tile_list_courier_eta_banks_kernel(
         z1_plane = keep.tile([P, T2], U8, name="z1_plane", align_bytes=64)
 
         def quantise(b, c, z):
-            tag = ("codes0", "slot4", "slot1", "slot2")[c] if b == 0 else f"codes{PACK + c}"
+            tag = ("codes0", "codes2", "codes3", "slot0")[c] if b == 0 else f"slot{PACK + c}"
             codes = keep.tile([P, BANK], U32, name=f"z_codes{b}_{c}", tag=tag, align_bytes=64)
             plane = (late_plane, z1_plane)[b][:, c * BANK : (c + 1) * BANK]
             nc.vector.quantize_mx(out=codes[:].bitcast(E4M3), scales=plane, in_=z[:])
             z_codes[b, c] = codes
             z_plane[b, c] = plane
 
-        def last_sum(c):
-            cols = slice(c * BANK, (c + 1) * BANK)
-            halves = pairs[1][:, ((c + 1) * PACK - 2) * BANK + 1 : (c + 1) * PACK * BANK : 2]
-            rows = last_road[0][:] if c == 0 else last_road[1][:, cols.start - BANK : cols.stop - BANK]
-            nc.vector.tensor_tensor(halves, page_of[LAST][:, cols], rows, ADD)
+        def odd_halves(cols):
+            c, t = divmod(cols.start, BANK)
+            first = (PACK * c + 2) * BANK + 2 * t + 1
+            return pairs[1][:, first : first + 2 * (cols.stop - cols.start) - 1 : 2]
 
-        def bank_of(c, nt):
-            return banks[(N // P * c + nt) % BANKS]
-
-        def curves(c, u):
-            curve = results.tile([P, 2, BANK], F32, name=("curve_low", "curve_high")[u], bufs=(2, CHUNKS)[u])
-            for e in range(2):
-                nt = 2 * u + e
-                for b in range(PASSES):
-                    w_cols = slice(b * N + nt * P, b * N + (nt + 1) * P)
-                    nc.tensor.matmul_mx(
-                        out=bank_of(c, nt)[:],
-                        lhsT=w2_codes[:, w_cols].bitcast(E4M3),
-                        lhsT_scale=w2_plane[:, w_cols],
-                        rhs=z_codes[b, c][:].bitcast(E4M3),
-                        rhs_scale=z_plane[b, c],
-                        start=(b == 0),
-                        stop=(b == PASSES - 1),
-                    )
-                nc.scalar.activation(curve[:, e, :], bank_of(c, nt)[:], TANH)
-            return curve
-
-        def jam_of(c, u):
-            return jams[u][:, :, c * BANK : (c + 1) * BANK]
-
-        last_sum(0)
-        z1 = [weave(1, 0)]
-        late_plane = keep.tile([P, T2 + PASSES * N], U8, name="late_plane", tag="late", align_bytes=64)
+        for c in range(VECTOR_COLUMNS // BANK, CHUNKS):
+            cols = slice(max(c * BANK, VECTOR_COLUMNS), (c + 1) * BANK)
+            nc.gpsimd.tensor_tensor(odd_halves(cols), page_of[LAST][:, cols], roads[LAST][:, cols], ADD)
+        for c, cols in enumerate(road_cols):
+            rows = road_banks[c][:, : cols.stop - cols.start]
+            nc.vector.tensor_tensor(odd_halves(cols), page_of[LAST][:, cols], rows, ADD)
+        z1 = [weave(1, c) for c in range(CHUNKS)]
+        late_plane = keep.tile(
+            [P, T2 + PASSES * N], U8, name="late_plane", tag=f"page{(SLICES - 1) % PAGES}", align_bytes=64
+        )
         w2_plane = late_plane[:, T2:]
         nc.vector.quantize_mx(out=w2_codes[:].bitcast(E4M3), scales=w2_plane, in_=w2_grouped[:])
-        quantise(0, 0, z0[0])
-        last_sum(1)
-        z1.append(weave(1, 1))
-        quantise(1, 0, z1[0])
-        quantise(0, 1, z0[1])
-        last_sum(2)
-        last_sum(3)
-        quantise(1, 1, z1[1])
-        for c in range(2, CHUNKS):
-            quantise(0, c, z0[c])
-            quantise(1, c, weave(1, c))
-
-        low = curves(0, 0)
-        high = curves(0, 1)
-        delay_low = results.tile([P, 2, BANK], F32, name="delay")
-        nc.vector.tensor_tensor(delay_low[:], low[:], jam_of(0, 0), MULT)
         for c in range(CHUNKS):
-            last_chunk = c + 1 == CHUNKS
-            if not last_chunk:
-                low = curves(c + 1, 0)
-            delay_high = results.tile([P, 2, BANK], F32, name="delay")
-            if last_chunk:
-                nc.vector.tensor_tensor(delay_high[:, 0, :], high[:, 0, :], jam_of(c, 1)[:, 0, :], MULT)
-                nc.gpsimd.tensor_tensor(high[:, 0, :], high[:, 1, :], jam_of(c, 1)[:, 1, :], MULT)
-                last_delay = high[:, 0, :]
-            else:
-                nc.vector.tensor_tensor(delay_high[:], high[:], jam_of(c, 1), MULT)
-                nc.gpsimd.tensor_tensor(high[:], low[:], jam_of(c + 1, 0), MULT)
-                last_delay = delay_high[:, 1, :]
-            for nt, delay in enumerate((delay_low[:, 0, :], delay_low[:, 1, :], delay_high[:, 0, :], last_delay)):
-                nc.vector.tensor_tensor(delay, delay, bank_of(c, nt)[:], ADD)
-                nc.sync.dma_start(out[nt * P : (nt + 1) * P, c * BANK : (c + 1) * BANK], delay)
-            if not last_chunk:
-                delay_low = high
-                high = curves(c + 1, 1)
+            quantise(0, c, z0[c])
+            quantise(1, c, z1[c])
+
+        curve_tiles = [
+            keep.tile([P, TILES // 2 * BANK], F32, name=f"curves{j}", tag=("pairs0", "curves1")[j], align_bytes=64)
+            for j in range(2)
+        ]
+        free_banks = banks[:first_free] + road_banks
+        bank_of, curve, delay = {}, {}, {}
+
+        def product(n):
+            c, nt = divmod(n, N // P)
+            bank_of[n] = free_banks[n]
+            for b in range(PASSES):
+                w_cols = slice(b * N + nt * P, b * N + (nt + 1) * P)
+                nc.tensor.matmul_mx(
+                    out=bank_of[n][:],
+                    lhsT=w2_codes[:, w_cols].bitcast(E4M3),
+                    lhsT_scale=w2_plane[:, w_cols],
+                    rhs=z_codes[b, c][:].bitcast(E4M3),
+                    rhs_scale=z_plane[b, c],
+                    start=(b == 0),
+                    stop=(b == PASSES - 1),
+                )
+            j, place = divmod(n, TILES // 2)
+            curve[n] = curve_tiles[j][:, place * BANK : (place + 1) * BANK]
+            nc.scalar.activation(curve[n], bank_of[n][:], TANH)
+
+        def vector_delay(n):
+            j = VECTOR_TILES.index(n)
+            delay[n] = curve[n]
+            nc.vector.tensor_tensor(delay[n], curve[n], jam_banks[j % JAM_BANKS][:], MULT)
+            if j + JAM_BANKS < VECTOR_SHARE:
+                bring_jam(j + JAM_BANKS)
+
+        first_delay = relay.tile([P, BANK], F32, name="first_delay", offset=(CHUNKS - 1) * Z_BYTES, align_bytes=64)
+        spent = [first_delay[:]]
+
+        def gpsimd_delay(n):
+            delay[n] = spent[-1]
+            nc.gpsimd.tensor_tensor(delay[n], curve[n], jam_of(n), MULT)
+            spent.append(curve[n])
+
+        def finish(n):
+            c, nt = divmod(n, N // P)
+            nc.vector.tensor_tensor(delay[n], delay[n], bank_of[n][:], ADD)
+            nc.sync.dma_start(out[nt * P : (nt + 1) * P, c * BANK : (c + 1) * BANK], delay[n])
+            free_banks.append(bank_of[n])
+            if len(bank_of) < TILES:
+                product(len(bank_of))
+
+        for n in range(len(free_banks)):
+            product(n)
+        for n in range(TILES + AHEAD):
+            if n < TILES:
+                (vector_delay if n in VECTOR_TILES else gpsimd_delay)(n)
+            if n >= AHEAD:
+                finish(n - AHEAD)

@@ -56,16 +56,18 @@ def tile_list_courier_eta_banks_kernel(
         psum = ctx.enter_context(tc.psum_pool(name="psum", bufs=1))
         banks = [psum.tile([P, BANK], F32, name=f"bank{j}") for j in range(BANKS)]
 
-        w1_plane = keep.tile([P, PASSES * H], U8, name="w1_plane", tag="codes1", align_bytes=64)
-        nc.gpsimd.memset(w1_plane[:].bitcast(I32), 0)
         tab_plane = keep.tile([P, T + 4], U8, name="tab_plane", tag="road0", align_bytes=64)
         for q in range(4):
             nc.vector.memset(tab_plane[32 * q : 32 * q + 24, :].bitcast(I32), 0)
+        w1_plane = keep.tile([P, PASSES * H], U8, name="w1_plane", tag="codes1", align_bytes=64)
+        nc.gpsimd.memset(w1_plane[:].bitcast(I32), 0)
         v_plane = keep.tile([P, PASSES * S], U8, name="v_plane", align_bytes=64)
         nc.gpsimd.memset(v_plane[96:128, :].bitcast(I32), 0)
         pages = [keep.tile([P, T2], F32, name=f"page{j}", tag=f"page{j}", align_bytes=64) for j in range(2)]
         for page in pages:
             nc.gpsimd.memset(page[:], 0.0)
+        ident = keep.tile([P, P], F32, name="ident", align_bytes=64)
+        make_identity(nc, ident[:])
 
         picks = lists.tile([P, S // LIST_ROWS], U16, name="picks")
         nc.sync.dma_start(picks[:], offs)
@@ -86,11 +88,16 @@ def tile_list_courier_eta_banks_kernel(
             )
 
         load_table(0)
-        w1_raw = keep.tile([P, PASSES * 2 * H], U8, name="w1_raw", tag="page2", align_bytes=64)
-        nc.sync.dma_start(
-            w1_raw[:].bitcast(I32).rearrange("p (a c) -> p a c", a=PASSES),
-            w1_words.bitcast(I32).rearrange("a p c -> p a c"),
-        )
+        w1_raw = {}
+
+        def load_w1(b):
+            w1_raw[b] = keep.tile([P, 2 * H], U8, name=f"w1_raw{b}", tag=("page2", "curves1")[b], align_bytes=64)
+            nc.sync.dma_start(
+                w1_raw[b][:].bitcast(I32).rearrange("p (a c) -> p a c", a=PASSES),
+                w1_words[:, :, b * H : (b + 1) * H].bitcast(I32).rearrange("a p c -> p a c"),
+            )
+
+        load_w1(0)
         for q in range(4):
             nc.sync.dma_start(
                 w1_plane[32 * q : 32 * q + 4, :].bitcast(I32).rearrange("r (a c) -> r a c", a=PASSES),
@@ -120,6 +127,7 @@ def tile_list_courier_eta_banks_kernel(
             nc.sync.dma_start(roads[k][:], road_rows[k // PACK, k % PACK])
 
         load_road(0)
+        load_w1(1)
         load_road(1)
         w2_raw = keep.tile([P, PASSES * PACK * N], F32, name="w2_raw", tag="wide1", align_bytes=64)
         nc.sync.dma_start(
@@ -129,25 +137,31 @@ def tile_list_courier_eta_banks_kernel(
         load_road(2)
         load_road(3)
 
-        w1_codes = keep.tile([P, PASSES * 2 * H], U8, name="w1_codes", tag="pairs0", align_bytes=64)
-        nc.vector.tensor_copy(
-            w1_codes[:].bitcast(U16).rearrange("p (g i m) -> p g i m", i=PACK, m=P),
-            w1_raw[:].bitcast(U16).rearrange("p (g m i) -> p g i m", i=PACK, m=P),
-        )
-        w1_scale = []
-        for b in range(PASSES):
-            ordered = keep.tile([P, H], U8, name=f"w1_scale{b}", tag=("page2", "late")[b], align_bytes=64)
+        w1_codes, w1_scale = {}, {}
+
+        def deal_codes(b):
+            w1_codes[b] = keep.tile([P, 2 * H], U8, name=f"w1_codes{b}", tag=("pairs1", "pairs0")[b], align_bytes=64)
+            (nc.vector, nc.gpsimd)[b].tensor_copy(
+                w1_codes[b][:].bitcast(U16).rearrange("p (a i m) -> p a i m", i=PACK, m=P),
+                w1_raw[b][:].bitcast(U16).rearrange("p (a m i) -> p a i m", i=PACK, m=P),
+            )
+
+        def deal_scales(b):
+            w1_scale[b] = keep.tile([P, H], U8, name=f"w1_scale{b}", tag=("page2", "w1_scale1")[b], align_bytes=64)
             nc.gpsimd.tensor_copy(
-                ordered[:].rearrange("p (a i m) -> p a i m", i=PACK, m=P),
+                w1_scale[b][:].rearrange("p (a i m) -> p a i m", i=PACK, m=P),
                 w1_plane[:].rearrange("p (a b m i) -> p b a i m", a=PASSES, i=PACK, m=P)[:, b],
             )
-            w1_scale.append(ordered)
+
+        deal_codes(0)
+        deal_scales(0)
+        deal_scales(1)
 
         v_codes = {}
         for half in range(2):
             for a in range(PASSES):
                 words = keep.tile(
-                    [P, BANK], U32, name=f"v_codes{a}{half}", tag=f"codes{2 * a + half}", align_bytes=64
+                    [P, BANK], U32, name=f"v_codes{a}{half}", tag=("codes0", "codes4", "codes2", "codes3")[2 * a + half], align_bytes=64
                 )
                 entries = picks[:, half * BANK // LIST_ROWS : (half + 1) * BANK // LIST_ROWS]
                 nc.vector.tensor_copy(words[:], tab[:, a * T : (a + 1) * T].bitcast(U32).indirect(entries))
@@ -158,32 +172,45 @@ def tile_list_courier_eta_banks_kernel(
             return [slice(sum(widths[:j]), sum(widths[: j + 1])) for j in range(len(widths))]
 
         h = {}
-        for step, k in enumerate(ORDER):
+
+        def first_product(step):
+            k = ORDER[step]
             b, i = divmod(k, PACK)
             h[k] = keep.tile([P, S], F32, name=f"h{k}", tag=f"slot{step}", align_bytes=64)
-            for half in range(2):
-                bank = banks[(2 * step + half) % FIRST_BANKS]
-                for a in range(PASSES):
-                    code0 = 2 * P * (a * SLICES + k)
-                    scale0 = P * (a * PACK + i)
-                    nc.tensor.matmul_mx(
-                        out=bank[:],
-                        lhsT=w1_codes[:, code0 : code0 + 2 * P].bitcast(E2M1),
-                        lhsT_scale=w1_scale[b][:, scale0 : scale0 + P],
-                        rhs=v_codes[a, half][:].bitcast(E4M3),
-                        rhs_scale=v_plane[:, a * S + half * BANK : a * S + (half + 1) * BANK],
-                        start=(a == 0),
-                        stop=(a == PASSES - 1),
-                    )
-                for cols in pieces_of(k):
-                    lo, hi = max(cols.start, half * BANK), min(cols.stop, (half + 1) * BANK)
-                    if lo < hi:
-                        nc.scalar.activation(
-                            h[k][:, lo:hi],
-                            bank[:, lo - half * BANK : hi - half * BANK],
-                            RELU,
-                            bias=bias[:, k : k + 1],
+            for j, cols in enumerate(pieces_of(k) if step == 0 else (slice(0, BANK), slice(BANK, S))):
+                half, start = divmod(cols.start, BANK)
+                count = cols.stop - cols.start
+                bank = banks[(2 * step + half) % FIRST_BANKS] if count == BANK else banks[FIRST_BANKS + j]
+                width = BANK if count == BANK else P
+                order = (1, 0) if count == BANK else (0, 1)
+                for first in range(0, count, width):
+                    for a in order:
+                        scale0 = P * (a * PACK + i)
+                        code0 = 2 * scale0
+                        entry0 = a * S + cols.start + first
+                        nc.tensor.matmul_mx(
+                            out=bank[:, first : first + width],
+                            lhsT=w1_codes[b][:, code0 : code0 + 2 * P].bitcast(E2M1),
+                            lhsT_scale=w1_scale[b][:, scale0 : scale0 + P],
+                            rhs=v_codes[a, half][:, start + first : start + first + width].bitcast(E4M3),
+                            rhs_scale=v_plane[:, entry0 : entry0 + width],
+                            start=(a == order[0]),
+                            stop=(a == order[-1]),
                         )
+                nc.scalar.activation(h[k][:, cols], bank[:, :count], RELU, bias=bias[:, k : k + 1])
+
+        def weigh(step):
+            k = ORDER[step]
+            for cols in pieces_of(k):
+                nc.gpsimd.tensor_tensor(h[k][:, cols], h[k][:, cols], weights[:, cols], MULT)
+
+        for step in range(PACK):
+            first_product(step)
+        weigh(0)
+        weigh(1)
+        deal_codes(1)
+        for step in range(PACK, SLICES):
+            first_product(step)
 
         w2_grouped = keep.tile([P, PASSES * PACK * N], BF16, name="w2_grouped", tag="codes0", align_bytes=64)
         for b in range(PASSES):
@@ -202,11 +229,6 @@ def tile_list_courier_eta_banks_kernel(
             jams.append(rows[:].rearrange("p (e t) -> p e t", e=2))
 
         page_of = {}
-
-        def weigh(step):
-            k = ORDER[step]
-            for cols in pieces_of(k):
-                nc.gpsimd.tensor_tensor(h[k][:, cols], h[k][:, cols], weights[:, cols], MULT)
 
         def put(step):
             k = ORDER[step]
@@ -257,16 +279,12 @@ def tile_list_courier_eta_banks_kernel(
             nc.scalar.copy(z[:].bitcast(F32).rearrange("p (t u) -> p t u", u=2), words)
             return z
 
-        weigh(0)
-        weigh(1)
         pages.append(keep.tile([P, T2], F32, name="page2", tag="page2", align_bytes=64))
         nc.gpsimd.memset(pages[2][:], 0.0)
         weigh(2)
         weigh(3)
         for step in range(PAGES):
             put(step)
-        ident = keep.tile([P, P], F32, name="ident", tag="codes1", align_bytes=64)
-        make_identity(nc, ident[:])
         for step in range(2):
             add_road(step)
             load_road(step + PACK)
@@ -354,8 +372,11 @@ def tile_list_courier_eta_banks_kernel(
         z1_plane = keep.tile([P, T2], U8, name="z1_plane", align_bytes=64)
 
         def quantise(b, c, z):
-            tag = ("codes0", "codes2", "codes3", "slot0")[c] if b == 0 else f"slot{PACK + c}"
-            codes = keep.tile([P, BANK], U32, name=f"z_codes{b}_{c}", tag=tag, align_bytes=64)
+            if b == 0 and c > 0:
+                codes = relay.tile([P, BANK], U32, name=f"z_codes0_{c}", offset=(c - 1) * Z_BYTES, align_bytes=64)
+            else:
+                tag = f"slot{PACK + c}" if b else "codes0"
+                codes = keep.tile([P, BANK], U32, name=f"z_codes{b}_{c}", tag=tag, align_bytes=64)
             plane = (late_plane, z1_plane)[b][:, c * BANK : (c + 1) * BANK]
             nc.vector.quantize_mx(out=codes[:].bitcast(E4M3), scales=plane, in_=z[:])
             z_codes[b, c] = codes
@@ -414,13 +435,18 @@ def tile_list_courier_eta_banks_kernel(
             if j + JAM_BANKS < VECTOR_SHARE:
                 bring_jam(j + JAM_BANKS)
 
-        first_delay = relay.tile([P, BANK], F32, name="first_delay", offset=(CHUNKS - 1) * Z_BYTES, align_bytes=64)
-        spent = [first_delay[:]]
+        held = [
+            keep.tile([P, 2 * BANK], F32, name="held0", tag=f"slot{CHUNKS - 1}", align_bytes=64),
+            relay.tile([P, 2 * BANK], F32, name="held1", offset=(CHUNKS - 1) * Z_BYTES, align_bytes=64),
+        ]
+        early_tiles = [n for n in range(len(free_banks)) if n not in VECTOR_TILES]
 
         def gpsimd_delay(n):
-            delay[n] = spent[-1]
+            delay[n] = curve[n]
+            if n in early_tiles:
+                j, place = divmod(early_tiles.index(n), 2)
+                delay[n] = held[j][:, place * BANK : (place + 1) * BANK]
             nc.gpsimd.tensor_tensor(delay[n], curve[n], jam_of(n), MULT)
-            spent.append(curve[n])
 
         def finish(n):
             c, nt = divmod(n, N // P)

@@ -33,7 +33,8 @@ STRIPS = T2 // STRIP
 FIRST_BANKS = 3
 ORDER = (0, 1, 2, 3, 6, 4, 5, 7)
 LAST = ORDER[-1]
-FIRST_PIECES = (128, 128, 256, 512)
+FIRST_PIECES = (128, 384, 512)
+FIRST_STEPS = 2
 TILES = N // P * CHUNKS
 VECTOR_SHARE = 7
 VECTOR_TILES = [n for n in range(TILES) if (TILES - 1 - n) * VECTOR_SHARE % TILES < VECTOR_SHARE]
@@ -42,7 +43,7 @@ ROAD_BANKS = 3
 AHEAD = 2
 Z_BYTES = 2 * PACK * BANK
 JAM_BANKS = 2
-FIRST_WEIGHTS = 256
+FIRST_WEIGHTS = 512
 
 
 def tile_list_courier_eta_banks_kernel(
@@ -87,7 +88,6 @@ def tile_list_courier_eta_banks_kernel(
                 tab[:, a * T : (a + 1) * T], tab_words[a].rearrange("p t i -> p (t i)").bitcast(I32)
             )
 
-        load_table(0)
         w1_raw = {}
 
         def load_w1(b):
@@ -98,6 +98,7 @@ def tile_list_courier_eta_banks_kernel(
             )
 
         load_w1(0)
+        load_table(0)
         for q in range(4):
             nc.sync.dma_start(
                 w1_plane[32 * q : 32 * q + 4, :].bitcast(I32).rearrange("r (a c) -> r a c", a=PASSES),
@@ -140,7 +141,7 @@ def tile_list_courier_eta_banks_kernel(
         w1_codes, w1_scale = {}, {}
 
         def deal_codes(b):
-            w1_codes[b] = keep.tile([P, 2 * H], U8, name=f"w1_codes{b}", tag=("pairs1", "pairs0")[b], align_bytes=64)
+            w1_codes[b] = keep.tile([P, 2 * H], U8, name=f"w1_codes{b}", tag=("pairs0", "pairs1")[b], align_bytes=64)
             (nc.vector, nc.gpsimd)[b].tensor_copy(
                 w1_codes[b][:].bitcast(U16).rearrange("p (a i m) -> p a i m", i=PACK, m=P),
                 w1_raw[b][:].bitcast(U16).rearrange("p (a m i) -> p a i m", i=PACK, m=P),
@@ -167,20 +168,25 @@ def tile_list_courier_eta_banks_kernel(
                 nc.vector.tensor_copy(words[:], tab[:, a * T : (a + 1) * T].bitcast(U32).indirect(entries))
                 v_codes[a, half] = words
 
-        def pieces_of(k):
-            widths = FIRST_PIECES if k == ORDER[0] else (S,)
-            return [slice(sum(widths[:j]), sum(widths[: j + 1])) for j in range(len(widths))]
+        first_pieces = [
+            slice(sum(FIRST_PIECES[:j]), sum(FIRST_PIECES[: j + 1])) for j in range(len(FIRST_PIECES))
+        ]
+        halves_of_list = (slice(0, BANK), slice(BANK, S))
 
-        h = {}
+        h = {k: keep.tile([P, S], F32, name=f"h{k}", tag=f"slot{step}", align_bytes=64) for step, k in enumerate(ORDER)}
+        narrow_banks = []
 
-        def first_product(step):
+        def first_product(step, pieces):
             k = ORDER[step]
             b, i = divmod(k, PACK)
-            h[k] = keep.tile([P, S], F32, name=f"h{k}", tag=f"slot{step}", align_bytes=64)
-            for j, cols in enumerate(pieces_of(k) if step == 0 else (slice(0, BANK), slice(BANK, S))):
+            for cols in pieces:
                 half, start = divmod(cols.start, BANK)
                 count = cols.stop - cols.start
-                bank = banks[(2 * step + half) % FIRST_BANKS] if count == BANK else banks[FIRST_BANKS + j]
+                if count == BANK:
+                    bank = banks[(2 * step + half) % FIRST_BANKS]
+                else:
+                    bank = banks[FIRST_BANKS + len(narrow_banks)]
+                    narrow_banks.append(bank)
                 width = BANK if count == BANK else P
                 order = (1, 0) if count == BANK else (0, 1)
                 for first in range(0, count, width):
@@ -199,18 +205,19 @@ def tile_list_courier_eta_banks_kernel(
                         )
                 nc.scalar.activation(h[k][:, cols], bank[:, :count], RELU, bias=bias[:, k : k + 1])
 
-        def weigh(step):
+        def weigh(step, cols=slice(0, S)):
             k = ORDER[step]
-            for cols in pieces_of(k):
-                nc.gpsimd.tensor_tensor(h[k][:, cols], h[k][:, cols], weights[:, cols], MULT)
+            nc.gpsimd.tensor_tensor(h[k][:, cols], h[k][:, cols], weights[:, cols], MULT)
 
-        for step in range(PACK):
-            first_product(step)
-        weigh(0)
-        weigh(1)
+        for cols in first_pieces:
+            for step in range(FIRST_STEPS):
+                first_product(step, [cols])
+                weigh(step, cols)
+        for step in range(FIRST_STEPS, PACK):
+            first_product(step, halves_of_list)
         deal_codes(1)
         for step in range(PACK, SLICES):
-            first_product(step)
+            first_product(step, halves_of_list)
 
         w2_grouped = keep.tile([P, PASSES * PACK * N], BF16, name="w2_grouped", tag="codes0", align_bytes=64)
         for b in range(PASSES):
@@ -230,12 +237,11 @@ def tile_list_courier_eta_banks_kernel(
 
         page_of = {}
 
-        def put(step):
+        def put(step, cols=slice(0, S)):
             k = ORDER[step]
             page_of[k] = pages[step % PAGES]
-            for cols in pieces_of(k):
-                entries = places[:, cols.start // LIST_ROWS : cols.stop // LIST_ROWS]
-                nc.vector.tensor_copy(page_of[k][:].indirect(entries), h[k][:, cols])
+            entries = places[:, cols.start // LIST_ROWS : cols.stop // LIST_ROWS]
+            nc.vector.tensor_copy(page_of[k][:].indirect(entries), h[k][:, cols])
 
         pairs = [
             keep.tile([P, PACK * T2], BF16, name=f"pairs{b}", tag=f"pairs{b}", align_bytes=64) for b in range(PASSES)
@@ -283,8 +289,10 @@ def tile_list_courier_eta_banks_kernel(
         nc.gpsimd.memset(pages[2][:], 0.0)
         weigh(2)
         weigh(3)
-        for step in range(PAGES):
-            put(step)
+        for cols in first_pieces:
+            for step in range(FIRST_STEPS):
+                put(step, cols)
+        put(2)
         for step in range(2):
             add_road(step)
             load_road(step + PACK)
@@ -372,10 +380,10 @@ def tile_list_courier_eta_banks_kernel(
         z1_plane = keep.tile([P, T2], U8, name="z1_plane", align_bytes=64)
 
         def quantise(b, c, z):
-            if b == 0 and c > 0:
-                codes = relay.tile([P, BANK], U32, name=f"z_codes0_{c}", offset=(c - 1) * Z_BYTES, align_bytes=64)
+            if b == 0 and c >= 2:
+                codes = relay.tile([P, BANK], U32, name=f"z_codes0_{c}", offset=(c - 2) * Z_BYTES, align_bytes=64)
             else:
-                tag = f"slot{PACK + c}" if b else "codes0"
+                tag = f"slot{PACK + c}" if b else ("codes0", "codes2")[c]
                 codes = keep.tile([P, BANK], U32, name=f"z_codes{b}_{c}", tag=tag, align_bytes=64)
             plane = (late_plane, z1_plane)[b][:, c * BANK : (c + 1) * BANK]
             nc.vector.quantize_mx(out=codes[:].bitcast(E4M3), scales=plane, in_=z[:])
@@ -450,8 +458,10 @@ def tile_list_courier_eta_banks_kernel(
 
         def finish(n):
             c, nt = divmod(n, N // P)
-            nc.vector.tensor_tensor(delay[n], delay[n], bank_of[n][:], ADD)
-            nc.sync.dma_start(out[nt * P : (nt + 1) * P, c * BANK : (c + 1) * BANK], delay[n])
+            cuts = (0, BANK - P, BANK) if n == TILES - 1 else (0, BANK)
+            for lo, hi in zip(cuts, cuts[1:]):
+                nc.vector.tensor_tensor(delay[n][:, lo:hi], delay[n][:, lo:hi], bank_of[n][:, lo:hi], ADD)
+                nc.sync.dma_start(out[nt * P : (nt + 1) * P, c * BANK + lo : c * BANK + hi], delay[n][:, lo:hi])
             free_banks.append(bank_of[n])
             if len(bank_of) < TILES:
                 product(len(bank_of))

@@ -43,7 +43,6 @@ ROAD_BANKS = 3
 AHEAD = 2
 Z_BYTES = 2 * PACK * BANK
 JAM_BANKS = 2
-FIRST_WEIGHTS = 512
 
 
 def tile_list_courier_eta_banks_kernel(
@@ -113,10 +112,14 @@ def tile_list_courier_eta_banks_kernel(
             (nc.scalar, nc.sync)[a].dma_start(
                 v_plane[0:100, a * S : (a + 1) * S].bitcast(I32), picked[first : first + 100, :].bitcast(I32)
             )
+        weights = keep.tile([P, S], F32, name="weights")
+        first_pieces = [
+            slice(sum(FIRST_PIECES[:j]), sum(FIRST_PIECES[: j + 1])) for j in range(len(FIRST_PIECES))
+        ]
+        nc.sync.dma_start(weights[:, first_pieces[0]], wgs[:, first_pieces[0]])
         places = lists.tile([P, S // LIST_ROWS], U16, name="places")
         nc.sync.dma_start(places[:], offs2)
-        weights = keep.tile([P, S], F32, name="weights")
-        for cols in (slice(0, FIRST_WEIGHTS), slice(FIRST_WEIGHTS, S)):
+        for cols in first_pieces[1:]:
             nc.sync.dma_start(weights[:, cols], wgs[:, cols])
 
         road_rows = road.rearrange("(b p i) t -> b i p t", b=PASSES, i=PACK)
@@ -164,13 +167,13 @@ def tile_list_courier_eta_banks_kernel(
                 words = keep.tile(
                     [P, BANK], U32, name=f"v_codes{a}{half}", tag=("codes0", "codes4", "codes2", "codes3")[2 * a + half], align_bytes=64
                 )
-                entries = picks[:, half * BANK // LIST_ROWS : (half + 1) * BANK // LIST_ROWS]
-                nc.vector.tensor_copy(words[:], tab[:, a * T : (a + 1) * T].bitcast(U32).indirect(entries))
+                cuts = (0, BANK // 2, BANK) if (a, half) == (1, 0) else (0, BANK)
+                for lo, hi in zip(cuts, cuts[1:]):
+                    entries = picks[:, (half * BANK + lo) // LIST_ROWS : (half * BANK + hi) // LIST_ROWS]
+                    window = tab[:, a * T : (a + 1) * T].bitcast(U32)
+                    nc.vector.tensor_copy(words[:, lo:hi], window.indirect(entries))
                 v_codes[a, half] = words
 
-        first_pieces = [
-            slice(sum(FIRST_PIECES[:j]), sum(FIRST_PIECES[: j + 1])) for j in range(len(FIRST_PIECES))
-        ]
         halves_of_list = (slice(0, BANK), slice(BANK, S))
 
         h = {k: keep.tile([P, S], F32, name=f"h{k}", tag=f"slot{step}", align_bytes=64) for step, k in enumerate(ORDER)}
@@ -324,7 +327,6 @@ def tile_list_courier_eta_banks_kernel(
                     banks[c][:, s * P : (s + 1) * P], words[:, (s % 2) * P : (s % 2 + 1) * P], ident[:]
                 )
             nc.scalar.copy(pairs[0][:].bitcast(F32)[:, T2 + c * BANK : T2 + (c + 1) * BANK], banks[c][:])
-        z0 = [weave(0, c) for c in range(CHUNKS)]
 
         def jam_of(n):
             c, nt = divmod(n, N // P)
@@ -366,6 +368,8 @@ def tile_list_courier_eta_banks_kernel(
             bring_jam(j)
         for c, cols in enumerate(road_cols):
             turn_blocks(road_banks[c], staged_road[c], cols.stop - cols.start)
+
+        z0 = [weave(0, c) for c in range(CHUNKS)]
 
         put(5)
         put(6)

@@ -35,14 +35,14 @@ ORDER = (0, 1, 2, 3, 6, 4, 5, 7)
 LAST = ORDER[-1]
 FIRST_PIECES = (128, 384, 512)
 FIRST_STEPS = 2
+Z_BYTES = 2 * PACK * BANK
+VECTOR_COLUMNS = 1280
+ROAD_BANKS = 3
 TILES = N // P * CHUNKS
 VECTOR_SHARE = 7
 VECTOR_TILES = [n for n in range(TILES) if (TILES - 1 - n) * VECTOR_SHARE % TILES < VECTOR_SHARE]
-VECTOR_COLUMNS = 1280
-ROAD_BANKS = 3
-AHEAD = 2
-Z_BYTES = 2 * PACK * BANK
 JAM_BANKS = 2
+AHEAD = 2
 
 
 def tile_list_courier_eta_banks_kernel(
@@ -64,8 +64,9 @@ def tile_list_courier_eta_banks_kernel(
         v_plane = keep.tile([P, PASSES * S], U8, name="v_plane", align_bytes=64)
         nc.gpsimd.memset(v_plane[96:128, :].bitcast(I32), 0)
         pages = [keep.tile([P, T2], F32, name=f"page{j}", tag=f"page{j}", align_bytes=64) for j in range(2)]
-        for page in pages:
-            nc.gpsimd.memset(page[:], 0.0)
+        nc.gpsimd.memset(pages[0][:], 0.0)
+        for c in range(CHUNKS):
+            nc.gpsimd.memset(pages[1][:, c * BANK : (c + 1) * BANK], 0.0)
         ident = keep.tile([P, P], F32, name="ident", align_bytes=64)
         make_identity(nc, ident[:])
 
@@ -108,9 +109,9 @@ def tile_list_courier_eta_banks_kernel(
         picked = keep.tile([P, S], U8, name="picked", tag="late", align_bytes=64)
         nc.vector.tensor_copy(picked[:], tab_plane[:, :T].indirect(picks[:]))
         for a in range(PASSES):
-            first = 24 + 4 * a
+            row0 = 24 + 4 * a
             (nc.scalar, nc.sync)[a].dma_start(
-                v_plane[0:100, a * S : (a + 1) * S].bitcast(I32), picked[first : first + 100, :].bitcast(I32)
+                v_plane[0:100, a * S : (a + 1) * S].bitcast(I32), picked[row0 : row0 + 100, :].bitcast(I32)
             )
         weights = keep.tile([P, S], F32, name="weights")
         first_pieces = [
@@ -164,9 +165,8 @@ def tile_list_courier_eta_banks_kernel(
         v_codes = {}
         for half in range(2):
             for a in range(PASSES):
-                words = keep.tile(
-                    [P, BANK], U32, name=f"v_codes{a}{half}", tag=("codes0", "codes4", "codes2", "codes3")[2 * a + half], align_bytes=64
-                )
+                tag = ("codes0", "codes4", "codes2", "codes3")[2 * a + half]
+                words = keep.tile([P, BANK], U32, name=f"v_codes{a}{half}", tag=tag, align_bytes=64)
                 cuts = (0, BANK // 2, BANK) if (a, half) == (1, 0) else (0, BANK)
                 for lo, hi in zip(cuts, cuts[1:]):
                     entries = picks[:, (half * BANK + lo) // LIST_ROWS : (half * BANK + hi) // LIST_ROWS]
@@ -176,14 +176,16 @@ def tile_list_courier_eta_banks_kernel(
 
         halves_of_list = (slice(0, BANK), slice(BANK, S))
 
-        h = {k: keep.tile([P, S], F32, name=f"h{k}", tag=f"slot{step}", align_bytes=64) for step, k in enumerate(ORDER)}
+        h = {
+            k: keep.tile([P, S], F32, name=f"h{k}", tag=f"slot{step}", align_bytes=64) for step, k in enumerate(ORDER)
+        }
         narrow_banks = []
 
         def first_product(step, pieces):
             k = ORDER[step]
             b, i = divmod(k, PACK)
             for cols in pieces:
-                half, start = divmod(cols.start, BANK)
+                half, within = divmod(cols.start, BANK)
                 count = cols.stop - cols.start
                 if count == BANK:
                     bank = banks[(2 * step + half) % FIRST_BANKS]
@@ -191,20 +193,20 @@ def tile_list_courier_eta_banks_kernel(
                     bank = banks[FIRST_BANKS + len(narrow_banks)]
                     narrow_banks.append(bank)
                 width = BANK if count == BANK else P
-                order = (1, 0) if count == BANK else (0, 1)
-                for first in range(0, count, width):
-                    for a in order:
+                passes = (1, 0) if count == BANK else (0, 1)
+                for col0 in range(0, count, width):
+                    for a in passes:
                         scale0 = P * (a * PACK + i)
                         code0 = 2 * scale0
-                        entry0 = a * S + cols.start + first
+                        entry0 = a * S + cols.start + col0
                         nc.tensor.matmul_mx(
-                            out=bank[:, first : first + width],
+                            out=bank[:, col0 : col0 + width],
                             lhsT=w1_codes[b][:, code0 : code0 + 2 * P].bitcast(E2M1),
                             lhsT_scale=w1_scale[b][:, scale0 : scale0 + P],
-                            rhs=v_codes[a, half][:, start + first : start + first + width].bitcast(E4M3),
+                            rhs=v_codes[a, half][:, within + col0 : within + col0 + width].bitcast(E4M3),
                             rhs_scale=v_plane[:, entry0 : entry0 + width],
-                            start=(a == order[0]),
-                            stop=(a == order[-1]),
+                            start=(a == passes[0]),
+                            stop=(a == passes[-1]),
                         )
                 nc.scalar.activation(h[k][:, cols], bank[:, :count], RELU, bias=bias[:, k : k + 1])
 
@@ -358,8 +360,8 @@ def tile_list_courier_eta_banks_kernel(
         staged_road = []
         for cols in road_cols:
             width = cols.stop - cols.start
-            first = JAM_BANKS * BANK + cols.start
-            staged_road.append(stage(early[:, first : first + width], roads[LAST][:, cols], width))
+            place0 = JAM_BANKS * BANK + cols.start
+            staged_road.append(stage(early[:, place0 : place0 + width], roads[LAST][:, cols], width))
 
         def bring_jam(j):
             turn_blocks(jam_banks[j % JAM_BANKS], staged[j])
@@ -396,8 +398,8 @@ def tile_list_courier_eta_banks_kernel(
 
         def odd_halves(cols):
             c, t = divmod(cols.start, BANK)
-            first = (PACK * c + 2) * BANK + 2 * t + 1
-            return pairs[1][:, first : first + 2 * (cols.stop - cols.start) - 1 : 2]
+            half0 = (PACK * c + 2) * BANK + 2 * t + 1
+            return pairs[1][:, half0 : half0 + 2 * (cols.stop - cols.start) - 1 : 2]
 
         for c in range(VECTOR_COLUMNS // BANK, CHUNKS):
             cols = slice(max(c * BANK, VECTOR_COLUMNS), (c + 1) * BANK)
@@ -462,10 +464,8 @@ def tile_list_courier_eta_banks_kernel(
 
         def finish(n):
             c, nt = divmod(n, N // P)
-            cuts = (0, BANK - P, BANK) if n == TILES - 1 else (0, BANK)
-            for lo, hi in zip(cuts, cuts[1:]):
-                nc.vector.tensor_tensor(delay[n][:, lo:hi], delay[n][:, lo:hi], bank_of[n][:, lo:hi], ADD)
-                nc.sync.dma_start(out[nt * P : (nt + 1) * P, c * BANK + lo : c * BANK + hi], delay[n][:, lo:hi])
+            nc.vector.tensor_tensor(delay[n], delay[n], bank_of[n][:], ADD)
+            nc.sync.dma_start(out[nt * P : (nt + 1) * P, c * BANK : (c + 1) * BANK], delay[n])
             free_banks.append(bank_of[n])
             if len(bank_of) < TILES:
                 product(len(bank_of))

@@ -57,12 +57,11 @@ def tile_list_courier_eta_banks_kernel(
         banks = [psum.tile([P, BANK], F32, name=f"bank{j}") for j in range(BANKS)]
 
         tab_plane = keep.tile([P, T + 4], U8, name="tab_plane", tag="road0", align_bytes=64)
-        for q in range(4):
-            nc.vector.memset(tab_plane[32 * q : 32 * q + 24, :].bitcast(I32), 0)
+        for rows in (slice(0, 16), slice(32, 48), slice(64, 128)):
+            nc.vector.memset(tab_plane[rows, :].bitcast(I32), 0)
         w1_plane = keep.tile([P, PASSES * H], U8, name="w1_plane", tag="codes1", align_bytes=64)
         nc.gpsimd.memset(w1_plane[:].bitcast(I32), 0)
         v_plane = keep.tile([P, PASSES * S], U8, name="v_plane", align_bytes=64)
-        nc.gpsimd.memset(v_plane[96:128, :].bitcast(I32), 0)
         pages = [keep.tile([P, T2], F32, name=f"page{j}", tag=f"page{j}", align_bytes=64) for j in range(2)]
         nc.gpsimd.memset(pages[0][:], 0.0)
         for c in range(CHUNKS):
@@ -72,11 +71,9 @@ def tile_list_courier_eta_banks_kernel(
 
         picks = lists.tile([P, S // LIST_ROWS], U16, name="picks")
         nc.sync.dma_start(picks[:], offs)
-        for q in range(4):
-            nc.sync.dma_start(
-                tab_plane[32 * q + 24 : 32 * q + 32, :T].bitcast(I32),
-                tab_scales[:, 4 * q : 4 * q + 4, :].bitcast(I32),
-            )
+        scale_rows = tab_scales.bitcast(I32).rearrange("a (u e d) t -> e (a u) d t", u=2, e=2)
+        for e in range(2):
+            nc.sync.dma_start(tab_plane[32 * e + 16 : 32 * e + 32, :T].bitcast(I32), scale_rows[e])
         bias = keep.tile([P, SLICES], F32, name="bias")
         nc.sync.dma_start(
             bias[:].rearrange("p (b i) -> p b i", i=PACK), b1.rearrange("(b p i) -> p b i", b=PASSES, i=PACK)
@@ -91,7 +88,7 @@ def tile_list_courier_eta_banks_kernel(
         w1_raw = {}
 
         def load_w1(b):
-            w1_raw[b] = keep.tile([P, 2 * H], U8, name=f"w1_raw{b}", tag=("page2", "curves1")[b], align_bytes=64)
+            w1_raw[b] = keep.tile([P, 2 * H], U8, name=f"w1_raw{b}", tag=("w2_codes", "curves1")[b], align_bytes=64)
             nc.sync.dma_start(
                 w1_raw[b][:].bitcast(I32).rearrange("p (a c) -> p a c", a=PASSES),
                 w1_words[:, :, b * H : (b + 1) * H].bitcast(I32).rearrange("a p c -> p a c"),
@@ -109,10 +106,12 @@ def tile_list_courier_eta_banks_kernel(
         picked = keep.tile([P, S], U8, name="picked", tag="late", align_bytes=64)
         nc.vector.tensor_copy(picked[:], tab_plane[:, :T].indirect(picks[:]))
         for a in range(PASSES):
-            row0 = 24 + 4 * a
-            (nc.scalar, nc.sync)[a].dma_start(
-                v_plane[0:100, a * S : (a + 1) * S].bitcast(I32), picked[row0 : row0 + 100, :].bitcast(I32)
-            )
+            for u in range(2):
+                row0 = 16 + 8 * a + 4 * u
+                nc.sync.dma_start(
+                    v_plane[64 * u : 64 * u + 64, a * S : (a + 1) * S].bitcast(I32),
+                    picked[row0 : row0 + 64, :].bitcast(I32),
+                )
         weights = keep.tile([P, S], F32, name="weights")
         first_pieces = [
             slice(sum(FIRST_PIECES[:j]), sum(FIRST_PIECES[: j + 1])) for j in range(len(FIRST_PIECES))
@@ -146,7 +145,7 @@ def tile_list_courier_eta_banks_kernel(
 
         def deal_codes(b):
             w1_codes[b] = keep.tile([P, 2 * H], U8, name=f"w1_codes{b}", tag=("pairs0", "pairs1")[b], align_bytes=64)
-            (nc.vector, nc.gpsimd)[b].tensor_copy(
+            nc.scalar.copy(
                 w1_codes[b][:].bitcast(U16).rearrange("p (a i m) -> p a i m", i=PACK, m=P),
                 w1_raw[b][:].bitcast(U16).rearrange("p (a m i) -> p a i m", i=PACK, m=P),
             )
@@ -380,7 +379,7 @@ def tile_list_courier_eta_banks_kernel(
         add_road(5)
         add_road(6)
 
-        w2_codes = keep.tile([P, PASSES * N], U32, name="w2_codes", align_bytes=64)
+        w2_codes = keep.tile([P, PASSES * N], U32, name="w2_codes", tag="w2_codes", align_bytes=64)
         z_codes = {}
         z_plane = {}
         z1_plane = keep.tile([P, T2], U8, name="z1_plane", align_bytes=64)

@@ -42,7 +42,7 @@ TILES = N // P * CHUNKS
 VECTOR_SHARE = 7
 VECTOR_TILES = [n for n in range(TILES) if (TILES - 1 - n) * VECTOR_SHARE % TILES < VECTOR_SHARE]
 JAM_BANKS = 2
-AHEAD = 2
+VECTOR_LAG, GPSIMD_LAG = 1, 3
 
 
 def tile_list_courier_eta_banks_kernel(
@@ -259,9 +259,9 @@ def tile_list_courier_eta_banks_kernel(
                 nc.gpsimd.tensor_tensor(halves, page_of[k][:], roads[k][:], ADD)
             else:
                 nc.gpsimd.tensor_tensor(
-                    pairs[b][:].rearrange("p (c u t e) -> p c u t e", u=2, t=BANK, e=2)[:, :, i // 2, :, i % 2],
-                    page_of[k][:].rearrange("p (c t) -> p c t", t=BANK),
-                    roads[k][:].rearrange("p (c t) -> p c t", t=BANK),
+                    pairs[b][:].rearrange("p (c u t e) -> p c u t e", u=2, t=STRIP, e=2)[:, :, i // 2, :, i % 2],
+                    page_of[k][:].rearrange("p (c t) -> p c t", t=STRIP),
+                    roads[k][:].rearrange("p (c t) -> p c t", t=STRIP),
                     ADD,
                 )
 
@@ -285,7 +285,9 @@ def tile_list_courier_eta_banks_kernel(
             else:
                 z = relay.tile([P, PACK * BANK], BF16, name=f"z1_{c}", offset=c * Z_BYTES, align_bytes=64)
                 chunk = pairs[b][:, c * PACK * BANK : (c + 1) * PACK * BANK]
-                words = chunk.bitcast(F32).rearrange("p (u t) -> p t u", u=2)
+                words = chunk.bitcast(F32).rearrange("p (j u t) -> p j t u", u=2, t=STRIP)
+                nc.scalar.copy(z[:].bitcast(F32).rearrange("p (j t u) -> p j t u", u=2, t=STRIP), words)
+                return z
             nc.scalar.copy(z[:].bitcast(F32).rearrange("p (t u) -> p t u", u=2), words)
             return z
 
@@ -396,25 +398,32 @@ def tile_list_courier_eta_banks_kernel(
             z_plane[b, c] = plane
 
         def odd_halves(cols):
-            c, t = divmod(cols.start, BANK)
-            half0 = (PACK * c + 2) * BANK + 2 * t + 1
-            return pairs[1][:, half0 : half0 + 2 * (cols.stop - cols.start) - 1 : 2]
+            strips = pairs[1][:].rearrange("p (j u t e) -> p j u t e", u=2, t=STRIP, e=2)
+            return strips[:, cols.start // STRIP : cols.stop // STRIP, 1, :, 1]
 
-        for c in range(VECTOR_COLUMNS // BANK, CHUNKS):
-            cols = slice(max(c * BANK, VECTOR_COLUMNS), (c + 1) * BANK)
-            nc.gpsimd.tensor_tensor(odd_halves(cols), page_of[LAST][:, cols], roads[LAST][:, cols], ADD)
+        def by_strip(rows):
+            return rows.rearrange("p (j t) -> p j t", t=STRIP)
+
+        cols = slice(VECTOR_COLUMNS, T2)
+        nc.gpsimd.tensor_tensor(odd_halves(cols), by_strip(page_of[LAST][:, cols]), by_strip(roads[LAST][:, cols]), ADD)
         for c, cols in enumerate(road_cols):
             rows = road_banks[c][:, : cols.stop - cols.start]
-            nc.vector.tensor_tensor(odd_halves(cols), page_of[LAST][:, cols], rows, ADD)
+            nc.vector.tensor_tensor(odd_halves(cols), by_strip(page_of[LAST][:, cols]), by_strip(rows), ADD)
         z1 = [weave(1, c) for c in range(CHUNKS)]
         late_plane = keep.tile(
             [P, T2 + PASSES * N], U8, name="late_plane", tag=f"page{(SLICES - 1) % PAGES}", align_bytes=64
         )
         w2_plane = late_plane[:, T2:]
-        nc.vector.quantize_mx(out=w2_codes[:].bitcast(E4M3), scales=w2_plane, in_=w2_grouped[:])
         for c in range(CHUNKS):
-            quantise(0, c, z0[c])
-            quantise(1, c, z1[c])
+            for b in range(PASSES):
+                if c == 0:
+                    cols = slice(b * N, (b + 1) * N)
+                    nc.vector.quantize_mx(
+                        out=w2_codes[:, cols].bitcast(E4M3),
+                        scales=w2_plane[:, cols],
+                        in_=w2_grouped[:, b * PACK * N : (b + 1) * PACK * N],
+                    )
+                quantise(b, c, (z0, z1)[b][c])
 
         curve_tiles = [
             keep.tile([P, TILES // 2 * BANK], F32, name=f"curves{j}", tag=("pairs0", "curves1")[j], align_bytes=64)
@@ -426,7 +435,8 @@ def tile_list_courier_eta_banks_kernel(
         def product(n):
             c, nt = divmod(n, N // P)
             bank_of[n] = free_banks[n]
-            for b in range(PASSES):
+            passes = (0, 1) if n < 2 else (1, 0)
+            for b in passes:
                 w_cols = slice(b * N + nt * P, b * N + (nt + 1) * P)
                 nc.tensor.matmul_mx(
                     out=bank_of[n][:],
@@ -434,8 +444,8 @@ def tile_list_courier_eta_banks_kernel(
                     lhsT_scale=w2_plane[:, w_cols],
                     rhs=z_codes[b, c][:].bitcast(E4M3),
                     rhs_scale=z_plane[b, c],
-                    start=(b == 0),
-                    stop=(b == PASSES - 1),
+                    start=(b == passes[0]),
+                    stop=(b == passes[-1]),
                 )
             j, place = divmod(n, TILES // 2)
             curve[n] = curve_tiles[j][:, place * BANK : (place + 1) * BANK]
@@ -471,8 +481,10 @@ def tile_list_courier_eta_banks_kernel(
 
         for n in range(len(free_banks)):
             product(n)
-        for n in range(TILES + AHEAD):
+        for n in range(TILES + GPSIMD_LAG):
             if n < TILES:
                 (vector_delay if n in VECTOR_TILES else gpsimd_delay)(n)
-            if n >= AHEAD:
-                finish(n - AHEAD)
+            if n - VECTOR_LAG in VECTOR_TILES:
+                finish(n - VECTOR_LAG)
+            if n >= GPSIMD_LAG and n - GPSIMD_LAG not in VECTOR_TILES:
+                finish(n - GPSIMD_LAG)

@@ -41,6 +41,9 @@ ROAD_BANKS = 3
 TILES = N // P * CHUNKS
 VECTOR_SHARE = 7
 VECTOR_TILES = [n for n in range(TILES) if (TILES - 1 - n) * VECTOR_SHARE % TILES < VECTOR_SHARE]
+LATE_FIRSTS = [(c, 0) for c in range(CHUNKS - 2, CHUNKS)]
+IN_ORDER = [(c, nt) for c in range(CHUNKS) for nt in range(N // P) if (c, nt) not in LATE_FIRSTS]
+TILE_ORDER = IN_ORDER[: N // P] + LATE_FIRSTS + IN_ORDER[N // P :]
 JAM_BANKS = 2
 VECTOR_LAG, GPSIMD_LAG = 1, 3
 
@@ -332,7 +335,7 @@ def tile_list_courier_eta_banks_kernel(
             nc.scalar.copy(pairs[0][:].bitcast(F32)[:, T2 + c * BANK : T2 + (c + 1) * BANK], banks[c][:])
 
         def jam_of(n):
-            c, nt = divmod(n, N // P)
+            c, nt = TILE_ORDER[n]
             return jams[nt // 2][:, nt % 2, c * BANK : (c + 1) * BANK]
 
         def turn_blocks(bank, source, width=BANK):
@@ -414,7 +417,7 @@ def tile_list_courier_eta_banks_kernel(
             [P, T2 + PASSES * N], U8, name="late_plane", tag=f"page{(SLICES - 1) % PAGES}", align_bytes=64
         )
         w2_plane = late_plane[:, T2:]
-        for c in range(CHUNKS):
+        for c in range(2):
             for b in range(PASSES):
                 if c == 0:
                     cols = slice(b * N, (b + 1) * N)
@@ -423,6 +426,9 @@ def tile_list_courier_eta_banks_kernel(
                         scales=w2_plane[:, cols],
                         in_=w2_grouped[:, b * PACK * N : (b + 1) * PACK * N],
                     )
+                quantise(b, c, (z0, z1)[b][c])
+        for b in range(PASSES):
+            for c in range(2, CHUNKS):
                 quantise(b, c, (z0, z1)[b][c])
 
         curve_tiles = [
@@ -433,7 +439,7 @@ def tile_list_courier_eta_banks_kernel(
         bank_of, curve, delay = {}, {}, {}
 
         def product(n):
-            c, nt = divmod(n, N // P)
+            c, nt = TILE_ORDER[n]
             bank_of[n] = free_banks[n]
             passes = (0, 1) if n < 2 else (1, 0)
             for b in passes:
@@ -459,8 +465,8 @@ def tile_list_courier_eta_banks_kernel(
                 bring_jam(j + JAM_BANKS)
 
         held = [
-            keep.tile([P, 2 * BANK], F32, name="held0", tag=f"slot{CHUNKS - 1}", align_bytes=64),
-            relay.tile([P, 2 * BANK], F32, name="held1", offset=(CHUNKS - 1) * Z_BYTES, align_bytes=64),
+            relay.tile([P, 2 * BANK], F32, name=f"held{c}", offset=c * Z_BYTES, align_bytes=64)
+            for c in range(CHUNKS - 2, CHUNKS)
         ]
         early_tiles = [n for n in range(len(free_banks)) if n not in VECTOR_TILES]
 
@@ -472,7 +478,7 @@ def tile_list_courier_eta_banks_kernel(
             nc.gpsimd.tensor_tensor(delay[n], curve[n], jam_of(n), MULT)
 
         def finish(n):
-            c, nt = divmod(n, N // P)
+            c, nt = TILE_ORDER[n]
             nc.vector.tensor_tensor(delay[n], delay[n], bank_of[n][:], ADD)
             nc.sync.dma_start(out[nt * P : (nt + 1) * P, c * BANK : (c + 1) * BANK], delay[n])
             free_banks.append(bank_of[n])

@@ -466,7 +466,7 @@ def tile_list_courier_eta_banks_kernel(
 
         held = [
             relay.tile([P, 2 * BANK], F32, name=f"held{c}", offset=c * Z_BYTES, align_bytes=64)
-            for c in range(CHUNKS - 2, CHUNKS)
+            for c in (CHUNKS - 1, CHUNKS - 2)
         ]
         early_tiles = [n for n in range(len(free_banks)) if n not in VECTOR_TILES]
 

@@ -46,6 +46,19 @@ IN_ORDER = [(c, nt) for c in range(CHUNKS) for nt in range(N // P) if (c, nt) no
 TILE_ORDER = IN_ORDER[: N // P] + LATE_FIRSTS + IN_ORDER[N // P :]
 JAM_BANKS = 2
 VECTOR_LAG, GPSIMD_LAG = 1, 3
+REGIONS = (
+    [(f"road{j}", 4 * T2) for j in range(PACK)]
+    + [(f"wide{j}", 8 * T2) for j in range(2)]
+    + [(f"page{j}", 4 * T2) for j in range(PAGES)]
+    + [(f"pairs{j}", 8 * T2) for j in range(PASSES)]
+    + [(f"slot{j}", 4 * S) for j in range(SLICES)]
+    + [("relay", CHUNKS * Z_BYTES), ("curves1", 8 * T2), ("codes0", 2 * PASSES * PACK * N)]
+    + [(f"codes{j}", 4 * BANK) for j in range(1, 5)]
+    + [("w2_codes", 4 * PASSES * N), ("v_plane", PASSES * S), ("picked", S), ("weights", 4 * S)]
+    + [("ident", 4 * P), ("bias", 64), ("w1_scale1", H), ("turned", 4 * T2), ("z1_plane", T2)]
+    + [("staged", 4 * BANK * (VECTOR_SHARE - JAM_BANKS))]
+)
+START = {name: sum(size for other, size in REGIONS[:j]) for j, (name, own) in enumerate(REGIONS)}
 
 
 def tile_list_courier_eta_banks_kernel(
@@ -54,22 +67,25 @@ def tile_list_courier_eta_banks_kernel(
     nc = tc.nc
     with ExitStack() as ctx:
         lists = ctx.enter_context(tc.tile_pool(name="lists", bufs=1))
-        keep = ctx.enter_context(tc.tile_pool(name="keep", bufs=1))
-        relay = ctx.enter_context(tc.tile_pool(name="relay", bufs=1))
+        arena = ctx.enter_context(tc.tile_pool(name="arena", bufs=1))
         psum = ctx.enter_context(tc.psum_pool(name="psum", bufs=1))
         banks = [psum.tile([P, BANK], F32, name=f"bank{j}") for j in range(BANKS)]
 
-        tab_plane = keep.tile([P, T + 4], U8, name="tab_plane", tag="road0", align_bytes=64)
+        def place(name, columns, dtype, region, byte0=0):
+            return arena.tile([P, columns], dtype, name=name, offset=START[region] + byte0, align_bytes=64)
+
+        tab_plane = place("tab_plane", T + 4, U8, "road0")
         for rows in (slice(0, 16), slice(32, 48), slice(64, 128)):
             nc.vector.memset(tab_plane[rows, :].bitcast(I32), 0)
-        w1_plane = keep.tile([P, PASSES * H], U8, name="w1_plane", tag="codes1", align_bytes=64)
-        nc.gpsimd.memset(w1_plane[:].bitcast(I32), 0)
-        v_plane = keep.tile([P, PASSES * S], U8, name="v_plane", align_bytes=64)
-        pages = [keep.tile([P, T2], F32, name=f"page{j}", tag=f"page{j}", align_bytes=64) for j in range(2)]
+        w1_planes = [place(f"w1_plane{b}", H, U8, "codes1", b * H) for b in range(PASSES)]
+        for b in range(PASSES):
+            nc.gpsimd.memset(w1_planes[b][:].bitcast(I32), 0)
+        v_plane = place("v_plane", PASSES * S, U8, "v_plane")
+        pages = [place(f"page{j}", T2, F32, f"page{j}") for j in range(2)]
         nc.gpsimd.memset(pages[0][:], 0.0)
         for c in range(CHUNKS):
             nc.gpsimd.memset(pages[1][:, c * BANK : (c + 1) * BANK], 0.0)
-        ident = keep.tile([P, P], F32, name="ident", align_bytes=64)
+        ident = place("ident", P, F32, "ident")
         make_identity(nc, ident[:])
 
         picks = lists.tile([P, S // LIST_ROWS], U16, name="picks")
@@ -77,36 +93,34 @@ def tile_list_courier_eta_banks_kernel(
         scale_rows = tab_scales.bitcast(I32).rearrange("a (u e d) t -> e (a u) d t", u=2, e=2)
         for e in range(2):
             nc.sync.dma_start(tab_plane[32 * e + 16 : 32 * e + 32, :T].bitcast(I32), scale_rows[e])
-        bias = keep.tile([P, SLICES], F32, name="bias")
-        nc.sync.dma_start(
-            bias[:].rearrange("p (b i) -> p b i", i=PACK), b1.rearrange("(b p i) -> p b i", b=PASSES, i=PACK)
-        )
-        tab = keep.tile([P, PASSES * T], I32, name="tab", tag="wide0", align_bytes=64)
+        tab = [place(f"tab{a}", T, I32, "wide0", 4 * T * a) for a in range(PASSES)]
 
         def load_table(a):
-            nc.sync.dma_start(
-                tab[:, a * T : (a + 1) * T], tab_words[a].rearrange("p t i -> p (t i)").bitcast(I32)
-            )
+            nc.sync.dma_start(tab[a][:], tab_words[a].rearrange("p t i -> p (t i)").bitcast(I32))
 
         w1_raw = {}
 
         def load_w1(b):
-            w1_raw[b] = keep.tile([P, 2 * H], U8, name=f"w1_raw{b}", tag=("w2_codes", "curves1")[b], align_bytes=64)
+            w1_raw[b] = place(f"w1_raw{b}", 2 * H, U8, ("w2_codes", "curves1")[b])
             nc.sync.dma_start(
                 w1_raw[b][:].bitcast(I32).rearrange("p (a c) -> p a c", a=PASSES),
                 w1_words[:, :, b * H : (b + 1) * H].bitcast(I32).rearrange("a p c -> p a c"),
             )
 
+        w1_rows = w1_scales.bitcast(I32).rearrange("a (q d) (b c) -> b d q a c", d=4, b=PASSES)
+
+        def load_w1_scales(b):
+            for d in range(4):
+                nc.sync.dma_start(
+                    w1_planes[b][d:P:32, :].bitcast(I32).rearrange("q (a c) -> q a c", a=PASSES), w1_rows[b, d]
+                )
+
         load_w1(0)
         load_table(0)
-        for q in range(4):
-            nc.sync.dma_start(
-                w1_plane[32 * q : 32 * q + 4, :].bitcast(I32).rearrange("r (a c) -> r a c", a=PASSES),
-                w1_scales[:, 4 * q : 4 * q + 4, :].bitcast(I32).rearrange("a r c -> r a c"),
-            )
+        load_w1_scales(0)
         load_table(1)
 
-        picked = keep.tile([P, S], U8, name="picked", tag="late", align_bytes=64)
+        picked = place("picked", S, U8, "picked")
         nc.vector.tensor_copy(picked[:], tab_plane[:, :T].indirect(picks[:]))
         for a in range(PASSES):
             for u in range(2):
@@ -115,7 +129,11 @@ def tile_list_courier_eta_banks_kernel(
                     v_plane[64 * u : 64 * u + 64, a * S : (a + 1) * S].bitcast(I32),
                     picked[row0 : row0 + 64, :].bitcast(I32),
                 )
-        weights = keep.tile([P, S], F32, name="weights")
+        bias = place("bias", SLICES, F32, "bias")
+        nc.sync.dma_start(
+            bias[:].rearrange("p (b i) -> p b i", i=PACK), b1.rearrange("(b p i) -> p b i", b=PASSES, i=PACK)
+        )
+        weights = place("weights", S, F32, "weights")
         first_pieces = [
             slice(sum(FIRST_PIECES[:j]), sum(FIRST_PIECES[: j + 1])) for j in range(len(FIRST_PIECES))
         ]
@@ -130,13 +148,14 @@ def tile_list_courier_eta_banks_kernel(
 
         def load_road(step):
             k = ORDER[step]
-            roads[k] = keep.tile([P, T2], F32, name=f"road{k}", tag=f"road{step % PACK}", align_bytes=64)
+            roads[k] = place(f"road{k}", T2, F32, f"road{step % PACK}")
             nc.sync.dma_start(roads[k][:], road_rows[k // PACK, k % PACK])
 
+        load_w1_scales(1)
         load_road(0)
         load_w1(1)
         load_road(1)
-        w2_raw = keep.tile([P, PASSES * PACK * N], F32, name="w2_raw", tag="wide1", align_bytes=64)
+        w2_raw = place("w2_raw", PASSES * PACK * N, F32, "wide1")
         nc.sync.dma_start(
             w2_raw[:].rearrange("p (b c) -> p b c", b=PASSES),
             w2.rearrange("(b p i) n -> p b (i n)", b=PASSES, i=PACK),
@@ -146,46 +165,55 @@ def tile_list_courier_eta_banks_kernel(
 
         w1_codes, w1_scale = {}, {}
 
-        def deal_codes(b):
-            w1_codes[b] = keep.tile([P, 2 * H], U8, name=f"w1_codes{b}", tag=("pairs0", "pairs1")[b], align_bytes=64)
+        def deal_codes(k0, count):
+            b, i0 = divmod(k0, PACK)
+            codes = place(f"w1_codes{k0}", 2 * PASSES * count * P, U8, f"pairs{b}", 2 * PASSES * i0 * P)
             nc.scalar.copy(
-                w1_codes[b][:].bitcast(U16).rearrange("p (a i m) -> p a i m", i=PACK, m=P),
-                w1_raw[b][:].bitcast(U16).rearrange("p (a m i) -> p a i m", i=PACK, m=P),
+                codes[:].bitcast(U16).rearrange("p (a i m) -> p a i m", i=count, m=P),
+                w1_raw[b][:].bitcast(U16).rearrange("p (a m i) -> p a i m", i=PACK, m=P)[:, :, i0 : i0 + count, :],
             )
+            for i in range(count):
+                for a in range(PASSES):
+                    code0 = 2 * P * (a * count + i)
+                    w1_codes[k0 + i, a] = codes[:, code0 : code0 + 2 * P]
 
-        def deal_scales(b):
-            w1_scale[b] = keep.tile([P, H], U8, name=f"w1_scale{b}", tag=("page2", "w1_scale1")[b], align_bytes=64)
+        def deal_scales(k0, count):
+            b, i0 = divmod(k0, PACK)
+            scales = place(f"w1_scale{k0}", PASSES * count * P, U8, "page2" if i0 else "w1_scale1")
             nc.gpsimd.tensor_copy(
-                w1_scale[b][:].rearrange("p (a i m) -> p a i m", i=PACK, m=P),
-                w1_plane[:].rearrange("p (a b m i) -> p b a i m", a=PASSES, i=PACK, m=P)[:, b],
+                scales[:].rearrange("p (a i m) -> p a i m", i=count, m=P),
+                w1_planes[b][:].rearrange("p (a m i) -> p a i m", i=PACK, m=P)[:, :, i0 : i0 + count, :],
             )
+            for i in range(count):
+                for a in range(PASSES):
+                    scale0 = P * (a * count + i)
+                    w1_scale[k0 + i, a] = scales[:, scale0 : scale0 + P]
 
-        deal_codes(0)
-        deal_scales(0)
-        deal_scales(1)
+        for k0 in range(0, PACK, FIRST_STEPS):
+            deal_codes(k0, FIRST_STEPS)
+            deal_scales(k0, FIRST_STEPS)
 
         v_codes = {}
         for half in range(2):
             for a in range(PASSES):
                 tag = ("codes0", "codes4", "codes2", "codes3")[2 * a + half]
-                words = keep.tile([P, BANK], U32, name=f"v_codes{a}{half}", tag=tag, align_bytes=64)
-                cuts = (0, BANK // 2, BANK) if (a, half) == (1, 0) else (0, BANK)
+                words = place(f"v_codes{a}{half}", BANK, U32, tag)
+                cuts = (0, FIRST_PIECES[0], BANK) if (a, half) == (1, 0) else (0, BANK)
                 for lo, hi in zip(cuts, cuts[1:]):
                     entries = picks[:, (half * BANK + lo) // LIST_ROWS : (half * BANK + hi) // LIST_ROWS]
-                    window = tab[:, a * T : (a + 1) * T].bitcast(U32)
+                    window = tab[a][:].bitcast(U32)
                     nc.vector.tensor_copy(words[:, lo:hi], window.indirect(entries))
                 v_codes[a, half] = words
 
         halves_of_list = (slice(0, BANK), slice(BANK, S))
 
         h = {
-            k: keep.tile([P, S], F32, name=f"h{k}", tag=f"slot{step}", align_bytes=64) for step, k in enumerate(ORDER)
+            k: place(f"h{k}", S, F32, f"slot{step}") for step, k in enumerate(ORDER)
         }
         narrow_banks = []
 
         def first_product(step, pieces):
             k = ORDER[step]
-            b, i = divmod(k, PACK)
             for cols in pieces:
                 half, within = divmod(cols.start, BANK)
                 count = cols.stop - cols.start
@@ -198,13 +226,11 @@ def tile_list_courier_eta_banks_kernel(
                 passes = (1, 0) if count == BANK else (0, 1)
                 for col0 in range(0, count, width):
                     for a in passes:
-                        scale0 = P * (a * PACK + i)
-                        code0 = 2 * scale0
                         entry0 = a * S + cols.start + col0
                         nc.tensor.matmul_mx(
                             out=bank[:, col0 : col0 + width],
-                            lhsT=w1_codes[b][:, code0 : code0 + 2 * P].bitcast(E2M1),
-                            lhsT_scale=w1_scale[b][:, scale0 : scale0 + P],
+                            lhsT=w1_codes[k, a].bitcast(E2M1),
+                            lhsT_scale=w1_scale[k, a],
                             rhs=v_codes[a, half][:, within + col0 : within + col0 + width].bitcast(E4M3),
                             rhs_scale=v_plane[:, entry0 : entry0 + width],
                             start=(a == passes[0]),
@@ -222,11 +248,12 @@ def tile_list_courier_eta_banks_kernel(
                 weigh(step, cols)
         for step in range(FIRST_STEPS, PACK):
             first_product(step, halves_of_list)
-        deal_codes(1)
+        deal_codes(PACK, PACK)
+        deal_scales(PACK, PACK)
         for step in range(PACK, SLICES):
             first_product(step, halves_of_list)
 
-        w2_grouped = keep.tile([P, PASSES * PACK * N], BF16, name="w2_grouped", tag="codes0", align_bytes=64)
+        w2_grouped = place("w2_grouped", PASSES * PACK * N, BF16, "codes0")
         for b in range(PASSES):
             cols = slice(b * PACK * N, (b + 1) * PACK * N)
             nc.scalar.copy(
@@ -235,7 +262,7 @@ def tile_list_courier_eta_banks_kernel(
             )
         jams = []
         for u in range(2):
-            rows = keep.tile([P, 2 * T2], F32, name=f"jam{u}", tag=f"wide{u}", align_bytes=64)
+            rows = place(f"jam{u}", 2 * T2, F32, f"wide{u}")
             nc.sync.dma_start(
                 rows[:].rearrange("p (e t) -> p e t", e=2),
                 jam[2 * u * P : 2 * (u + 1) * P, :].rearrange("(e p) t -> p e t", e=2),
@@ -251,7 +278,7 @@ def tile_list_courier_eta_banks_kernel(
             nc.vector.tensor_copy(page_of[k][:].indirect(entries), h[k][:, cols])
 
         pairs = [
-            keep.tile([P, PACK * T2], BF16, name=f"pairs{b}", tag=f"pairs{b}", align_bytes=64) for b in range(PASSES)
+            place(f"pairs{b}", PACK * T2, BF16, f"pairs{b}") for b in range(PASSES)
         ]
 
         def add_road(step):
@@ -283,10 +310,10 @@ def tile_list_courier_eta_banks_kernel(
 
         def weave(b, c):
             if b == 0:
-                z = keep.tile([P, PACK * BANK], BF16, name=f"z0_{c}", tag=f"slot{c}", align_bytes=64)
+                z = place(f"z0_{c}", PACK * BANK, BF16, f"slot{c}")
                 words = pairs[b][:].bitcast(F32).rearrange("p (u t) -> p t u", u=2)[:, c * BANK : (c + 1) * BANK, :]
             else:
-                z = relay.tile([P, PACK * BANK], BF16, name=f"z1_{c}", offset=c * Z_BYTES, align_bytes=64)
+                z = place(f"z1_{c}", PACK * BANK, BF16, "relay", c * Z_BYTES)
                 chunk = pairs[b][:, c * PACK * BANK : (c + 1) * PACK * BANK]
                 words = chunk.bitcast(F32).rearrange("p (j u t) -> p j t u", u=2, t=STRIP)
                 nc.scalar.copy(z[:].bitcast(F32).rearrange("p (j t u) -> p j t u", u=2, t=STRIP), words)
@@ -294,7 +321,7 @@ def tile_list_courier_eta_banks_kernel(
             nc.scalar.copy(z[:].bitcast(F32).rearrange("p (t u) -> p t u", u=2), words)
             return z
 
-        pages.append(keep.tile([P, T2], F32, name="page2", tag="page2", align_bytes=64))
+        pages.append(place("page2", T2, F32, "page2"))
         nc.gpsimd.memset(pages[2][:], 0.0)
         weigh(2)
         weigh(3)
@@ -320,7 +347,7 @@ def tile_list_courier_eta_banks_kernel(
         turned = []
         for j in range(STRIPS):
             turn(j, page_of[3], 1, stop=True)
-            strip = keep.tile([P, 2 * STRIP], BF16, name=f"turned{j}", align_bytes=64)
+            strip = place(f"turned{j}", 2 * STRIP, BF16, "turned", 4 * STRIP * j)
             nc.scalar.copy(
                 strip[:].rearrange("t (s p e) -> t s p e", s=2, e=2),
                 banks[j][:].rearrange("t (s e p) -> t s p e", s=2, e=2),
@@ -357,8 +384,8 @@ def tile_list_courier_eta_banks_kernel(
 
         staged = {}
         for j in range(JAM_BANKS, VECTOR_SHARE):
-            staged[j] = stage(keep.tile([P, BANK], F32, name=f"staged{j}")[:], jam_of(VECTOR_TILES[j]))
-        early = relay.tile([P, CHUNKS * Z_BYTES // 4], F32, name="early", offset=0, align_bytes=64)
+            staged[j] = stage(place(f"staged{j}", BANK, F32, "staged", 4 * BANK * (j - JAM_BANKS))[:], jam_of(VECTOR_TILES[j]))
+        early = place("early", CHUNKS * Z_BYTES // 4, F32, "relay", 0)
         for j in range(JAM_BANKS):
             staged[j] = stage(early[:, j * BANK : (j + 1) * BANK], jam_of(VECTOR_TILES[j]))
         staged_road = []
@@ -384,17 +411,17 @@ def tile_list_courier_eta_banks_kernel(
         add_road(5)
         add_road(6)
 
-        w2_codes = keep.tile([P, PASSES * N], U32, name="w2_codes", tag="w2_codes", align_bytes=64)
+        w2_codes = place("w2_codes", PASSES * N, U32, "w2_codes")
         z_codes = {}
         z_plane = {}
-        z1_plane = keep.tile([P, T2], U8, name="z1_plane", align_bytes=64)
+        z1_plane = place("z1_plane", T2, U8, "z1_plane")
 
         def quantise(b, c, z):
             if b == 0 and c >= 2:
-                codes = relay.tile([P, BANK], U32, name=f"z_codes0_{c}", offset=(c - 2) * Z_BYTES, align_bytes=64)
+                codes = place(f"z_codes0_{c}", BANK, U32, "relay", (c - 2) * Z_BYTES)
             else:
                 tag = f"slot{PACK + c}" if b else ("codes0", "codes2")[c]
-                codes = keep.tile([P, BANK], U32, name=f"z_codes{b}_{c}", tag=tag, align_bytes=64)
+                codes = place(f"z_codes{b}_{c}", BANK, U32, tag)
             plane = (late_plane, z1_plane)[b][:, c * BANK : (c + 1) * BANK]
             nc.vector.quantize_mx(out=codes[:].bitcast(E4M3), scales=plane, in_=z[:])
             z_codes[b, c] = codes
@@ -413,9 +440,7 @@ def tile_list_courier_eta_banks_kernel(
             rows = road_banks[c][:, : cols.stop - cols.start]
             nc.vector.tensor_tensor(odd_halves(cols), by_strip(page_of[LAST][:, cols]), by_strip(rows), ADD)
         z1 = [weave(1, c) for c in range(CHUNKS)]
-        late_plane = keep.tile(
-            [P, T2 + PASSES * N], U8, name="late_plane", tag=f"page{(SLICES - 1) % PAGES}", align_bytes=64
-        )
+        late_plane = place("late_plane", T2 + PASSES * N, U8, f"page{(SLICES - 1) % PAGES}")
         w2_plane = late_plane[:, T2:]
         for c in range(2):
             for b in range(PASSES):
@@ -432,7 +457,7 @@ def tile_list_courier_eta_banks_kernel(
                 quantise(b, c, (z0, z1)[b][c])
 
         curve_tiles = [
-            keep.tile([P, TILES // 2 * BANK], F32, name=f"curves{j}", tag=("pairs0", "curves1")[j], align_bytes=64)
+            place(f"curves{j}", TILES // 2 * BANK, F32, ("pairs0", "curves1")[j])
             for j in range(2)
         ]
         free_banks = banks[:first_free] + road_banks
@@ -465,7 +490,7 @@ def tile_list_courier_eta_banks_kernel(
                 bring_jam(j + JAM_BANKS)
 
         held = [
-            relay.tile([P, 2 * BANK], F32, name=f"held{c}", offset=c * Z_BYTES, align_bytes=64)
+            place(f"held{c}", 2 * BANK, F32, "relay", c * Z_BYTES)
             for c in (CHUNKS - 1, CHUNKS - 2)
         ]
         early_tiles = [n for n in range(len(free_banks)) if n not in VECTOR_TILES]

@@ -77,9 +77,8 @@ def tile_list_courier_eta_banks_kernel(
         tab_plane = place("tab_plane", T + 4, U8, "road0")
         for rows in (slice(0, 16), slice(32, 48), slice(64, 128)):
             nc.vector.memset(tab_plane[rows, :].bitcast(I32), 0)
-        w1_planes = [place(f"w1_plane{b}", H, U8, "codes1", b * H) for b in range(PASSES)]
-        for b in range(PASSES):
-            nc.gpsimd.memset(w1_planes[b][:].bitcast(I32), 0)
+        w1_plane = place("w1_plane", PASSES * H, U8, "codes1")
+        nc.gpsimd.memset(w1_plane[:].bitcast(I32), 0)
         v_plane = place("v_plane", PASSES * S, U8, "v_plane")
         pages = [place(f"page{j}", T2, F32, f"page{j}") for j in range(2)]
         nc.gpsimd.memset(pages[0][:], 0.0)
@@ -93,6 +92,10 @@ def tile_list_courier_eta_banks_kernel(
         scale_rows = tab_scales.bitcast(I32).rearrange("a (u e d) t -> e (a u) d t", u=2, e=2)
         for e in range(2):
             nc.sync.dma_start(tab_plane[32 * e + 16 : 32 * e + 32, :T].bitcast(I32), scale_rows[e])
+        bias = place("bias", SLICES, F32, "bias")
+        nc.sync.dma_start(
+            bias[:].rearrange("p (b i) -> p b i", i=PACK), b1.rearrange("(b p i) -> p b i", b=PASSES, i=PACK)
+        )
         tab = [place(f"tab{a}", T, I32, "wide0", 4 * T * a) for a in range(PASSES)]
 
         def load_table(a):
@@ -107,32 +110,29 @@ def tile_list_courier_eta_banks_kernel(
                 w1_words[:, :, b * H : (b + 1) * H].bitcast(I32).rearrange("a p c -> p a c"),
             )
 
-        w1_rows = w1_scales.bitcast(I32).rearrange("a (q d) (b c) -> b d q a c", d=4, b=PASSES)
-
-        def load_w1_scales(b):
-            for d in range(4):
-                nc.sync.dma_start(
-                    w1_planes[b][d:P:32, :].bitcast(I32).rearrange("q (a c) -> q a c", a=PASSES), w1_rows[b, d]
-                )
-
         load_w1(0)
         load_table(0)
-        load_w1_scales(0)
+        for q in range(4):
+            nc.sync.dma_start(
+                w1_plane[32 * q : 32 * q + 4, :].bitcast(I32).rearrange("r (a c) -> r a c", a=PASSES),
+                w1_scales[:, 4 * q : 4 * q + 4, :].bitcast(I32).rearrange("a r c -> r a c"),
+            )
         load_table(1)
 
         picked = place("picked", S, U8, "picked")
         nc.vector.tensor_copy(picked[:], tab_plane[:, :T].indirect(picks[:]))
-        for a in range(PASSES):
-            for u in range(2):
-                row0 = 16 + 8 * a + 4 * u
-                nc.sync.dma_start(
-                    v_plane[64 * u : 64 * u + 64, a * S : (a + 1) * S].bitcast(I32),
-                    picked[row0 : row0 + 64, :].bitcast(I32),
-                )
-        bias = place("bias", SLICES, F32, "bias")
-        nc.sync.dma_start(
-            bias[:].rearrange("p (b i) -> p b i", i=PACK), b1.rearrange("(b p i) -> p b i", b=PASSES, i=PACK)
-        )
+
+        def shift_scales(half):
+            for a in range(PASSES):
+                for u in range(2):
+                    row0 = 16 + 8 * a + 4 * u
+                    entry0 = a * S + half * BANK
+                    nc.sync.dma_start(
+                        v_plane[64 * u : 64 * u + 64, entry0 : entry0 + BANK].bitcast(I32),
+                        picked[row0 : row0 + 64, half * BANK : (half + 1) * BANK].bitcast(I32),
+                    )
+
+        shift_scales(0)
         weights = place("weights", S, F32, "weights")
         first_pieces = [
             slice(sum(FIRST_PIECES[:j]), sum(FIRST_PIECES[: j + 1])) for j in range(len(FIRST_PIECES))
@@ -140,8 +140,9 @@ def tile_list_courier_eta_banks_kernel(
         nc.sync.dma_start(weights[:, first_pieces[0]], wgs[:, first_pieces[0]])
         places = lists.tile([P, S // LIST_ROWS], U16, name="places")
         nc.sync.dma_start(places[:], offs2)
-        for cols in first_pieces[1:]:
-            nc.sync.dma_start(weights[:, cols], wgs[:, cols])
+        nc.sync.dma_start(weights[:, first_pieces[1]], wgs[:, first_pieces[1]])
+        shift_scales(1)
+        nc.sync.dma_start(weights[:, first_pieces[2]], wgs[:, first_pieces[2]])
 
         road_rows = road.rearrange("(b p i) t -> b i p t", b=PASSES, i=PACK)
         roads = {}
@@ -151,7 +152,6 @@ def tile_list_courier_eta_banks_kernel(
             roads[k] = place(f"road{k}", T2, F32, f"road{step % PACK}")
             nc.sync.dma_start(roads[k][:], road_rows[k // PACK, k % PACK])
 
-        load_w1_scales(1)
         load_road(0)
         load_w1(1)
         load_road(1)
@@ -179,26 +179,26 @@ def tile_list_courier_eta_banks_kernel(
 
         def deal_scales(k0, count):
             b, i0 = divmod(k0, PACK)
-            scales = place(f"w1_scale{k0}", PASSES * count * P, U8, "page2" if i0 else "w1_scale1")
+            scales = place(f"w1_scale{k0}", PASSES * count * P, U8, ("page2", "w1_scale1")[b])
             nc.gpsimd.tensor_copy(
                 scales[:].rearrange("p (a i m) -> p a i m", i=count, m=P),
-                w1_planes[b][:].rearrange("p (a m i) -> p a i m", i=PACK, m=P)[:, :, i0 : i0 + count, :],
+                w1_plane[:].rearrange("p (a b m i) -> p b a i m", a=PASSES, i=PACK, m=P)[:, b, :, i0 : i0 + count, :],
             )
             for i in range(count):
                 for a in range(PASSES):
                     scale0 = P * (a * count + i)
                     w1_scale[k0 + i, a] = scales[:, scale0 : scale0 + P]
 
-        for k0 in range(0, PACK, FIRST_STEPS):
-            deal_codes(k0, FIRST_STEPS)
-            deal_scales(k0, FIRST_STEPS)
+        deal_codes(0, PACK)
+        deal_scales(0, PACK)
+        deal_scales(PACK, PACK)
 
         v_codes = {}
         for half in range(2):
             for a in range(PASSES):
                 tag = ("codes0", "codes4", "codes2", "codes3")[2 * a + half]
                 words = place(f"v_codes{a}{half}", BANK, U32, tag)
-                cuts = (0, FIRST_PIECES[0], BANK) if (a, half) == (1, 0) else (0, BANK)
+                cuts = (0, BANK // 2, BANK) if (a, half) == (1, 0) else (0, BANK)
                 for lo, hi in zip(cuts, cuts[1:]):
                     entries = picks[:, (half * BANK + lo) // LIST_ROWS : (half * BANK + hi) // LIST_ROWS]
                     window = tab[a][:].bitcast(U32)
@@ -249,7 +249,6 @@ def tile_list_courier_eta_banks_kernel(
         for step in range(FIRST_STEPS, PACK):
             first_product(step, halves_of_list)
         deal_codes(PACK, PACK)
-        deal_scales(PACK, PACK)
         for step in range(PACK, SLICES):
             first_product(step, halves_of_list)
 

@@ -36,16 +36,16 @@ LAST = ORDER[-1]
 FIRST_PIECES = (128, 384, 512)
 FIRST_STEPS = 2
 Z_BYTES = 2 * PACK * BANK
-VECTOR_COLUMNS = 1280
-ROAD_BANKS = 3
+VECTOR_COLUMNS = 896
+ROAD_BANKS = 2
+TURN_FROM = T2 - BANK
 TILES = N // P * CHUNKS
-VECTOR_SHARE = 7
-VECTOR_TILES = [n for n in range(TILES) if (TILES - 1 - n) * VECTOR_SHARE % TILES < VECTOR_SHARE]
+VECTOR_TILES = [n for n in range(TILES) if n % 3 == 1 or n in (0, TILES - 1)]
+VECTOR_SHARE = len(VECTOR_TILES)
 LATE_FIRSTS = [(c, 0) for c in range(CHUNKS - 2, CHUNKS)]
 IN_ORDER = [(c, nt) for c in range(CHUNKS) for nt in range(N // P) if (c, nt) not in LATE_FIRSTS]
 TILE_ORDER = IN_ORDER[: N // P] + LATE_FIRSTS + IN_ORDER[N // P :]
 JAM_BANKS = 2
-VECTOR_LAG, GPSIMD_LAG = 1, 3
 REGIONS = (
     [(f"road{j}", 4 * T2) for j in range(PACK)]
     + [(f"wide{j}", 8 * T2) for j in range(2)]
@@ -55,7 +55,7 @@ REGIONS = (
     + [("relay", CHUNKS * Z_BYTES), ("curves1", 8 * T2), ("codes0", 2 * PASSES * PACK * N)]
     + [(f"codes{j}", 4 * BANK) for j in range(1, 5)]
     + [("w2_codes", 4 * PASSES * N), ("v_plane", PASSES * S), ("picked", S), ("weights", 4 * S)]
-    + [("ident", 4 * P), ("bias", 64), ("w1_scale1", H), ("turned", 4 * T2), ("z1_plane", T2)]
+    + [("ident", 4 * P), ("bias", 64), ("w1_scale1", H), ("turned", 4 * T2)]
     + [("staged", 4 * BANK * (VECTOR_SHARE - JAM_BANKS))]
 )
 START = {name: sum(size for other, size in REGIONS[:j]) for j, (name, own) in enumerate(REGIONS)}
@@ -122,17 +122,13 @@ def tile_list_courier_eta_banks_kernel(
         picked = place("picked", S, U8, "picked")
         nc.vector.tensor_copy(picked[:], tab_plane[:, :T].indirect(picks[:]))
 
-        def shift_scales(half):
-            for a in range(PASSES):
-                for u in range(2):
-                    row0 = 16 + 8 * a + 4 * u
-                    entry0 = a * S + half * BANK
-                    nc.sync.dma_start(
-                        v_plane[64 * u : 64 * u + 64, entry0 : entry0 + BANK].bitcast(I32),
-                        picked[row0 : row0 + 64, half * BANK : (half + 1) * BANK].bitcast(I32),
-                    )
-
-        shift_scales(0)
+        for a in range(PASSES):
+            for u in range(2):
+                row0 = 16 + 8 * a + 4 * u
+                nc.sync.dma_start(
+                    v_plane[64 * u : 64 * u + 64, a * S : (a + 1) * S].bitcast(I32),
+                    picked[row0 : row0 + 64, :].bitcast(I32),
+                )
         weights = place("weights", S, F32, "weights")
         first_pieces = [
             slice(sum(FIRST_PIECES[:j]), sum(FIRST_PIECES[: j + 1])) for j in range(len(FIRST_PIECES))
@@ -140,9 +136,8 @@ def tile_list_courier_eta_banks_kernel(
         nc.sync.dma_start(weights[:, first_pieces[0]], wgs[:, first_pieces[0]])
         places = lists.tile([P, S // LIST_ROWS], U16, name="places")
         nc.sync.dma_start(places[:], offs2)
-        nc.sync.dma_start(weights[:, first_pieces[1]], wgs[:, first_pieces[1]])
-        shift_scales(1)
-        nc.sync.dma_start(weights[:, first_pieces[2]], wgs[:, first_pieces[2]])
+        for cols in first_pieces[1:]:
+            nc.sync.dma_start(weights[:, cols], wgs[:, cols])
 
         road_rows = road.rearrange("(b p i) t -> b i p t", b=PASSES, i=PACK)
         roads = {}
@@ -277,10 +272,17 @@ def tile_list_courier_eta_banks_kernel(
             nc.vector.tensor_copy(page_of[k][:].indirect(entries), h[k][:, cols])
 
         pairs = [
-            place(f"pairs{b}", PACK * T2, BF16, f"pairs{b}") for b in range(PASSES)
+            place(f"pairs{b}", PACK * (T2, TURN_FROM)[b], BF16, f"pairs{b}") for b in range(PASSES)
         ]
 
-        def add_road(step):
+        def halves_of(i, cols):
+            blocks = pairs[1][:].rearrange("p (j u t e) -> p j u t e", u=2, t=P, e=2)
+            return blocks[:, cols.start // P : cols.stop // P, i // 2, :, i % 2]
+
+        def by_block(rows):
+            return rows.rearrange("p (j t) -> p j t", t=P)
+
+        def add_road(step, cols=slice(0, T2)):
             k = ORDER[step]
             b, i = divmod(k, PACK)
             if b == 0:
@@ -288,10 +290,7 @@ def tile_list_courier_eta_banks_kernel(
                 nc.gpsimd.tensor_tensor(halves, page_of[k][:], roads[k][:], ADD)
             else:
                 nc.gpsimd.tensor_tensor(
-                    pairs[b][:].rearrange("p (c u t e) -> p c u t e", u=2, t=STRIP, e=2)[:, :, i // 2, :, i % 2],
-                    page_of[k][:].rearrange("p (c t) -> p c t", t=STRIP),
-                    roads[k][:].rearrange("p (c t) -> p c t", t=STRIP),
-                    ADD,
+                    halves_of(i, cols), by_block(page_of[k][:, cols]), by_block(roads[k][:, cols]), ADD
                 )
 
         def turn(j, source, e, start=False, stop=False):
@@ -314,8 +313,8 @@ def tile_list_courier_eta_banks_kernel(
             else:
                 z = place(f"z1_{c}", PACK * BANK, BF16, "relay", c * Z_BYTES)
                 chunk = pairs[b][:, c * PACK * BANK : (c + 1) * PACK * BANK]
-                words = chunk.bitcast(F32).rearrange("p (j u t) -> p j t u", u=2, t=STRIP)
-                nc.scalar.copy(z[:].bitcast(F32).rearrange("p (j t u) -> p j t u", u=2, t=STRIP), words)
+                words = chunk.bitcast(F32).rearrange("p (j u t) -> p j t u", u=2, t=P)
+                nc.scalar.copy(z[:].bitcast(F32).rearrange("p (j t u) -> p j t u", u=2, t=P), words)
                 return z
             nc.scalar.copy(z[:].bitcast(F32).rearrange("p (t u) -> p t u", u=2), words)
             return z
@@ -360,6 +359,33 @@ def tile_list_courier_eta_banks_kernel(
                 )
             nc.scalar.copy(pairs[0][:].bitcast(F32)[:, T2 + c * BANK : T2 + (c + 1) * BANK], banks[c][:])
 
+        last_bank = banks[BANKS - 1]
+        upper = [
+            place("upper0", BANK, BF16, "relay", Z_BYTES // 2),
+            place("upper1", BANK, BF16, "relay", 2 * Z_BYTES - BANK),
+        ]
+
+        def turn_last(source, first):
+            for s in range(BANK // P):
+                t0 = TURN_FROM + s * P
+                nc.tensor.matmul(
+                    last_bank[:, s * P : (s + 1) * P],
+                    source[:, t0 : t0 + P],
+                    ident[:],
+                    start=(first and s == 0),
+                    stop=(not first and s == BANK // P - 1),
+                    is_transpose=True,
+                )
+
+        def round_last(e):
+            for j in range(2):
+                halves = upper[j][:].rearrange("t (c e) -> t c e", e=2)[:, :, e]
+                nc.scalar.copy(halves, last_bank[:, j * STRIP : (j + 1) * STRIP])
+
+        turn_last(roads[LAST - 1], True)
+        turn_last(page_of[LAST - 1], False)
+        round_last(0)
+
         def jam_of(n):
             c, nt = TILE_ORDER[n]
             return jams[nt // 2][:, nt % 2, c * BANK : (c + 1) * BANK]
@@ -369,29 +395,22 @@ def tile_list_courier_eta_banks_kernel(
                 nc.tensor.transpose(bank[:, s * P : (s + 1) * P], source[:, s * P : (s + 1) * P], ident[:])
 
         road_cols = [slice(c * BANK, min((c + 1) * BANK, VECTOR_COLUMNS)) for c in range(ROAD_BANKS)]
-        first_free = BANKS - ROAD_BANKS - JAM_BANKS
-        road_banks = banks[BANKS - ROAD_BANKS :]
+        first_free = BANKS - 1 - ROAD_BANKS - JAM_BANKS
+        road_banks = banks[BANKS - 1 - ROAD_BANKS : BANKS - 1]
         jam_banks = banks[first_free : first_free + JAM_BANKS]
-        turns = []
 
-        def stage(once, source, width=BANK):
-            bank = banks[len(turns) % first_free]
-            turns.append(bank)
-            turn_blocks(bank, source, width)
-            nc.scalar.copy(once, bank[:, :width])
+        def stage(once, source, bank):
+            turn_blocks(bank, source)
+            nc.scalar.copy(once, bank[:])
             return once
 
         staged = {}
         for j in range(JAM_BANKS, VECTOR_SHARE):
-            staged[j] = stage(place(f"staged{j}", BANK, F32, "staged", 4 * BANK * (j - JAM_BANKS))[:], jam_of(VECTOR_TILES[j]))
-        early = place("early", CHUNKS * Z_BYTES // 4, F32, "relay", 0)
+            staged[j] = stage(place(f"staged{j}", BANK, F32, "staged", 4 * BANK * (j - JAM_BANKS))[:], jam_of(VECTOR_TILES[j]), last_bank if j == VECTOR_SHARE - 1 else banks[j % 2])
+        early = place("early", JAM_BANKS * BANK, F32, "turned")
+        waiting_banks = [road_banks[1], banks[first_free - 1]]
         for j in range(JAM_BANKS):
-            staged[j] = stage(early[:, j * BANK : (j + 1) * BANK], jam_of(VECTOR_TILES[j]))
-        staged_road = []
-        for cols in road_cols:
-            width = cols.stop - cols.start
-            place0 = JAM_BANKS * BANK + cols.start
-            staged_road.append(stage(early[:, place0 : place0 + width], roads[LAST][:, cols], width))
+            staged[j] = stage(early[:, j * BANK : (j + 1) * BANK], jam_of(VECTOR_TILES[j]), waiting_banks[j])
 
         def bring_jam(j):
             turn_blocks(jam_banks[j % JAM_BANKS], staged[j])
@@ -399,58 +418,89 @@ def tile_list_courier_eta_banks_kernel(
         for j in range(JAM_BANKS):
             bring_jam(j)
         for c, cols in enumerate(road_cols):
-            turn_blocks(road_banks[c], staged_road[c], cols.stop - cols.start)
+            turn_blocks(waiting_banks[c], roads[LAST][:, cols], cols.stop - cols.start)
 
         z0 = [weave(0, c) for c in range(CHUNKS)]
 
         put(5)
         put(6)
-        add_road(4)
+        add_road(4, slice(0, TURN_FROM))
         put(7)
-        add_road(5)
-        add_road(6)
+        last_pairs = place("last_pairs", 2 * BANK, BF16, "pairs1", 2 * PACK * TURN_FROM)
+
+        def add_road_last(step):
+            k = ORDER[step]
+            halves = last_pairs[:].rearrange("p (t e) -> p t e", e=2)[:, :, k % 2]
+            nc.gpsimd.tensor_tensor(halves, page_of[k][:, TURN_FROM:], roads[k][:, TURN_FROM:], ADD)
+
+        add_road_last(5)
+        add_road(5, slice(0, TURN_FROM))
+        late_region = f"road{(SLICES - 3) % PACK}"
+        first_plane = place("first_plane", N, U8, late_region)
+        late_road = place("late_road", VECTOR_COLUMNS, F32, late_region, N)
+        for c, cols in enumerate(road_cols):
+            nc.scalar.copy(late_road[:, cols], waiting_banks[c][:, : cols.stop - cols.start])
+            turn_blocks(road_banks[c], late_road[:, cols], cols.stop - cols.start)
+        add_road_last(6)
+        add_road(6, slice(0, TURN_FROM))
+
+        def turn_back(u, strips):
+            for j in range(2):
+                turn_blocks(banks[j][:, u * STRIP : (u + 1) * STRIP], strips[j], STRIP)
+
+        lower = place("lower", BANK, F32, "relay", 0)
+        turn_blocks(last_bank, last_pairs[:].bitcast(F32))
+        nc.scalar.copy(lower[:], last_bank[:])
+        turn_back(0, [lower[:, :STRIP], lower[:, STRIP:]])
+        turn_last(roads[LAST], True)
 
         w2_codes = place("w2_codes", PASSES * N, U32, "w2_codes")
         z_codes = {}
         z_plane = {}
-        z1_plane = place("z1_plane", T2, U8, "z1_plane")
 
         def quantise(b, c, z):
             if b == 0 and c >= 2:
                 codes = place(f"z_codes0_{c}", BANK, U32, "relay", (c - 2) * Z_BYTES)
             else:
-                tag = f"slot{PACK + c}" if b else ("codes0", "codes2")[c]
+                tag = f"slot{PACK + c}" if b else ("codes3", "codes2")[c]
                 codes = place(f"z_codes{b}_{c}", BANK, U32, tag)
-            plane = (late_plane, z1_plane)[b][:, c * BANK : (c + 1) * BANK]
+            plane = late_plane[:, b * T2 + c * BANK : b * T2 + (c + 1) * BANK]
             nc.vector.quantize_mx(out=codes[:].bitcast(E4M3), scales=plane, in_=z[:])
             z_codes[b, c] = codes
             z_plane[b, c] = plane
 
-        def odd_halves(cols):
-            strips = pairs[1][:].rearrange("p (j u t e) -> p j u t e", u=2, t=STRIP, e=2)
-            return strips[:, cols.start // STRIP : cols.stop // STRIP, 1, :, 1]
+        def quantise_w2(b, plane):
+            nc.vector.quantize_mx(
+                out=w2_codes[:, b * N : (b + 1) * N].bitcast(E4M3),
+                scales=plane,
+                in_=w2_grouped[:, b * PACK * N : (b + 1) * PACK * N],
+            )
+            return plane
 
-        def by_strip(rows):
-            return rows.rearrange("p (j t) -> p j t", t=STRIP)
-
-        cols = slice(VECTOR_COLUMNS, T2)
-        nc.gpsimd.tensor_tensor(odd_halves(cols), by_strip(page_of[LAST][:, cols]), by_strip(roads[LAST][:, cols]), ADD)
+        w2_planes = [quantise_w2(0, first_plane[:])]
+        cols = slice(VECTOR_COLUMNS, TURN_FROM)
+        nc.gpsimd.tensor_tensor(
+            halves_of(PACK - 1, cols), by_block(page_of[LAST][:, cols]), by_block(roads[LAST][:, cols]), ADD
+        )
         for c, cols in enumerate(road_cols):
             rows = road_banks[c][:, : cols.stop - cols.start]
-            nc.vector.tensor_tensor(odd_halves(cols), by_strip(page_of[LAST][:, cols]), by_strip(rows), ADD)
-        z1 = [weave(1, c) for c in range(CHUNKS)]
-        late_plane = place("late_plane", T2 + PASSES * N, U8, f"page{(SLICES - 1) % PAGES}")
-        w2_plane = late_plane[:, T2:]
-        for c in range(2):
-            for b in range(PASSES):
-                if c == 0:
-                    cols = slice(b * N, (b + 1) * N)
-                    nc.vector.quantize_mx(
-                        out=w2_codes[:, cols].bitcast(E4M3),
-                        scales=w2_plane[:, cols],
-                        in_=w2_grouped[:, b * PACK * N : (b + 1) * PACK * N],
-                    )
-                quantise(b, c, (z0, z1)[b][c])
+            nc.vector.tensor_tensor(halves_of(PACK - 1, cols), by_block(page_of[LAST][:, cols]), by_block(rows), ADD)
+        turn_last(page_of[LAST], False)
+        round_last(1)
+        turn_back(1, [half[:].bitcast(F32) for half in upper])
+        z1 = [weave(1, c) for c in range(CHUNKS - 1)]
+        z1.append(place(f"z1_{CHUNKS - 1}", PACK * BANK, BF16, "relay", (CHUNKS - 1) * Z_BYTES))
+        for j in range(2):
+            nc.scalar.copy(
+                z1[-1][:].bitcast(F32)[:, j * BANK : (j + 1) * BANK].rearrange("p (t u) -> p t u", u=2),
+                banks[j][:].rearrange("p (u t) -> p t u", u=2),
+            )
+        late_plane = place("late_plane", PASSES * T2 + N, U8, f"page{(SLICES - 1) % PAGES}")
+        quantise(0, 0, z0[0])
+        w2_planes.append(quantise_w2(1, late_plane[:, PASSES * T2 :]))
+        quantise(1, 0, z1[0])
+        for b in range(PASSES):
+            quantise(b, 1, (z0, z1)[b][1])
         for b in range(PASSES):
             for c in range(2, CHUNKS):
                 quantise(b, c, (z0, z1)[b][c])
@@ -459,7 +509,7 @@ def tile_list_courier_eta_banks_kernel(
             place(f"curves{j}", TILES // 2 * BANK, F32, ("pairs0", "curves1")[j])
             for j in range(2)
         ]
-        free_banks = banks[:first_free] + road_banks
+        free_banks = [banks[2], road_banks[0], last_bank, road_banks[1], banks[0], banks[1]]
         bank_of, curve, delay = {}, {}, {}
 
         def product(n):
@@ -471,7 +521,7 @@ def tile_list_courier_eta_banks_kernel(
                 nc.tensor.matmul_mx(
                     out=bank_of[n][:],
                     lhsT=w2_codes[:, w_cols].bitcast(E4M3),
-                    lhsT_scale=w2_plane[:, w_cols],
+                    lhsT_scale=w2_planes[b][:, nt * P : (nt + 1) * P],
                     rhs=z_codes[b, c][:].bitcast(E4M3),
                     rhs_scale=z_plane[b, c],
                     start=(b == passes[0]),
@@ -488,17 +538,14 @@ def tile_list_courier_eta_banks_kernel(
             if j + JAM_BANKS < VECTOR_SHARE:
                 bring_jam(j + JAM_BANKS)
 
-        held = [
-            place(f"held{c}", 2 * BANK, F32, "relay", c * Z_BYTES)
-            for c in (CHUNKS - 1, CHUNKS - 2)
-        ]
+        held = place("held", 3 * BANK, F32, "relay", (CHUNKS - 2) * Z_BYTES)
         early_tiles = [n for n in range(len(free_banks)) if n not in VECTOR_TILES]
 
         def gpsimd_delay(n):
             delay[n] = curve[n]
             if n in early_tiles:
-                j, place = divmod(early_tiles.index(n), 2)
-                delay[n] = held[j][:, place * BANK : (place + 1) * BANK]
+                j = early_tiles.index(n)
+                delay[n] = held[:, j * BANK : (j + 1) * BANK]
             nc.gpsimd.tensor_tensor(delay[n], curve[n], jam_of(n), MULT)
 
         def finish(n):
@@ -511,10 +558,8 @@ def tile_list_courier_eta_banks_kernel(
 
         for n in range(len(free_banks)):
             product(n)
-        for n in range(TILES + GPSIMD_LAG):
+        for n in range(TILES + 1):
             if n < TILES:
                 (vector_delay if n in VECTOR_TILES else gpsimd_delay)(n)
-            if n - VECTOR_LAG in VECTOR_TILES:
-                finish(n - VECTOR_LAG)
-            if n >= GPSIMD_LAG and n - GPSIMD_LAG not in VECTOR_TILES:
-                finish(n - GPSIMD_LAG)
+            if n > 0:
+                finish(n - 1)

@@ -435,9 +435,7 @@ def tile_list_courier_eta_banks_kernel(
 
         add_road_last(5)
         add_road(5, slice(0, TURN_FROM))
-        late_region = f"road{(SLICES - 3) % PACK}"
-        first_plane = place("first_plane", N, U8, late_region)
-        late_road = place("late_road", VECTOR_COLUMNS, F32, late_region, N)
+        late_road = place("late_road", VECTOR_COLUMNS, F32, "turned", 4 * JAM_BANKS * BANK)
         for c, cols in enumerate(road_cols):
             nc.scalar.copy(late_road[:, cols], waiting_banks[c][:, : cols.stop - cols.start])
             turn_blocks(road_banks[c], late_road[:, cols], cols.stop - cols.start)
@@ -477,7 +475,6 @@ def tile_list_courier_eta_banks_kernel(
             )
             return plane
 
-        w2_planes = [quantise_w2(0, first_plane[:])]
         cols = slice(VECTOR_COLUMNS, TURN_FROM)
         nc.gpsimd.tensor_tensor(
             halves_of(PACK - 1, cols), by_block(page_of[LAST][:, cols]), by_block(roads[LAST][:, cols]), ADD
@@ -495,9 +492,10 @@ def tile_list_courier_eta_banks_kernel(
                 z1[-1][:].bitcast(F32)[:, j * BANK : (j + 1) * BANK].rearrange("p (t u) -> p t u", u=2),
                 banks[j][:].rearrange("p (u t) -> p t u", u=2),
             )
-        late_plane = place("late_plane", PASSES * T2 + N, U8, f"page{(SLICES - 1) % PAGES}")
+        late_plane = place("late_plane", PASSES * (T2 + N), U8, f"page{(SLICES - 1) % PAGES}")
+        w2_planes = [quantise_w2(0, late_plane[:, PASSES * T2 : PASSES * T2 + N])]
         quantise(0, 0, z0[0])
-        w2_planes.append(quantise_w2(1, late_plane[:, PASSES * T2 :]))
+        w2_planes.append(quantise_w2(1, late_plane[:, PASSES * T2 + N :]))
         quantise(1, 0, z1[0])
         for b in range(PASSES):
             quantise(b, 1, (z0, z1)[b][1])
@@ -538,14 +536,14 @@ def tile_list_courier_eta_banks_kernel(
             if j + JAM_BANKS < VECTOR_SHARE:
                 bring_jam(j + JAM_BANKS)
 
-        held = place("held", 3 * BANK, F32, "relay", (CHUNKS - 2) * Z_BYTES)
+        held = [place(f"held{c}", 2 * BANK, F32, "relay", c * Z_BYTES) for c in (CHUNKS - 1, CHUNKS - 2)]
         early_tiles = [n for n in range(len(free_banks)) if n not in VECTOR_TILES]
 
         def gpsimd_delay(n):
             delay[n] = curve[n]
             if n in early_tiles:
-                j = early_tiles.index(n)
-                delay[n] = held[:, j * BANK : (j + 1) * BANK]
+                j, slot = divmod(early_tiles.index(n), 2)
+                delay[n] = held[j][:, slot * BANK : (slot + 1) * BANK]
             nc.gpsimd.tensor_tensor(delay[n], curve[n], jam_of(n), MULT)
 
         def finish(n):

@@ -40,7 +40,7 @@ VECTOR_COLUMNS = 896
 ROAD_BANKS = 2
 TURN_FROM = T2 - BANK
 TILES = N // P * CHUNKS
-VECTOR_TILES = [n for n in range(TILES) if n % 3 == 1 or n in (0, TILES - 1)]
+VECTOR_TILES = [n for n in range(TILES) if n == 0 or n % 5 in (1, 3)]
 VECTOR_SHARE = len(VECTOR_TILES)
 LATE_FIRSTS = [(c, 0) for c in range(CHUNKS - 2, CHUNKS)]
 IN_ORDER = [(c, nt) for c in range(CHUNKS) for nt in range(N // P) if (c, nt) not in LATE_FIRSTS]
@@ -361,8 +361,8 @@ def tile_list_courier_eta_banks_kernel(
 
         last_bank = banks[BANKS - 1]
         upper = [
-            place("upper0", BANK, BF16, "relay", Z_BYTES // 2),
-            place("upper1", BANK, BF16, "relay", 2 * Z_BYTES - BANK),
+            place("upper0", BANK, BF16, "relay", 2 * Z_BYTES - BANK),
+            place("upper1", BANK, BF16, "relay", (CHUNKS - 1) * Z_BYTES),
         ]
 
         def turn_last(source, first):
@@ -504,16 +504,16 @@ def tile_list_courier_eta_banks_kernel(
                 quantise(b, c, (z0, z1)[b][c])
 
         curve_tiles = [
-            place(f"curves{j}", TILES // 2 * BANK, F32, ("pairs0", "curves1")[j])
+            place(f"curves{j}", TILES // 2 * BANK, F32, ("pairs1", "curves1")[j])
             for j in range(2)
         ]
-        free_banks = [banks[2], road_banks[0], last_bank, road_banks[1], banks[0], banks[1]]
+        free_banks = [last_bank, banks[2], road_banks[0], road_banks[1], banks[0], banks[1]]
         bank_of, curve, delay = {}, {}, {}
 
         def product(n):
             c, nt = TILE_ORDER[n]
             bank_of[n] = free_banks[n]
-            passes = (0, 1) if n < 2 else (1, 0)
+            passes = (0, 1) if n == 0 else (1, 0)
             for b in passes:
                 w_cols = slice(b * N + nt * P, b * N + (nt + 1) * P)
                 nc.tensor.matmul_mx(

@@ -36,11 +36,11 @@ LAST = ORDER[-1]
 FIRST_PIECES = (128, 384, 512)
 FIRST_STEPS = 2
 Z_BYTES = 2 * PACK * BANK
-VECTOR_COLUMNS = 896
+VECTOR_COLUMNS = 1024
 ROAD_BANKS = 2
 TURN_FROM = T2 - BANK
 TILES = N // P * CHUNKS
-VECTOR_TILES = [n for n in range(TILES) if n == 0 or n % 5 in (1, 3)]
+VECTOR_TILES = [n for n in range(TILES) if n == 0 or n % 5 in (2, 4)]
 VECTOR_SHARE = len(VECTOR_TILES)
 LATE_FIRSTS = [(c, 0) for c in range(CHUNKS - 2, CHUNKS)]
 IN_ORDER = [(c, nt) for c in range(CHUNKS) for nt in range(N // P) if (c, nt) not in LATE_FIRSTS]
@@ -308,15 +308,14 @@ def tile_list_courier_eta_banks_kernel(
 
         def weave(b, c):
             if b == 0:
-                z = place(f"z0_{c}", PACK * BANK, BF16, f"slot{c}")
-                words = pairs[b][:].bitcast(F32).rearrange("p (u t) -> p t u", u=2)[:, c * BANK : (c + 1) * BANK, :]
+                z = place(f"z0_{c}", 2 * PACK * BANK, BF16, f"slot{c}")
+                words = pairs[b][:].bitcast(F32).rearrange("p (u t) -> p t u", u=2)[:, c * BANK : (c + 2) * BANK, :]
+                nc.scalar.copy(z[:].bitcast(F32).rearrange("p (t u) -> p t u", u=2), words)
             else:
                 z = place(f"z1_{c}", PACK * BANK, BF16, "relay", c * Z_BYTES)
                 chunk = pairs[b][:, c * PACK * BANK : (c + 1) * PACK * BANK]
                 words = chunk.bitcast(F32).rearrange("p (j u t) -> p j t u", u=2, t=P)
                 nc.scalar.copy(z[:].bitcast(F32).rearrange("p (j t u) -> p j t u", u=2, t=P), words)
-                return z
-            nc.scalar.copy(z[:].bitcast(F32).rearrange("p (t u) -> p t u", u=2), words)
             return z
 
         pages.append(place("page2", T2, F32, "page2"))
@@ -420,7 +419,7 @@ def tile_list_courier_eta_banks_kernel(
         for c, cols in enumerate(road_cols):
             turn_blocks(waiting_banks[c], roads[LAST][:, cols], cols.stop - cols.start)
 
-        z0 = [weave(0, c) for c in range(CHUNKS)]
+        z0 = {c: weave(0, c) for c in range(0, CHUNKS, 2)}
 
         put(5)
         put(6)
@@ -456,24 +455,14 @@ def tile_list_courier_eta_banks_kernel(
         z_codes = {}
         z_plane = {}
 
-        def quantise(b, c, z):
-            if b == 0 and c >= 2:
-                codes = place(f"z_codes0_{c}", BANK, U32, "relay", (c - 2) * Z_BYTES)
-            else:
-                tag = f"slot{PACK + c}" if b else ("codes3", "codes2")[c]
-                codes = place(f"z_codes{b}_{c}", BANK, U32, tag)
-            plane = late_plane[:, b * T2 + c * BANK : b * T2 + (c + 1) * BANK]
+        def quantise(b, c, z, region):
+            width = z.shape[1] // PACK
+            codes = place(f"z_codes{b}_{c}", width, U32, region)
+            plane = late_plane[:, b * T2 + c * BANK : b * T2 + c * BANK + width]
             nc.vector.quantize_mx(out=codes[:].bitcast(E4M3), scales=plane, in_=z[:])
-            z_codes[b, c] = codes
-            z_plane[b, c] = plane
-
-        def quantise_w2(b, plane):
-            nc.vector.quantize_mx(
-                out=w2_codes[:, b * N : (b + 1) * N].bitcast(E4M3),
-                scales=plane,
-                in_=w2_grouped[:, b * PACK * N : (b + 1) * PACK * N],
-            )
-            return plane
+            for j in range(width // BANK):
+                z_codes[b, c + j] = codes[:, j * BANK : (j + 1) * BANK]
+                z_plane[b, c + j] = plane[:, j * BANK : (j + 1) * BANK]
 
         cols = slice(VECTOR_COLUMNS, TURN_FROM)
         nc.gpsimd.tensor_tensor(
@@ -493,15 +482,13 @@ def tile_list_courier_eta_banks_kernel(
                 banks[j][:].rearrange("p (u t) -> p t u", u=2),
             )
         late_plane = place("late_plane", PASSES * (T2 + N), U8, f"page{(SLICES - 1) % PAGES}")
-        w2_planes = [quantise_w2(0, late_plane[:, PASSES * T2 : PASSES * T2 + N])]
-        quantise(0, 0, z0[0])
-        w2_planes.append(quantise_w2(1, late_plane[:, PASSES * T2 + N :]))
-        quantise(1, 0, z1[0])
-        for b in range(PASSES):
-            quantise(b, 1, (z0, z1)[b][1])
-        for b in range(PASSES):
-            for c in range(2, CHUNKS):
-                quantise(b, c, (z0, z1)[b][c])
+        w2_plane = late_plane[:, PASSES * T2 :]
+        nc.vector.quantize_mx(out=w2_codes[:].bitcast(E4M3), scales=w2_plane, in_=w2_grouped[:])
+        quantise(0, 0, z0[0], "codes2")
+        quantise(1, 0, z1[0], f"slot{PACK}")
+        quantise(0, 2, z0[2], "relay")
+        for c in range(1, CHUNKS):
+            quantise(1, c, z1[c], f"slot{PACK + c}")
 
         curve_tiles = [
             place(f"curves{j}", TILES // 2 * BANK, F32, ("pairs1", "curves1")[j])
@@ -519,8 +506,8 @@ def tile_list_courier_eta_banks_kernel(
                 nc.tensor.matmul_mx(
                     out=bank_of[n][:],
                     lhsT=w2_codes[:, w_cols].bitcast(E4M3),
-                    lhsT_scale=w2_planes[b][:, nt * P : (nt + 1) * P],
-                    rhs=z_codes[b, c][:].bitcast(E4M3),
+                    lhsT_scale=w2_plane[:, w_cols],
+                    rhs=z_codes[b, c].bitcast(E4M3),
                     rhs_scale=z_plane[b, c],
                     start=(b == passes[0]),
                     stop=(b == passes[-1]),

from contextlib import ExitStack

import concourse.mybir as mybir
from concourse.masks import make_identity

K, T, S, T2, H, N = 1024, 2048, 1024, 2048, 1024, 512
FLOPS = 2 * K * H * S + 2 * H * N * T2

F32 = mybir.dt.float32
BF16 = mybir.dt.bfloat16
I32 = mybir.dt.int32
U32 = mybir.dt.uint32
U16 = mybir.dt.uint16
U8 = mybir.dt.uint8
E4M3 = mybir.dt.float8_e4m3fn_x4
E2M1 = mybir.dt.float4_e2m1fn_x4
MULT = mybir.AluOpType.mult
ADD = mybir.AluOpType.add
RELU = mybir.ActivationFunctionType.Relu
TANH = mybir.ActivationFunctionType.Tanh

P = 128
PACK = 4
BANK = 512
BANKS = 8
PASSES = 2
SLICES = PASSES * PACK
CHUNKS = T2 // BANK
LIST_ROWS = 16
PAGES = 3
STRIP = 256
STRIPS = T2 // STRIP
FIRST_BANKS = 3
ORDER = (0, 1, 2, 3, 6, 4, 5, 7)
LAST = ORDER[-1]
FIRST_PIECES = (128, 384, 512)
FIRST_STEPS = 2
Z_BYTES = 2 * PACK * BANK
VECTOR_COLUMNS = 1024
ROAD_BANKS = 2
TURN_FROM = T2 - BANK
TILES = N // P * CHUNKS
VECTOR_TILES = [n for n in range(TILES) if n == 0 or n % 5 in (2, 4)]
VECTOR_SHARE = len(VECTOR_TILES)
LATE_FIRSTS = [(c, 0) for c in range(CHUNKS - 2, CHUNKS)]
IN_ORDER = [(c, nt) for c in range(CHUNKS) for nt in range(N // P) if (c, nt) not in LATE_FIRSTS]
TILE_ORDER = IN_ORDER[: N // P] + LATE_FIRSTS + IN_ORDER[N // P :]
JAM_BANKS = 2
REGIONS = (
    [(f"road{j}", 4 * T2) for j in range(PACK)]
    + [(f"wide{j}", 8 * T2) for j in range(2)]
    + [(f"page{j}", 4 * T2) for j in range(PAGES)]
    + [(f"pairs{j}", 8 * T2) for j in range(PASSES)]
    + [(f"slot{j}", 4 * S) for j in range(SLICES)]
    + [("relay", CHUNKS * Z_BYTES), ("curves1", 8 * T2), ("codes0", 2 * PASSES * PACK * N)]
    + [(f"codes{j}", 4 * BANK) for j in range(1, 5)]
    + [("w2_codes", 4 * PASSES * N), ("v_plane", PASSES * S), ("picked", S), ("weights", 4 * S)]
    + [("ident", 4 * P), ("bias", 64), ("w1_scale1", H), ("turned", 4 * T2)]
    + [("staged", 4 * BANK * (VECTOR_SHARE - JAM_BANKS))]
)
START = {name: sum(size for other, size in REGIONS[:j]) for j, (name, own) in enumerate(REGIONS)}


def tile_list_courier_eta_banks_kernel(
    tc, tab_words, tab_scales, offs, w1_words, w1_scales, b1, offs2, wgs, road, w2, jam, out
):
    nc = tc.nc
    with ExitStack() as ctx:
        lists = ctx.enter_context(tc.tile_pool(name="lists", bufs=1))
        arena = ctx.enter_context(tc.tile_pool(name="arena", bufs=1))
        psum = ctx.enter_context(tc.psum_pool(name="psum", bufs=1))
        banks = [psum.tile([P, BANK], F32, name=f"bank{j}") for j in range(BANKS)]

        def place(name, columns, dtype, region, byte0=0):
            return arena.tile([P, columns], dtype, name=name, offset=START[region] + byte0, align_bytes=64)

        tab_plane = place("tab_plane", T + 4, U8, "road0")
        for rows in (slice(0, 16), slice(32, 48), slice(64, 128)):
            nc.vector.memset(tab_plane[rows, :].bitcast(I32), 0)
        w1_plane = place("w1_plane", PASSES * H, U8, "codes1")
        nc.gpsimd.memset(w1_plane[:].bitcast(I32), 0)
        v_plane = place("v_plane", PASSES * S, U8, "v_plane")
        pages = [place(f"page{j}", T2, F32, f"page{j}") for j in range(2)]
        nc.gpsimd.memset(pages[0][:], 0.0)
        for c in range(CHUNKS):
            nc.gpsimd.memset(pages[1][:, c * BANK : (c + 1) * BANK], 0.0)
        ident = place("ident", P, F32, "ident")
        make_identity(nc, ident[:])

        picks = lists.tile([P, S // LIST_ROWS], U16, name="picks")
        nc.sync.dma_start(picks[:], offs)
        scale_rows = tab_scales.bitcast(I32).rearrange("a (u e d) t -> e (a u) d t", u=2, e=2)
        for e in range(2):
            nc.sync.dma_start(tab_plane[32 * e + 16 : 32 * e + 32, :T].bitcast(I32), scale_rows[e])
        bias = place("bias", SLICES, F32, "bias")
        nc.sync.dma_start(
            bias[:].rearrange("p (b i) -> p b i", i=PACK), b1.rearrange("(b p i) -> p b i", b=PASSES, i=PACK)
        )
        tab = [place(f"tab{a}", T, I32, "wide0", 4 * T * a) for a in range(PASSES)]

        def load_table(a):
            nc.sync.dma_start(tab[a][:], tab_words[a].rearrange("p t i -> p (t i)").bitcast(I32))

        w1_raw = {}

        def load_w1(b):
            w1_raw[b] = place(f"w1_raw{b}", 2 * H, U8, ("w2_codes", "curves1")[b])
            nc.sync.dma_start(
                w1_raw[b][:].bitcast(I32).rearrange("p (a c) -> p a c", a=PASSES),
                w1_words[:, :, b * H : (b + 1) * H].bitcast(I32).rearrange("a p c -> p a c"),
            )

        load_w1(0)
        load_table(0)
        for q in range(4):
            nc.sync.dma_start(
                w1_plane[32 * q : 32 * q + 4, :].bitcast(I32).rearrange("r (a c) -> r a c", a=PASSES),
                w1_scales[:, 4 * q : 4 * q + 4, :].bitcast(I32).rearrange("a r c -> r a c"),
            )
        load_table(1)

        picked = place("picked", S, U8, "picked")
        nc.vector.tensor_copy(picked[:], tab_plane[:, :T].indirect(picks[:]))

        for a in range(PASSES):
            for u in range(2):
                row0 = 16 + 8 * a + 4 * u
                nc.sync.dma_start(
                    v_plane[64 * u : 64 * u + 64, a * S : (a + 1) * S].bitcast(I32),
                    picked[row0 : row0 + 64, :].bitcast(I32),
                )
        weights = place("weights", S, F32, "weights")
        first_pieces = [
            slice(sum(FIRST_PIECES[:j]), sum(FIRST_PIECES[: j + 1])) for j in range(len(FIRST_PIECES))
        ]
        nc.sync.dma_start(weights[:, first_pieces[0]], wgs[:, first_pieces[0]])
        places = lists.tile([P, S // LIST_ROWS], U16, name="places")
        nc.sync.dma_start(places[:], offs2)
        for cols in first_pieces[1:]:
            nc.sync.dma_start(weights[:, cols], wgs[:, cols])

        road_rows = road.rearrange("(b p i) t -> b i p t", b=PASSES, i=PACK)
        roads = {}

        def load_road(step):
            k = ORDER[step]
            roads[k] = place(f"road{k}", T2, F32, f"road{step % PACK}")
            nc.sync.dma_start(roads[k][:], road_rows[k // PACK, k % PACK])

        load_road(0)
        load_w1(1)
        load_road(1)
        w2_raw = place("w2_raw", PASSES * PACK * N, F32, "wide1")
        nc.sync.dma_start(
            w2_raw[:].rearrange("p (b c) -> p b c", b=PASSES),
            w2.rearrange("(b p i) n -> p b (i n)", b=PASSES, i=PACK),
        )
        load_road(2)
        load_road(3)

        w1_codes, w1_scale = {}, {}

        def deal_codes(k0, count):
            b, i0 = divmod(k0, PACK)
            codes = place(f"w1_codes{k0}", 2 * PASSES * count * P, U8, f"pairs{b}", 2 * PASSES * i0 * P)
            nc.scalar.copy(
                codes[:].bitcast(U16).rearrange("p (a i m) -> p a i m", i=count, m=P),
                w1_raw[b][:].bitcast(U16).rearrange("p (a m i) -> p a i m", i=PACK, m=P)[:, :, i0 : i0 + count, :],
            )
            for i in range(count):
                for a in range(PASSES):
                    code0 = 2 * P * (a * count + i)
                    w1_codes[k0 + i, a] = codes[:, code0 : code0 + 2 * P]

        def deal_scales(k0, count):
            b, i0 = divmod(k0, PACK)
            scales = place(f"w1_scale{k0}", PASSES * count * P, U8, ("page2", "w1_scale1")[b])
            nc.gpsimd.tensor_copy(
                scales[:].rearrange("p (a i m) -> p a i m", i=count, m=P),
                w1_plane[:].rearrange("p (a b m i) -> p b a i m", a=PASSES, i=PACK, m=P)[:, b, :, i0 : i0 + count, :],
            )
            for i in range(count):
                for a in range(PASSES):
                    scale0 = P * (a * count + i)
                    w1_scale[k0 + i, a] = scales[:, scale0 : scale0 + P]

        deal_codes(0, PACK)
        deal_scales(0, PACK)
        deal_scales(PACK, PACK)

        v_codes = {}
        for half in range(2):
            for a in range(PASSES):
                tag = ("codes0", "codes4", "codes2", "codes3")[2 * a + half]
                words = place(f"v_codes{a}{half}", BANK, U32, tag)
                cuts = (0, BANK // 2, BANK) if (a, half) == (1, 0) else (0, BANK)
                for lo, hi in zip(cuts, cuts[1:]):
                    entries = picks[:, (half * BANK + lo) // LIST_ROWS : (half * BANK + hi) // LIST_ROWS]
                    window = tab[a][:].bitcast(U32)
                    nc.vector.tensor_copy(words[:, lo:hi], window.indirect(entries))
                v_codes[a, half] = words

        halves_of_list = (slice(0, BANK), slice(BANK, S))

        h = {
            k: place(f"h{k}", S, F32, f"slot{step}") for step, k in enumerate(ORDER)
        }
        narrow_banks = []

        def first_product(step, pieces):
            k = ORDER[step]
            for cols in pieces:
                half, within = divmod(cols.start, BANK)
                count = cols.stop - cols.start
                if count == BANK:
                    bank = banks[(2 * step + half) % FIRST_BANKS]
                else:
                    bank = banks[FIRST_BANKS + len(narrow_banks)]
                    narrow_banks.append(bank)
                width = BANK if count == BANK else P
                passes = (1, 0) if count == BANK else (0, 1)
                for col0 in range(0, count, width):
                    for a in passes:
                        entry0 = a * S + cols.start + col0
                        nc.tensor.matmul_mx(
                            out=bank[:, col0 : col0 + width],
                            lhsT=w1_codes[k, a].bitcast(E2M1),
                            lhsT_scale=w1_scale[k, a],
                            rhs=v_codes[a, half][:, within + col0 : within + col0 + width].bitcast(E4M3),
                            rhs_scale=v_plane[:, entry0 : entry0 + width],
                            start=(a == passes[0]),
                            stop=(a == passes[-1]),
                        )
                nc.scalar.activation(h[k][:, cols], bank[:, :count], RELU, bias=bias[:, k : k + 1])

        def weigh(step, cols=slice(0, S)):
            k = ORDER[step]
            nc.gpsimd.tensor_tensor(h[k][:, cols], h[k][:, cols], weights[:, cols], MULT)

        for cols in first_pieces:
            for step in range(FIRST_STEPS):
                first_product(step, [cols])
                weigh(step, cols)
        for step in range(FIRST_STEPS, PACK):
            first_product(step, halves_of_list)
        deal_codes(PACK, PACK)
        for step in range(PACK, SLICES):
            first_product(step, halves_of_list)

        w2_grouped = place("w2_grouped", PASSES * PACK * N, BF16, "codes0")
        for b in range(PASSES):
            cols = slice(b * PACK * N, (b + 1) * PACK * N)
            nc.scalar.copy(
                w2_grouped[:, cols].rearrange("p (n i) -> p n i", i=PACK),
                w2_raw[:, cols].rearrange("p (i n) -> p n i", i=PACK),
            )
        jams = []
        for u in range(2):
            rows = place(f"jam{u}", 2 * T2, F32, f"wide{u}")
            nc.sync.dma_start(
                rows[:].rearrange("p (e t) -> p e t", e=2),
                jam[2 * u * P : 2 * (u + 1) * P, :].rearrange("(e p) t -> p e t", e=2),
            )
            jams.append(rows[:].rearrange("p (e t) -> p e t", e=2))

        page_of = {}

        def put(step, cols=slice(0, S)):
            k = ORDER[step]
            page_of[k] = pages[step % PAGES]
            entries = places[:, cols.start // LIST_ROWS : cols.stop // LIST_ROWS]
            nc.vector.tensor_copy(page_of[k][:].indirect(entries), h[k][:, cols])

        pairs = [
            place(f"pairs{b}", PACK * (T2, TURN_FROM)[b], BF16, f"pairs{b}") for b in range(PASSES)
        ]

        def halves_of(i, cols):
            blocks = pairs[1][:].rearrange("p (j u t e) -> p j u t e", u=2, t=P, e=2)
            return blocks[:, cols.start // P : cols.stop // P, i // 2, :, i % 2]

        def by_block(rows):
            return rows.rearrange("p (j t) -> p j t", t=P)

        def add_road(step, cols=slice(0, T2)):
            k = ORDER[step]
            b, i = divmod(k, PACK)
            if b == 0:
                halves = pairs[b][:].rearrange("p (u t e) -> p u t e", u=2, e=2)[:, i // 2, :, i % 2]
                nc.gpsimd.tensor_tensor(halves, page_of[k][:], roads[k][:], ADD)
            else:
                nc.gpsimd.tensor_tensor(
                    halves_of(i, cols), by_block(page_of[k][:, cols]), by_block(roads[k][:, cols]), ADD
                )

        def turn(j, source, e, start=False, stop=False):
            for s in range(2):
                t0 = j * STRIP + s * P
                c0 = (2 * s + e) * P
                nc.tensor.matmul(
                    banks[j][:, c0 : c0 + P],
                    source[:, t0 : t0 + P],
                    ident[:],
                    start=(start and s == 0),
                    stop=(stop and s == 1),
                    is_transpose=True,
                )

        def weave(b, c):
            if b == 0:
                z = place(f"z0_{c}", 2 * PACK * BANK, BF16, f"slot{c}")
                words = pairs[b][:].bitcast(F32).rearrange("p (u t) -> p t u", u=2)[:, c * BANK : (c + 2) * BANK, :]
                nc.scalar.copy(z[:].bitcast(F32).rearrange("p (t u) -> p t u", u=2), words)
            else:
                z = place(f"z1_{c}", PACK * BANK, BF16, "relay", c * Z_BYTES)
                chunk = pairs[b][:, c * PACK * BANK : (c + 1) * PACK * BANK]
                words = chunk.bitcast(F32).rearrange("p (j u t) -> p j t u", u=2, t=P)
                nc.scalar.copy(z[:].bitcast(F32).rearrange("p (j t u) -> p j t u", u=2, t=P), words)
            return z

        pages.append(place("page2", T2, F32, "page2"))
        nc.gpsimd.memset(pages[2][:], 0.0)
        weigh(2)
        weigh(3)
        for cols in first_pieces:
            for step in range(FIRST_STEPS):
                put(step, cols)
        put(2)
        for step in range(2):
            add_road(step)
            load_road(step + PACK)
            weigh(step + PACK)
            put(step + PAGES)
        weigh(6)
        weigh(7)

        for j in range(STRIPS):
            turn(j, roads[2], 0, start=True)
            turn(j, roads[3], 1)
        load_road(6)
        load_road(7)
        for j in range(STRIPS):
            turn(j, page_of[2], 0)
        turned = []
        for j in range(STRIPS):
            turn(j, page_of[3], 1, stop=True)
            strip = place(f"turned{j}", 2 * STRIP, BF16, "turned", 4 * STRIP * j)
            nc.scalar.copy(
                strip[:].rearrange("t (s p e) -> t s p e", s=2, e=2),
                banks[j][:].rearrange("t (s e p) -> t s p e", s=2, e=2),
            )
            turned.append(strip)
        for c in range(CHUNKS):
            for s in range(BANK // P):
                words = turned[2 * c + s // 2][:].bitcast(F32)
                nc.tensor.transpose(
                    banks[c][:, s * P : (s + 1) * P], words[:, (s % 2) * P : (s % 2 + 1) * P], ident[:]
                )
            nc.scalar.copy(pairs[0][:].bitcast(F32)[:, T2 + c * BANK : T2 + (c + 1) * BANK], banks[c][:])

        last_bank = banks[BANKS - 1]
        upper = [
            place("upper0", BANK, BF16, "relay", 2 * Z_BYTES - BANK),
            place("upper1", BANK, BF16, "relay", (CHUNKS - 1) * Z_BYTES),
        ]

        def turn_last(source, first):
            for s in range(BANK // P):
                t0 = TURN_FROM + s * P
                nc.tensor.matmul(
                    last_bank[:, s * P : (s + 1) * P],
                    source[:, t0 : t0 + P],
                    ident[:],
                    start=(first and s == 0),
                    stop=(not first and s == BANK // P - 1),
                    is_transpose=True,
                )

        def round_last(e):
            for j in range(2):
                halves = upper[j][:].rearrange("t (c e) -> t c e", e=2)[:, :, e]
                nc.scalar.copy(halves, last_bank[:, j * STRIP : (j + 1) * STRIP])

        turn_last(roads[LAST - 1], True)
        turn_last(page_of[LAST - 1], False)
        round_last(0)

        def jam_of(n):
            c, nt = TILE_ORDER[n]
            return jams[nt // 2][:, nt % 2, c * BANK : (c + 1) * BANK]

        def turn_blocks(bank, source, width=BANK):
            for s in range(width // P):
                nc.tensor.transpose(bank[:, s * P : (s + 1) * P], source[:, s * P : (s + 1) * P], ident[:])

        road_cols = [slice(c * BANK, min((c + 1) * BANK, VECTOR_COLUMNS)) for c in range(ROAD_BANKS)]
        first_free = BANKS - 1 - ROAD_BANKS - JAM_BANKS
        road_banks = banks[BANKS - 1 - ROAD_BANKS : BANKS - 1]
        jam_banks = banks[first_free : first_free + JAM_BANKS]

        def stage(once, source, bank):
            turn_blocks(bank, source)
            nc.scalar.copy(once, bank[:])
            return once

        staged = {}
        for j in range(JAM_BANKS, VECTOR_SHARE):
            staged[j] = stage(place(f"staged{j}", BANK, F32, "staged", 4 * BANK * (j - JAM_BANKS))[:], jam_of(VECTOR_TILES[j]), last_bank if j == VECTOR_SHARE - 1 else banks[j % 2])
        early = place("early", JAM_BANKS * BANK, F32, "turned")
        waiting_banks = [road_banks[1], banks[first_free - 1]]
        for j in range(JAM_BANKS):
            staged[j] = stage(early[:, j * BANK : (j + 1) * BANK], jam_of(VECTOR_TILES[j]), waiting_banks[j])

        def bring_jam(j):
            turn_blocks(jam_banks[j % JAM_BANKS], staged[j])

        for j in range(JAM_BANKS):
            bring_jam(j)
        for c, cols in enumerate(road_cols):
            turn_blocks(waiting_banks[c], roads[LAST][:, cols], cols.stop - cols.start)

        z0 = {c: weave(0, c) for c in range(0, CHUNKS, 2)}

        put(5)
        put(6)
        add_road(4, slice(0, TURN_FROM))
        put(7)
        last_pairs = place("last_pairs", 2 * BANK, BF16, "pairs1", 2 * PACK * TURN_FROM)

        def add_road_last(step):
            k = ORDER[step]
            halves = last_pairs[:].rearrange("p (t e) -> p t e", e=2)[:, :, k % 2]
            nc.gpsimd.tensor_tensor(halves, page_of[k][:, TURN_FROM:], roads[k][:, TURN_FROM:], ADD)

        add_road_last(5)
        add_road(5, slice(0, TURN_FROM))
        late_road = place("late_road", VECTOR_COLUMNS, F32, "turned", 4 * JAM_BANKS * BANK)
        for c, cols in enumerate(road_cols):
            nc.scalar.copy(late_road[:, cols], waiting_banks[c][:, : cols.stop - cols.start])
            turn_blocks(road_banks[c], late_road[:, cols], cols.stop - cols.start)
        add_road_last(6)
        add_road(6, slice(0, TURN_FROM))

        def turn_back(u, strips):
            for j in range(2):
                turn_blocks(banks[j][:, u * STRIP : (u + 1) * STRIP], strips[j], STRIP)

        lower = place("lower", BANK, F32, "relay", 0)
        turn_blocks(last_bank, last_pairs[:].bitcast(F32))
        nc.scalar.copy(lower[:], last_bank[:])
        turn_back(0, [lower[:, :STRIP], lower[:, STRIP:]])
        turn_last(roads[LAST], True)

        w2_codes = place("w2_codes", PASSES * N, U32, "w2_codes")
        z_codes = {}
        z_plane = {}

        def quantise(b, c, z, region):
            width = z.shape[1] // PACK
            codes = place(f"z_codes{b}_{c}", width, U32, region)
            plane = late_plane[:, b * T2 + c * BANK : b * T2 + c * BANK + width]
            nc.vector.quantize_mx(out=codes[:].bitcast(E4M3), scales=plane, in_=z[:])
            for j in range(width // BANK):
                z_codes[b, c + j] = codes[:, j * BANK : (j + 1) * BANK]
                z_plane[b, c + j] = plane[:, j * BANK : (j + 1) * BANK]

        cols = slice(VECTOR_COLUMNS, TURN_FROM)
        nc.gpsimd.tensor_tensor(
            halves_of(PACK - 1, cols), by_block(page_of[LAST][:, cols]), by_block(roads[LAST][:, cols]), ADD
        )
        for c, cols in enumerate(road_cols):
            rows = road_banks[c][:, : cols.stop - cols.start]
            nc.vector.tensor_tensor(halves_of(PACK - 1, cols), by_block(page_of[LAST][:, cols]), by_block(rows), ADD)
        turn_last(page_of[LAST], False)
        round_last(1)
        turn_back(1, [half[:].bitcast(F32) for half in upper])
        z1 = [weave(1, c) for c in range(CHUNKS - 1)]
        z1.append(place(f"z1_{CHUNKS - 1}", PACK * BANK, BF16, "relay", (CHUNKS - 1) * Z_BYTES))
        for j in range(2):
            nc.scalar.copy(
                z1[-1][:].bitcast(F32)[:, j * BANK : (j + 1) * BANK].rearrange("p (t u) -> p t u", u=2),
                banks[j][:].rearrange("p (u t) -> p t u", u=2),
            )
        late_plane = place("late_plane", PASSES * (T2 + N), U8, f"page{(SLICES - 1) % PAGES}")
        w2_plane = late_plane[:, PASSES * T2 :]
        nc.vector.quantize_mx(out=w2_codes[:].bitcast(E4M3), scales=w2_plane, in_=w2_grouped[:])
        quantise(0, 0, z0[0], "codes2")
        quantise(1, 0, z1[0], f"slot{PACK}")
        quantise(0, 2, z0[2], "relay")
        for c in range(1, CHUNKS):
            quantise(1, c, z1[c], f"slot{PACK + c}")

        curve_tiles = [
            place(f"curves{j}", TILES // 2 * BANK, F32, ("pairs1", "curves1")[j])
            for j in range(2)
        ]
        free_banks = [last_bank, banks[2], road_banks[0], road_banks[1], banks[0], banks[1]]
        bank_of, curve, delay = {}, {}, {}

        def product(n):
            c, nt = TILE_ORDER[n]
            bank_of[n] = free_banks[n]
            passes = (0, 1) if n == 0 else (1, 0)
            for b in passes:
                w_cols = slice(b * N + nt * P, b * N + (nt + 1) * P)
                nc.tensor.matmul_mx(
                    out=bank_of[n][:],
                    lhsT=w2_codes[:, w_cols].bitcast(E4M3),
                    lhsT_scale=w2_plane[:, w_cols],
                    rhs=z_codes[b, c].bitcast(E4M3),
                    rhs_scale=z_plane[b, c],
                    start=(b == passes[0]),
                    stop=(b == passes[-1]),
                )
            j, place = divmod(n, TILES // 2)
            curve[n] = curve_tiles[j][:, place * BANK : (place + 1) * BANK]
            nc.scalar.activation(curve[n], bank_of[n][:], TANH)

        def vector_delay(n):
            j = VECTOR_TILES.index(n)
            delay[n] = curve[n]
            nc.vector.tensor_tensor(delay[n], curve[n], jam_banks[j % JAM_BANKS][:], MULT)
            if j + JAM_BANKS < VECTOR_SHARE:
                bring_jam(j + JAM_BANKS)

        held = [place(f"held{c}", 2 * BANK, F32, "relay", c * Z_BYTES) for c in (CHUNKS - 1, CHUNKS - 2)]
        early_tiles = [n for n in range(len(free_banks)) if n not in VECTOR_TILES]

        def gpsimd_delay(n):
            delay[n] = curve[n]
            if n in early_tiles:
                j, slot = divmod(early_tiles.index(n), 2)
                delay[n] = held[j][:, slot * BANK : (slot + 1) * BANK]
            nc.gpsimd.tensor_tensor(delay[n], curve[n], jam_of(n), MULT)

        def finish(n):
            c, nt = TILE_ORDER[n]
            nc.vector.tensor_tensor(delay[n], delay[n], bank_of[n][:], ADD)
            nc.sync.dma_start(out[nt * P : (nt + 1) * P, c * BANK : (c + 1) * BANK], delay[n])
            free_banks.append(bank_of[n])
            if len(bank_of) < TILES:
                product(len(bank_of))

        for n in range(len(free_banks)):
            product(n)
        for n in range(TILES + 1):
            if n < TILES:
                (vector_delay if n in VECTOR_TILES else gpsimd_delay)(n)
            if n > 0:
                finish(n - 1)
